import numpy as np, ml_dtypes
CORES = [8,136,40,168]
N = 4
BF = ml_dtypes.bfloat16
P, D, SI, CAP, RO, PM, CM, LM = 512, 4, 2048, 128, 4, 1024, 4096, 49
DIST = np.array([0, 0, 0, 1])
def home(r, s):
    return (r - DIST[s // P]) % N
def lengths(rng, pw, big):
    e = np.zeros(P, np.int64); e[rng.permutation(P)[:big]] = LM - 1; t = (D - 1) * P - big * (LM - 1)
    e = e + np.bincount(rng.permutation(P)[np.minimum((P * rng.random(t) ** pw).astype(np.int64), P - 1)], minlength=P)
    e = np.minimum(e, LM - 1); o = rng.permutation(P); room = LM - 1 - e[o]
    e[o] += np.clip((D - 1) * P - np.sum(e) - (np.add.accumulate(room) - room), 0, room)
    return e + 1
def lists(rng, pw, big):
    calls = np.argsort(rng.random((N, 8, SI)), axis=-1)
    lens = np.array([[lengths(rng, pw, big) for g in range(8)] for r in range(N)])
    rid = np.array([[np.repeat(np.arange(P), lens[r, g]) for g in range(8)] for r in range(N)])
    return calls, lens, rid
def change(rng, b, k):
    m = np.argsort(rng.random(b.shape), axis=1) < k[:, None]
    return np.where(m, (b + rng.integers(1, 15, b.shape)) % 15, b)
def paint(rng, rid, share, loose):
    base = rng.integers(0, 15, (P, 16)); other = change(rng, base, rng.choice(np.array([0, 2, 4, 9]), P))
    n = rng.choice(np.array([7, 8, 9, 10, 16]), P); two = rng.random(P) < share; pick = (rng.random(SI) < 0.4) & two[rid]; out = []
    for b in (base, other):
        c = np.where(pick[:, None], change(rng, b, n)[rid], b[rid])
        c = np.where(rng.random(c.shape) < 0.03, rng.integers(0, 15, c.shape), c)
        out.append(np.where(rng.random(c.shape) < loose, 15, c))
    return np.stack(out).astype(np.int8)
def formals(rng):
    return np.where(rng.random((N, 8, 16, P)) < 0.4, 15, rng.integers(0, 15, (N, 8, 16, P)))
def mixed(rng, a):
    return rng.permuted(np.tile(np.array(a), (N, 2)), axis=1)
def pack(calls, lens, c, v):
    jump = np.zeros((N, 8, 16, 2 * SI), np.int8)
    for r in range(N):
        for g in range(8):
            s = calls[r, g]; q = home(r, s)
            jump[q, g, :, s] = c[r, g, 0]; jump[q, g, :, SI + s] = c[r, g, 1]
    return {"jump": jump.reshape(N, 128, 2 * SI).astype(np.float32).astype(BF), "form": np.ascontiguousarray(v).reshape(N, 128, P).astype(np.float32).astype(BF),
            "calls": calls.astype(np.int32), "runs": lens.astype(np.int32)}
def setup_inputs(rng):
    calls, lens, rid = lists(rng, 1.5, 0); share = mixed(rng, [0.05, 0.2, 0.5, 0.9]); loose = mixed(rng, [0.03, 0.06, 0.12, 0.2])
    c = np.stack([np.stack([paint(rng, rid[r, g], share[r, g], loose[r, g]) for g in range(8)]) for r in range(N)])
    return pack(calls, lens, c, formals(rng))
def setup_inputs_spread(rng):
    calls, lens, rid = lists(rng, 3.0, 0); q = mixed(rng, [0.2, 0.5, 0.8, 0.95])
    ex = np.where(rng.random((N, 8, 16)) < q[:, :, None], 12.0, rng.choice(np.array([0.25, 1.0, 3.0]), (N, 8, 16)))
    c = np.minimum((16 * rng.random((N, 8, 2, SI, 16)) ** ex[:, :, None, None, :]).astype(np.int8), 15)
    v = np.minimum((16 * rng.random((N, 8, 16, P)) ** ex[:, :, :, None]).astype(np.int8), 15)
    return pack(calls, lens, c, v)
def setup_inputs_ends(rng):
    n = (D - 1) * P // (LM - 1); half = np.arange(SI // 2); zig = np.stack([half, SI - 1 - half], axis=1).reshape(-1)
    calls = np.argsort(rng.random((N, 8, SI)), axis=-1)
    for r in range(N):
        for g in range(1, 8, 2): calls[r, g] = np.roll(zig, int(rng.integers(0, SI)))
    big = np.concatenate([np.argsort(rng.random((N, 8, P - 1)), axis=-1) < n - 1, np.ones((N, 8, 1), bool)], axis=-1); lens = np.where(big, LM, 1)
    lane = np.arange(16); m = np.stack([lane < 0, lane >= 0, lane >= 7, lane >= 8])
    kind = np.stack([rng.choice(5, (N, 8, SI), p=[0.06, 0.7, 0.1, 0.08, 0.06]), rng.choice(5, (N, 8, SI), p=[0.3, 0.3, 0.15, 0.15, 0.1])], axis=2)
    kind[..., SI - LM] = 0; kind[..., SI - 2] = 3; kind[..., SI - 1] = 2
    c = np.where((kind == 4)[..., None], rng.random(kind.shape + (16,)) < 0.5, m[np.minimum(kind, 3)]).astype(np.int8) * 15
    kv = rng.choice(5, (N, 8, P), p=[0.25, 0.5, 0.1, 0.1, 0.05])
    v = np.where((kv == 4)[..., None], rng.random(kv.shape + (16,)) < 0.5, m[np.minimum(kv, 3)]).astype(np.int8).transpose(0, 1, 3, 2) * 15
    for r in range(N):
        for g in range(8):
            for k in (SI - 2, SI - 1):
                s = int(calls[r, g, k]); v[int(home(r, s)), g, :, s % P] = 15
    return pack(calls, lens, c, v)
def setup_inputs_corners(rng):
    calls, lens, rid = lists(rng, 1.0, 4); c = np.zeros((N, 8, 2, SI, 16), np.int8)
    v = formals(rng); v[:, :, 0] = 15
    for r in range(N):
        for g in range(8):
            n = (CAP, CAP + 1, P, CAP - 1, 1, 0, CAP, CAP - 1)[(g + r) % 8]; L = lens[r, g]; d = rid[r, g]
            hot = np.zeros(P, bool); hot[rng.permutation(np.flatnonzero(L >= 2))[:n]] = True
            pos = np.arange(SI) - (np.add.accumulate(L) - L)[d]; how = rng.integers(0, 3, P)[d]
            m = hot[d] & (pos > 0) & np.where(how == 0, pos == L[d] - 1, np.where(how == 1, pos == 1, True))
            b = rng.integers(0, 15, (P, 16))[d]; x = change(rng, b, np.full(SI, 8)); x = np.where((x != b) & (rng.random(x.shape) < 0.3), 15, x)
            c[r, g, 0] = np.where((pos == 0)[:, None], b, np.where(m[:, None], change(rng, b, np.full(SI, 9)), x))
            c[r, g, 1] = paint(rng, d, 0.5, 0.1)[1]
    return pack(calls, lens, c, v)
def long_lists(rng, calls, lens, rid, r, g):
    L = lens[r, g]; two = np.flatnonzero(L == 2)[:min(LM - 1, CAP // 4)]; n = len(two)
    front = np.concatenate([np.flatnonzero(L == LM)[:1], two, np.flatnonzero(L == 1)[:3]])
    lens[r, g] = np.concatenate([L[front], np.delete(L, front)]); rid[r, g] = np.repeat(np.arange(P), lens[r, g])
    p = np.arange(1, n + 1); u = LM + 2 * n
    at = np.concatenate([rng.permutation(LM - 1)[:n], LM + 2 * p - 2, LM + 2 * p - 1, np.array([LM - 1, u, u + 1, u + 2])])
    s = np.concatenate([2 * P + p, p, P + p, np.array([n + 1, n + 2, n + 3, P + n + 3])])
    a = np.full(SI, -1, np.int64); a[at] = s; a[a < 0] = rng.permutation(np.setdiff1d(np.arange(SI), s)); calls[r, g] = a
    return n
def long_values(rng, c, v, r, g, n):
    b = rng.integers(0, 15, 16); A = rng.integers(0, 15, (n, 16)); u = LM + 2 * n; k = LM + 2 * np.arange(n)
    z = np.concatenate([change(rng, np.tile(b[:15], (LM - 2, 1)), np.full(LM - 2, 7)), np.full((LM - 2, 1), (b[15] + 1) % 15)], axis=1)
    c[r, g, :, 0] = b; c[r, g, :, 1:LM - 1] = z; c[r, g, :, LM - 1] = np.where(rng.permutation(16) < 9, 15, b)
    c[r, g, 0, k] = A; c[r, g, 0, k + 1] = (A + 1) % 15; c[r, g, 1, LM:u] = 15
    c[r, g, :, u:u + 2] = 15; c[r, g, :, u + 2] = (b + 1) % 15
    v[r, g, 0] = 15; v[r, g, :, n + 1:n + 4] = b[:, None]
def deep_lists(rng, calls, lens, rid, r, g):
    m = (0, 1, 1, 3)[r % 4]; L = lens[r, g]; n = LM // 2; h = n + 9; p = np.arange(7, h)
    front = np.concatenate([np.flatnonzero(L == x)[:y] for x, y in ((LM, 6), (3, 1), (2, n + 2), (1, 2))])
    lens[r, g] = np.concatenate([L[front], np.delete(L, front)]); rid[r, g] = np.repeat(np.arange(P), lens[r, g])
    quiet = rng.permutation((np.arange(4)[:, None] * P + np.arange(h + 2, h + 66)).reshape(-1))[:5 * LM + m]
    grow = rng.permutation(np.concatenate([2 * P + p[2:], 3 * P + p[2:]]))[:LM - 1 - m]
    s = np.concatenate([quiet[:5 * LM], np.array([6]), grow, quiet[5 * LM:], np.array([2 * P + 7, 2 * P + 8, h]), np.stack([p, P + p], axis=1).reshape(-1), np.array([h + 1, P + h + 1])])
    calls[r, g] = np.concatenate([s, rng.permutation(np.setdiff1d(np.arange(SI), s))])
def deep_values(rng, c, v, lens, rid, r, g):
    w = r % 4; m = (0, 1, 1, 3)[w]; some = (0, LM - 33, 0, LM - 16)[w]; n = LM // 2; h = n + 9; u = 5 * LM; k = u + LM; e = k + 3 + 2 * (n + 2)
    b = rng.integers(0, 15, 16); star = (b + 7) % 15; o = rng.permutation(16)
    stay = np.concatenate([np.array([False]), rng.permutation(np.arange(LM - 3 - m) < some), np.array([False]), np.full(m, w == 3)])
    z = np.tile(b, (LM - 1, 1)); z[:, o[:4]] = (z[:, o[:4]] + rng.integers(0, 2, (LM - 1, 4))) % 15
    half = b.copy(); half[o[8:]] = star[o[8:]]; z[stay] = half
    if w == 1 or w == 2: z[-1, o[4:8]] = (b[o[4:8]] + 1) % 15
    if w == 3: z[-1, o[8]] = b[o[8]]; z[-1, o[0]] = star[o[0]]
    c[r, g, :, :u] = b; c[r, g, 0, u] = star; c[r, g, 1, u] = b; c[r, g, :, u + 1:k] = z
    a = rng.integers(0, 15, 16); A = rng.integers(0, 15, (n + 2, 16)); A[0] = a; t = k + 3 + 2 * np.arange(n + 2)
    c[r, g, 0, k] = a; c[r, g, 0, k + 1] = (a + 1) % 15; c[r, g, 1, k:k + 2] = 15; c[r, g, :, k + 2] = np.where(np.arange(16) == 0, 15, a)
    c[r, g, 0, t] = A; c[r, g, 0, t + 1] = (A + 1) % 15; c[r, g, 1, k + 3:e] = 15
    c[r, g, :, e] = 15; c[r, g, :, e + 1] = (a + 1) % 15
    top = int(np.sum(lens[r, g, :h + 66])); c[r, g, :, e + 2:top] = rng.integers(0, 15, (P, 16))[rid[r, g, e + 2:top]]
    v[r, g, 0] = 15; v[r, g, 0, 6] = a[0]; v[r, g, :, h:h + 2] = a[:, None]
def setup_inputs_crowd(rng):
    calls, lens, rid = lists(rng, 1.0, (D - 1) * P // (LM - 1) // 2); c = np.zeros((N, 8, 2, SI, 16), np.int8); v = formals(rng)
    for r in range(N):
        for g in range(8):
            grow = RO == 4 and g == 7; n = long_lists(rng, calls, lens, rid, r, g) if grow else 0
            deep = RO == 4 and g == 3
            if deep: deep_lists(rng, calls, lens, rid, r, g)
            L = lens[r, g]; d = rid[r, g]; pos = np.arange(SI) - (np.add.accumulate(L) - L)[d]; last = (pos == L[d] - 1)[:, None]
            hot = np.zeros(P, bool); hot[rng.permutation(np.flatnonzero(L >= 2))[:CAP - 1]] = True
            for i in range(2):
                b = rng.integers(0, 15, (P, 16))[d]; x = (b + pos[:, None]) % 15
                if g % 4 == 1: x = np.where(last, b, x)
                if g % 4 == 2 and i == 0: x = np.where(hot[d][:, None], x, b)
                if g % 4 == 3 and i == 0: x = b
                x[:, 13:] = np.where(rng.random((SI, 3)) < 0.5, 15, x[:, 13:])
                c[r, g, i] = x
            if g % 4 >= 2: v[r, g, 0] = 15
            if grow: long_values(rng, c, v, r, g, n)
            if deep: deep_values(rng, c, v, lens, rid, r, g)
    return pack(calls, lens, c, v)
def setup_inputs_calm(rng):
    calls, lens, rid = lists(rng, 3.0, 0); c = np.zeros((N, 8, 2, SI, 16), np.int8); v = formals(rng)
    for r in range(N):
        for g in range(8):
            L = lens[r, g]; d = rid[r, g]; first = np.add.accumulate(L) - L; cs = calls[r, g]
            base = rng.integers(0, 15, (P, 16)); o = np.argsort(rng.random((P, 16)), axis=1)
            one = np.where(o < 6, 15, base); two = np.where((o == 6) | (o == 7), (base + 1) % 15, one)
            c[r, g, 0] = one[d]; c[r, g, 1] = two[d]
            ones = [int(a) for a in rng.permutation(np.flatnonzero(L == 1))]; more = [int(a) for a in rng.permutation(np.flatnonzero(L >= 2))]
            for t in range(RO):
                for i in range((g + r + t) % 4):
                    if len(ones) < t + 1 or len(more) < 1: continue
                    x = more.pop(); ys = [ones.pop() for a in range(max(t, 1))]; by_pass = (i + t + r) % 2 == 0
                    lo = int(first[x]); at = lo + int(L[x]) - 1; b = base[x]
                    c[r, g, :, lo:at + 1] = b
                    if by_pass: c[r, g, :, at] = np.where(rng.permutation(16) < 9, 15, b)
                    else: c[r, g, 1, at] = np.where(rng.permutation(16) < 9, (b + 1) % 15, b)
                    put = [(at, ys[0])] + [(int(first[ys[a]]), ys[a + 1]) for a in range(len(ys) - 1)]
                    for k, s in put:
                        w = int(np.flatnonzero(cs == s)[0]); cs[w] = cs[k]; cs[k] = s
                    for y in ys:
                        if by_pass: v[r, g, :, y] = b
                        else: v[r, g, 0, y] = 15
                    for y in ys[:-1]: c[r, g, :, int(first[y])] = 15
                    if t > 0: c[r, g, :, int(first[ys[-1]])] = (b + 1) % 15
                    elif by_pass: v[r, g, :, ys[0]] = (b + 1) % 15
                    else: v[r, g, 0, ys[0]] = 3
    return pack(calls, lens, c, v)
def check_inputs(d):
    bad = []
    for k, lo, hi in (("jump", 0, 15), ("form", 0, 15), ("calls", 0, SI - 1), ("runs", 1, LM)):
        a = np.asarray(d[k]).astype(np.float64)
        if not (np.min(a) >= lo and np.max(a) <= hi): bad.append("range of " + k)
        if np.any(np.floor(a) != a): bad.append("whole numbers in " + k)
    if np.any(np.sort(np.asarray(d["calls"]), axis=-1) != np.arange(SI)): bad.append("permutation in calls")
    if np.any(np.sum(np.asarray(d["runs"]).astype(np.int64), axis=-1) != SI): bad.append("sum of runs")
    return bad
def reference(jump, form, calls, runs):
    J = jump.astype(np.float32).astype(np.int16).reshape(N, 8, 16, 2 * SI)
    V = np.full((N, 8, 16, PM), 15, np.int16); V[..., :P] = form.astype(np.float32).astype(np.int16).reshape(N, 8, 16, P)
    cnt = np.full((N, 8), P, np.int64); state = {}
    for r in range(N):
        for g in range(8):
            s = calls[r, g].astype(np.int64); state[r, g] = (s, s % P, np.repeat(np.arange(P), runs[r, g]))
    for rnd in range(RO):
        V2 = np.full_like(V, 15); clone = np.full((N, 8, PM), -1, np.int64); mid = {}
        for r in range(N):
            for g in range(8):
                s, c, e = state[r, g]; q = home(r, s)
                F = V[q, g, :, c]
                a = J[q, g, :, s + SI * (F[:, 0] < 15)]; A = np.where(a < 15, a, F)
                first = np.append(True, e[1:] != e[:-1]); at = np.flatnonzero(first); rid = np.add.accumulate(first.astype(np.int64)) - 1
                dis = np.add.reduce((A != A[at[rid]]).astype(np.int64), axis=1) >= 9
                has = np.maximum.reduceat(dis.astype(np.int64), at); before = np.add.accumulate(has) - has
                split = (has == 1) & (before < CAP); num = cnt[r, g] + before
                clone[r, g, e[at[split]]] = num[split]
                mv = dis & split[rid]; e = np.where(mv, num[rid], e)
                o = np.argsort(2 * rid + mv, kind="stable"); s, c, e, A = s[o], c[o], e[o], A[o]
                at = np.flatnonzero(np.append(True, e[1:] != e[:-1]))
                lo = np.minimum.reduceat(A, at, axis=0); hi = np.maximum.reduceat(A, at, axis=0)
                V2[r, g][:, e[at]] = np.where(lo == hi, lo, 15).T
                cnt[r, g] += np.count_nonzero(split); mid[r, g] = (s, c, e)
        for r in range(N):
            for g in range(8):
                s, c, e = mid[r, g]; to = clone[home(r, s), g, c]
                o = np.repeat(np.arange(len(s)), 1 + (to >= 0)); dup = np.append(False, o[1:] == o[:-1])
                state[r, g] = (s[o], np.where(dup, to[o], c[o]), e[o])
        V = V2
    y = np.full((3, N, 8, CM), -1, np.float32)
    for r in range(N):
        for g in range(8):
            for i in range(3): y[i, r, g, :len(state[r, g][i])] = state[r, g][i]
    return {"ysite": y[0], "ycaller": y[1], "ycallee": y[2], "yform": V.reshape(N, 128, PM).astype(np.float32).astype(BF)}

@@ -1,0 +1,745 @@
+from concourse.mybir import AluOpType as OP, AxisListType as AX, ActivationFunctionType as AF
+
+F32, BF, I32, U16 = "float32", "bfloat16", "int32", "uint16"
+NW = 272
+O = 16
+NF, NB, NI, NU = 29, 23, 7, 5
+CJ = (0, 2048, 4096, 1024)
+KO, KF = 16384, 8192
+PAD = KO + 1023
+SCRATCH = {
+    "J": ("sbuf", [128, 4096], BF), "H": ("sbuf", [128, 4096], BF), "TT": ("sbuf", [128, 5120], BF),
+    "TR": ("sbuf", [128, 4096], BF), "A": ("sbuf", [128, 4096], BF), "NQ": ("sbuf", [128, 3584], BF),
+    "S": ("sbuf", [128, 3584], F32), "V": ("sbuf", [128, 4112], F32), "X": ("sbuf", [128, 4624], F32),
+    "WA": ("sbuf", [128, 4112], F32),
+    "CF": ("sbuf", [128, 1040], BF), "RR": ("sbuf", [128, 1024], BF), "BW": ("sbuf", [128, 1024], F32),
+    "GF": ("sbuf", [128, 1024], F32), "RC": ("sbuf", [128, 1024], F32), "EW": ("sbuf", [128, 1024], F32),
+    "N": ("sbuf", [128, NF * NW], F32), "SM": ("sbuf", [128, 12 * 64], F32), "SU": ("sbuf", [128, 12 * 64], U16),
+    "NBF": ("sbuf", [128, NB * NW], BF), "NIN": ("sbuf", [128, NI * NW], I32), "NUN": ("sbuf", [128, NU * NW], U16),
+    "CM": ("sbuf", [128, 15 * 160], F32), "CB": ("sbuf", [128, 48 * 128], BF), "COL": ("sbuf", [128, 56 * 4], F32),
+    "RP": ("sbuf", [128, 3 * 384], F32),
+}
+for _t in range(4):
+    SCRATCH["CT%d" % _t] = ("sbuf", [128, 1024 + 512 + 128 * _t], BF)
+    SCRATCH["TI%d" % _t] = ("sbuf", [128, 512 + 128 * _t], BF)
+for _b in range(8):
+    SCRATCH["P%d" % _b] = ("psum", [128, 512], F32)
+SEMAPHORES = ["ev", "ea", "et", "eg"] + ["d%d" % i for i in range(100)] + ["r%d" % i for i in range(16)] + ["l%d" % i for i in range(16)]
+HOP = 0.15
+
+
+def plan(T, core, nxt, topo):
+    ops = []
+    tiles = {}
+    grp = ["init", ""]
+
+    def V(b, lo, hi, step=1, tag=None, lane=None):
+        rows = slice(None) if lane is None else slice(lane, 128, 16)
+        ap = T[b][rows, lo:hi] if step == 1 else T[b][rows, lo:hi:step]
+        w = SCRATCH[b]
+        if w[0] == "psum":
+            r = (b, 0, 512, None)
+        else:
+            r = (b, lo, hi, ("L", lane) if lane is not None else tag)
+        return {"ap": ap, "r": [r], "n": len(range(lo, hi, step)), "dt": w[2], "ps": w[0] == "psum", "ind": False}
+
+    def tile(b, w):
+        def at(name, lo=0, hi=w, slots=1):
+            d = tiles.setdefault(b, {})
+            if name not in d:
+                d[name] = len(d)
+                if slots > 1:
+                    d[name + "+"] = len(d)
+            return V(b, d[name] * w + lo, d[name] * w + hi)
+        return at
+
+    f, bb, ii, u = tile("N", NW), tile("NBF", NW), tile("NIN", NW), tile("NUN", NW)
+    sm, su, cm, cb, col4 = tile("SM", 64), tile("SU", 64), tile("CM", 160), tile("CB", 128), tile("COL", 4)
+    col = lambda name: col4(name, 0, 1)
+    cf = lambda name, lo=0, hi=128: cm(name, lo, hi)
+    PS = lambda b, lo, hi: V("P%d" % b, lo, hi)
+
+    def IND(w, o):
+        return {"ap": w["ap"].indirect(o["ap"]), "r": w["r"], "o": o["r"], "n": 16 * o["n"], "dt": w["dt"], "ps": False, "ind": True}
+
+    def add(alts, outs, ins, kind="c", lat=0.0):
+        rd, wr = [], []
+        for x in ins:
+            if isinstance(x, dict):
+                (wr if x["ps"] else rd).extend(x["r"])
+                rd.extend(x.get("o", []))
+        for x in outs:
+            wr.extend(x["r"])
+            rd.extend(x.get("o", []))
+        ops.append({"alts": alts, "rd": rd, "wr": wr, "kind": kind, "lat": lat, "g": grp[0] + grp[1]})
+        return len(ops) - 1
+
+    def ap(x):
+        return x["ap"] if isinstance(x, dict) else x
+
+    def vc(o, ins, base=1.0):
+        if o["ind"]:
+            base = SCAT
+        elif any(x["ind"] for x in ins):
+            base = 1.6
+        elif all(x["dt"] in (BF, U16) for x in ins + [o]):
+            base = base / 2
+        return 0.06 + max(64, ins[0]["n"] * base) * 1e-3
+
+    def ac(o, i):
+        return 0.07 + max(64, i["n"] * (SCAT if o["ind"] else 1.6 if i["ind"] else 1.0)) * 1e-3
+
+    def cp(o, i):
+        add([("v", lambda e: e.tensor_copy(o["ap"], i["ap"]), vc(o, [i]))], [o], [i])
+
+    def tt(o, a, b, op):
+        add([("v", lambda e: e.tensor_tensor(o["ap"], a["ap"], b["ap"], op), vc(o, [a, b], 1.0 if a["ps"] or b["ps"] else 2.0))], [o], [a, b])
+
+    def tsf(o, a, s1, o0, s2, o1):
+        if o1 is None:
+            return lambda e: e.tensor_scalar(o["ap"], a["ap"], ap(s1), None, o0)
+        return lambda e: e.tensor_scalar(o["ap"], a["ap"], ap(s1), ap(s2), o0, o1)
+
+    def ts(o, a, s1, o0, s2=None, o1=None):
+        add([("v", tsf(o, a, s1, o0, s2, o1), vc(o, [a]))], [o], [a, s1, s2])
+
+    def scan(o, a, b, init, o0, o1):
+        add([("v", lambda e: e.tensor_tensor_scan(o["ap"], a["ap"], b["ap"], ap(init), o0, o1), vc(o, [a, b]))], [o], [a, b, init])
+
+    def red(o, a, op):
+        add([("v", lambda e: e.tensor_reduce(o["ap"], a["ap"], AX.X, op), 0.06 + max(64, a["n"]) * 1e-3)], [o], [a])
+
+    def ms(o, c):
+        add([("v", lambda e: e.memset(o["ap"], c), vc(o, [o]))], [o], [])
+
+    def act(o, i, fn, bias=0.0, scale=1.0):
+        if o["ind"]:
+            fa = lambda e: e.activation(o["ap"], i["ap"], fn)
+        else:
+            fa = lambda e: e.activation(o["ap"], i["ap"], fn, bias=ap(bias), scale=ap(scale))
+        add([("a", fa, ac(o, i))], [o], [i, bias, scale])
+
+    def aff(o, i, scale=1.0, bias=0.0):
+        add([("a", lambda e: e.activation(o["ap"], i["ap"], AF.Identity, bias=ap(bias), scale=ap(scale)), ac(o, i)),
+             ("v", tsf(o, i, scale, OP.mult, bias, OP.add), vc(o, [i]))], [o], [i, bias, scale])
+
+    def mm(groups, first=True, final=True):
+        def fm(e):
+            for o, lst in groups:
+                for k, (l, r) in enumerate(lst):
+                    last = e.matmul(o["ap"], l["ap"], r["ap"], first and k == 0, final and k == len(lst) - 1)
+            return last
+        c = sum(max(64, r["n"]) * (4 if r["dt"] == F32 else 1) for o, lst in groups for l, r in lst)
+        add([("t", fm, 0.06 + c * 0.6e-3)], [o for o, _ in groups], [x for _, lst in groups for lr in lst for x in lr])
+
+    def mm4(group):
+        for a in range(0, 16, 4):
+            mm([(group[0], group[1][a:a + 4])], a == 0, a == 12)
+
+    def dma(q, o, i, nb=0):
+        add([(q, lambda e: e.dma_start(ap(o), ap(i)), 0.1)], [o] if isinstance(o, dict) else [], [i], "d", 1.9 + nb / 150e3)
+
+    def iota(o, pat, base, chm):
+        kw = {} if o["dt"] == I32 else {"allow_small_or_imprecise_dtypes": True}
+        add([("g", lambda e: e.iota(o["ap"], pat, base, chm, **kw), 0.13 + 2e-3 * o["n"])], [o], [])
+
+    def asel(o, i, step, cmp, base, chm):
+        add([("g", lambda e: e.affine_select(o["ap"], i["ap"], [[step, 128]], cmp, 0.0, base, chm), 0.43)], [o], [i])
+
+    nsend = [0]
+
+    def send(src, dst):
+        k = nsend[0]
+        nsend[0] += 1
+        rid, pid = topo.addr(nxt, core)
+        m = topo.mask(core, nxt)
+        fs = lambda e: e.remote_dma(dst["ap"], src["ap"], T.sem["r%d" % k], T.sem["l%d" % k], pid, rid, m)
+        s = add([("g", fs, 1.0)], [], [src], "s", 1.5 + src["n"] * 256 / 80e3)
+        r = add([(None, None, 0.0)], [dst], [], "r")
+        for x in (s, r):
+            ops[x]["k"] = k
+            ops[x]["cnt"] = len(topo.engines(core, nxt))
+        ops[r]["after"] = s
+
+    dma("s", ii("runb", 0, 32), T.runs[:])
+    dma("a", V("RR", 0, 512), T.form[:], 128e3)
+    for n_, j in enumerate((3, 0, 1, 2)):
+        for sp in range(2):
+            dma("sa"[sp], V("J", j * 1024 + sp * 512, j * 1024 + sp * 512 + 512), T.jump[:, sp * 2048 + j * 512: sp * 2048 + j * 512 + 512], 128e3 * (2 * n_ + 2))
+        if n_ == 0:
+            dma("s", ii("calls", 0, 128), T.calls[:])
+    iota(ii("runb", 64, 65), [[0, 1]], 0, 1)
+    iota(cf("xg"), [[16, 8], [0, 16]], 0, 0)
+    iota(f("ci", 0, 256), [[1, 256]], 0, 0)
+    ts(ii("runb", 68, 69), ii("runb", 64, 65), 15, OP.bitwise_and)
+    ts(ii("runb", 72, 73), ii("runb", 64, 65), 112, OP.bitwise_and)
+    cp(col("lane"), ii("runb", 68, 69))
+    cp(col("g16"), ii("runb", 72, 73))
+    ts(cf("BO"), cf("xg"), col("g16"), OP.is_equal)
+    ts(sm("rm", 0, 16), f("ci", 0, 16), col("lane"), OP.is_equal)
+    rm = lambda i: sm("rm", i, i + 1)
+    ts(cm("xm"), f("ci", 0, 160), col("g16"), OP.subtract)
+    ts(cb("Z", 0, 144, 2), cm("xm", 0, 144), 15.0, OP.is_equal)
+    ts(cb("Z0", 0, 144, 2), cb("Z", 0, 144), rm(0), OP.mult)
+    asel(cf("UT"), cf("BO"), 1, OP.is_gt, 0, -1)
+    asel(cb("ID"), cf("BO"), 1, OP.is_equal, 0, -1)
+    asel(cf("LO"), cf("BO"), -1, OP.is_gt, 0, 1)
+    asel(cf("SH"), cf("BO"), -1, OP.is_equal, -1, 1)
+    ms(f("one", 0, 272), 1.0)
+    ms(bb("one", 0, 272), 1.0)
+    ms(f("zero", 0, 257), 0.0)
+    ms(f("kfc", 0, 129), float(KF))
+    aff(cf("I"), cb("ID"))
+    aff(cf("NI"), cb("ID"), -1.0)
+    aff(cb("NI"), cb("ID"), -1.0)
+    ms(col("m129"), -129.0 / 16)
+    ts(sm("pN"), f("ci", 0, 64), 16.0, OP.mult, col("lane"), OP.add)
+    for lo in range(0, 2064, 516):
+        iota(V("X", lo, lo + 516), [[1, 516]], lo, 0)
+    for nm in ("UT", "LO"):
+        aff(cb(nm), cf(nm))
+        tt(cb(nm + "i"), cb(nm), cb("ID"), OP.add)
+        aff(cb(nm + "b"), cb(nm), -64.0, 64.0)
+    aff(cm("Z3", 0, 144), cb("Z", 0, 144), rm(3))
+    aff(cm("Z4", 0, 144), cb("Z", 0, 144), rm(4))
+
+    def fill(b, lane, w, src="zero"):
+        dma("s", V(b, 0, w, lane=lane), f(src, 0, w // 16), 30e3)
+
+    def conv(out, Zn, src, lo, ncol, band=cb):
+        return (out, [(band(Zn, 15 - i, 143 - i), V(src, lo + i, lo + 16 * ncol, 16)) for i in range(16)])
+
+    def link(tri, out, bank, s2=None):
+        mm([(PS(bank, 0, 128), [(cb("hf"), cb(tri)), (cb("ID"), cb(tri + "b"))]),
+            (PS(bank, 128, 129), [(cb(tri + "i"), cb("hf", 0, 1))])])
+        if s2 is None:
+            ts(out, PS(bank, 0, 128), PS(bank, 128, 129), OP.is_equal)
+        else:
+            ts(out, PS(bank, 0, 128), PS(bank, 128, 129), OP.is_equal, s2, OP.mult)
+
+    def table(t):
+        n = 512 + 128 * t
+        grp[0] = "tab"
+        mm([conv(PS(7, 0, n // 16), "Z0", "CF", 0, n // 16)])
+        ts(sm("jo", 0, n // 16), PS(7, 0, n // 16), 0.5, OP.is_gt, 512.0, OP.mult)
+        tt(sm("jo2", 0, n // 16), sm("jo", 0, n // 16), sm("body", 0, n // 16), OP.add)
+        ts(su("jo", 0, n // 16), sm("jo2", 0, n // 16), 0.25, OP.add)
+        for j in (3, 0, 1, 2):
+            tt(V("TR", j * 1024, j * 1024 + n), IND(V("H", j * 1024, j * 1024 + 1024), su("jo", 0, n // 16)), V("CF", 0, n), OP.min)
+            if j == 3:
+                send(V("TR", 3072, 3072 + n), V("TI%d" % t, 0, n))
+            else:
+                act(V("TT", CJ[j], CJ[j] + n), V("TR", j * 1024, j * 1024 + n), AF.Abs)
+        act(V("TT", CJ[3], CJ[3] + n), V("TI%d" % t, 0, n), AF.Abs)
+
+    def finish(t, thr):
+        K = 128 + 32 * t
+        kf, key = ii("kf", 0, K), ii("key", 0, K)
+        grp[0] = "fin"
+        red(col("nb"), f("v", 0, K), OP.min)
+        ts(cb("hf"), f("zero", 0, 128), col("nb"), OP.add, thr, OP.is_lt)
+        link("UT", cf("LK"), 3)
+        ts(bb("nf", 0, K), kf, KO + KF - 0.5, OP.is_gt)
+        ts(f("fk", 0, K), kf, -float(KO + KF), OP.add, 0.0, OP.min)
+        scan(f("s0", 0, K), bb("nf", 0, K), f("fk", 0, K), 0.0, OP.mult, OP.add)
+        ts(key, kf, KF - 1, OP.bitwise_and)
+        cp(u("key", 0, K), key)
+        mm([(PS(5, 0, 1), [(cf("LK"), f("s0", K - 1, K))])])
+        scan(f("lkn", 0, K), bb("nf", 0, K), f("fk", 0, K), PS(5, 0, 1), OP.mult, OP.add)
+        ts(u("lk", 0, K), f("lkn", 0, K), float(KF), OP.add)
+        grp[0] = "fin2"
+        aff(f("lkey", 0, K), f("lkn", 0, K), 1.0, float(KF))
+        ts(ii("ka", 0, K), kf, 2047, OP.bitwise_and)
+        cp(u("ck", 0, K), ii("ka", 0, K))
+        aff(col("nf0"), bb("nf", 0, 1))
+        mm([(PS(6, 0, 1), [(cf("SH"), col("nf0"))])])
+        aff(bb("nf", K, K + 1), PS(6, 0, 1))
+        ts(su("rev", 0, K // 16), sm("pN", 0, K // 16), -1.0, OP.mult, K - 1.0, OP.add)
+        ts(su("rev", 16, 16 + K // 16), sm("pN", 0, K // 16), -1.0, OP.mult, K + 0.0, OP.add)
+        aff(bb("nlr", 0, K), IND(bb("nf", 0, K + 1), su("rev", 16, 16 + K // 16)))
+        link("LO", cf("LB"), 4, col("nf0"))
+        if t < 3:
+            ts(ii("kb", 0, K), kf, 31744, OP.bitwise_and)
+            cp(bb("kh0", 0, K), ii("kb", 0, K))
+        else:
+            ts(ii("kb", 0, K), kf, 6144, OP.bitwise_and)
+            ts(ii("vi", 0, K), kf, 1024, OP.bitwise_and)
+            ts(bb("t1", 0, K), ii("kb", 0, K), 0.25, OP.mult, 1024.0, OP.add)
+            ts(bb("t2", 0, K), ii("vi", 0, K), 1.5, OP.mult)
+            tt(bb("kh0", 0, K), bb("t1", 0, K), bb("t2", 0, K), OP.add)
+
+    ts(V("CF", 0, 512), V("RR", 0, 512), -1.0, OP.mult, 15.0, OP.add)
+    aff(sm("body", 0, 32), sm("pN", 0, 32))
+    for n_, j in enumerate((3, 0, 1, 2)):
+        ts(V("A", j * 1024, j * 1024 + 1024), V("J", j * 1024, j * 1024 + 1024), 14.5, OP.is_lt, -15.0, OP.mult)
+        for h in range(2):
+            lo = j * 1024 + 512 * h
+            b = 1 + (2 * n_ + h) % 2
+            mm([(PS(b, 0, 512), [(cb("ID"), V("J", lo, lo + 512)), (cb("ID"), V("A", lo, lo + 512))])])
+            act(V("H", lo, lo + 512), PS(b, 0, 512), AF.Identity)
+    ms(V("TT", 512, 1024), 0.0)
+    ms(V("TT", 1536, 2048), 0.0)
+    ms(V("TT", 2560, 4096), 0.0)
+    ms(V("TT", 4608, 5120), 0.0)
+    fill("WA", 0, 2064, "kfc")
+    cp(sm("runb", 0, 32), ii("runb", 0, 32))
+    scan(sm("rs", 0, 32), f("one", 0, 32), sm("runb", 0, 32), 0.0, OP.mult, OP.add)
+    mm([(PS(5, 0, 1), [(cf("UT"), sm("rs", 31, 32))])])
+    tt(sm("rs2", 0, 32), sm("rs", 0, 32), sm("runb", 0, 32), OP.subtract)
+    ts(su("st", 0, 32), sm("rs2", 0, 32), PS(5, 0, 1), OP.add, float(O), OP.add)
+    ms(V("RC", 0, 512), 0.0)
+    act(IND(V("WA", 0, 2064), su("st", 0, 32)), V("RC", 0, 512), AF.Silu)
+    dma("s", f("v", 0, 128), V("WA", O, O + 2048, lane=0))
+    ts(ii("ka", 0, 128), ii("calls", 0, 128), 9, OP.logical_shift_right)
+    ts(f("t1", 0, 128), ii("ka", 0, 128), 1536.0, OP.mult, float(KO), OP.add)
+    ts(f("t2", 0, 128), ii("calls", 0, 128), 1535.5, OP.is_gt, -5120.0, OP.mult)
+    tt(f("t3", 0, 128), f("t1", 0, 128), ii("calls", 0, 128), OP.add)
+    tt(f("t1", 0, 128), f("t3", 0, 128), f("t2", 0, 128), OP.add)
+    tt(ii("kf", 0, 128), f("t1", 0, 128), f("v", 0, 128), OP.add)
+    table(0)
+    finish(0, 1.0)
+    grp[0] = "init1"
+    ms(V("EW", 0, 1024), 0.0)
+    cp(sm("rs", 0, 32), su("st", 0, 32))
+    tt(sm("rs2", 0, 32), sm("rs", 0, 32), sm("runb", 0, 32), OP.add)
+    dma("s", V("EW", 0, 512, lane=3), sm("rs2", 0, 32))
+    dma("s", V("EW", 512, 1024, lane=3), sm("rs", 0, 32))
+    mm4(conv(PS(7, 0, 64), "Z3", "EW", 0, 64, cm))
+    ts(su("end", 0, 32), PS(7, 0, 32), -1.0, OP.add)
+    cp(su("stw", 0, 32), PS(7, 32, 64))
+    aff(f("ec", 0, 128), f("t1", 0, 128), 1.0, -float(KO))
+    dma("s", V("X", O, O + 2048, lane=4), f("ec", 0, 128))
+    aff(V("EW", 0, 512), IND(V("X", 0, 2064), su("stw", 0, 32)))
+    mm4(conv(PS(7, 0, 32), "Z4", "EW", 0, 32, cm))
+    cp(su("LK", 0, 32), PS(7, 0, 32))
+    grp[0] = "init2"
+    for lo in range(2064, 3600, 512):
+        iota(V("X", lo, lo + 512), [[1, 512]], lo, 0)
+    for ln in range(5, 12):
+        fill("X", ln, 3600)
+    aff(col("m56"), rm(5), 1.0, rm(6))
+    aff(col("w56"), rm(5), 16.0, rm(6))
+    aff(col("m12"), rm(1), 1.0, rm(2))
+    aff(col("o12"), col("m12"), 32.0)
+    aff(col("o56"), col("m56"), 32.0, col("o12"))
+    aff(col("hi"), rm(5), 1.0, rm(10))
+    aff(col("lo"), rm(6), 1.0, rm(11))
+    aff(col("wab"), rm(10), 16.0, rm(11))
+    aff(col("wa7"), rm(7), 1.0, col("wab"))
+    aff(col("w0c"), rm(0), 1.0, rm(12))
+    aff(col("w08"), rm(0), 1.0, rm(8))
+    aff(col("w089"), rm(9), 1.0, col("w08"))
+    aff(col("pc1"), rm(10), 63.0)
+    aff(col("pc2"), rm(11), 15.0, col("pc1"))
+    aff(col("padc"), rm(12), float(KO), col("pc2"))
+    for h in range(2):
+        iota(V("GF", 512 * h, 512 * h + 512), [[1, 32], [0, 16]], 32 * h, 0)
+    iota(V("RC", 512, 1024), [[0, 32], [1, 16]], 0, 0)
+    aff(V("BW", 0, 512), V("GF", 0, 512), col("hi"), col("o56"))
+    aff(V("BW", 512, 1024), V("GF", 512, 1024), rm(10), col("o12"))
+    aff(V("GF", 0, 512), V("RC", 512, 1024), col("lo"))
+    aff(V("GF", 512, 1024), V("RC", 512, 1024), rm(11))
+    for h in range(2):
+        tt(V("BW", 512 * h, 512 * h + 512), V("BW", 512 * h, 512 * h + 512), V("GF", 512 * h, 512 * h + 512), OP.add)
+    aff(cf("R1"), cf("BO"), rm(1))
+    aff(cf("R2"), cf("BO"), rm(2))
+    aff(cf("R5"), cf("BO"), col("w56"))
+    aff(cb("MC"), cb("Z", 14, 142), col("w0c"))
+    aff(cb("M2"), cb("Z", 15, 143), col("wab"))
+    tt(cb("MC"), cb("MC"), cb("M2"), OP.add)
+    aff(cb("M1"), cb("Z", 14, 142), col("w089"))
+    aff(cb("M2"), cb("Z", 15, 143), col("w56"))
+    tt(cb("M1"), cb("M1"), cb("M2"), OP.add)
+    aff(cb("M2"), cb("Z", 13, 141), col("wa7"))
+    tt(cb("M1"), cb("M1"), cb("M2"), OP.add)
+    ms(f("nod", 0, 257), 40000.0)
+    ms(f("W", 0, 4), 0.0)
+    iota(V("RP", 384, 768), [[0, 24], [1, 16]], 0, 0)
+    ts(V("RP", 0, 384), V("RP", 384, 768), col("lane"), OP.is_equal)
+    ts(V("RP", 384, 768), V("RP", 384, 768), 0.5, OP.is_gt)
+    for i in range(16):
+        aff(cb("C%d" % i), cf("BO"), rm(i))
+    for i in range(16):
+        aff(cb("A%d" % i), cb("Z", 15, 143), rm(i))
+    ms(V("V", 0, O), 0.0)
+    ms(V("CF", 1024, 1040), 0.0)
+    ms(col("len"), 2048.0 - 2048 - 2560 - 3072 - 3584)
+    ms(col("gs"), 0.0)
+    aff(col("b0"), rm(0), -544.0)
+    aff(col("b2"), rm(2), 1024.0, col("b0"))
+
+    for t in range(4):
+        K = 128 + 32 * t
+        L, n, K2, q = 16 * K, 512 + 128 * t, K + 32, K // 4
+        L2, last, nc = 16 * K2, t == 3, n // 16
+        N = lambda name: f(name, 0, K)
+        B = lambda name: bb(name, 0, K)
+        CT = "CT%d" % t
+        Tw = V("TT", 0, 4096 + n)
+        Xw, Vw = V("X", 0, L + O), V("V", 0, L + O)
+        rev = su("rev", 0, K // 16)
+        grp[0], grp[1] = "prep", "3" if last else ""
+        for lo in range(n, 1024, 256):
+            aff(V(CT, lo, min(lo + 256, 1024)), f("one", 0, min(256, 1024 - lo)), col("padc"))
+        aff(V("RC", 0, 128), f("one", 0, 128), 32.0)
+        if last:
+            for ln in range(3):
+                fill("WA", ln, L2 + O)
+            aff(col("bias"), rm(1), n + 128.0 + 1024, col("b2"))
+        else:
+            fill("WA", 0, L2 + O, "nod")
+            fill("WA", 1, L2 + O, "nod")
+            aff(col("bias"), rm(1), KO + KF + n + 128.0)
+            aff(col("lk2"), col("lane"), -float(K2))
+        grp[0] = "arg"
+        for c in range(4):
+            act(V("A", 16 * q * c, 16 * q * (c + 1)), IND(Tw, u("key", q * c, q * c + q)), AF.Identity)
+            tt(V("NQ", 16 * q * c, 16 * q * (c + 1)), IND(Tw, u("lk", q * c, q * c + q)), V("A", 16 * q * c, 16 * q * (c + 1)), OP.not_equal)
+            if c == 2:
+                mm([conv(PS(0, 0, 3 * q), "Z", "NQ", 0, 3 * q)])
+        mm([conv(PS(0, 3 * q, K), "Z", "NQ", 48 * q, q)])
+        grp[0] = "n1"
+        ts(B("dis"), PS(0, 0, K), 8.5, OP.is_gt)
+        scan(N("s0"), B("nf"), B("dis"), 0.0, OP.mult, OP.add)
+        mm([(PS(5, 0, 1), [(cf("LK"), f("s0", K - 1, K))])])
+        scan(bb("s1", 8, K + 8), B("nf"), B("dis"), PS(5, 0, 1), OP.mult, OP.add)
+        cp(bb("s1", 7, 8), PS(5, 0, 1))
+        tt(B("fd"), B("dis"), bb("s1", 7, K + 7), OP.is_gt)
+        scan(N("cum"), B("one"), B("fd"), 0.0, OP.mult, OP.add)
+        mm([(PS(5, 0, 1), [(cf("UT"), f("cum", K - 1, K)), (cf("BO"), col("m129"))]), (PS(5, 1, 2), [(cf("BO"), f("cum", K - 1, K))])])
+        tt(N("fk"), B("fd"), ii("key", 0, K), OP.mult)
+        scan(N("s0"), B("nf"), N("fk"), 0.0, OP.mult, OP.add)
+        mm([(PS(6, 0, 1), [(cf("LK"), f("s0", K - 1, K))])])
+        act(B("has"), bb("s1", 8, K + 8), AF.Sign)
+        ts(B("rn"), N("cum"), PS(5, 0, 1), OP.add, 0.0, OP.min)
+        ts(B("ok"), N("cum"), PS(5, 0, 1), OP.add, -0.5, OP.is_lt)
+        ts(col("cnt"), PS(5, 1, 2), 128.0, OP.min)
+        tt(N("r1"), B("rn"), B("has"), OP.mult)
+        dma("s", V("X", O, O + L, lane=0), N("r1"))
+        if not last:
+            act(N("nd"), N("r1"), AF.Relu, float(KO), float(KO))
+            dma("a", V("X", O, O + L, lane=12), N("nd"))
+        scan(N("fkg"), B("nf"), N("fk"), PS(6, 0, 1), OP.mult, OP.add)
+        dma("s", V("X", O, O + L, lane=1), N("fkg"))
+        tt(B("mv"), B("ok"), B("dis"), OP.mult)
+        grp[0] = "nl"
+        mm([(PS(3, 0, K), [(cf("I"), N("fkg")), (cf("NI"), N("lkey"))])])
+        tt(N("t1"), PS(3, 0, K), B("mv"), OP.mult)
+        mm([(PS(4, 0, K), [(cf("I"), N("t1")), (cf("I"), N("lkey"))])])
+        cp(u("nl", 0, K), PS(4, 0, K))
+        grp[0] = "m"
+        aff(col("mv0"), bb("mv", 0, 1))
+        mm([(PS(6, 0, 1), [(cf("SH"), col("mv0"))])])
+        aff(B("wi"), B("mv"), 511.0 / 512, 1.0 / 512)
+        aff(bb("wi", K, K + 1), PS(6, 0, 1), 511.0 / 512, 1.0 / 512)
+        aff(B("t1"), B("mv"), -511.0, 512.0)
+        tt(B("t2"), B("t1"), B("nf"), OP.mult)
+        tt(B("m"), B("t2"), bb("wi", 1, K + 1), OP.mult)
+        aff(B("st"), B("mv"), -1.0, 1.0)
+        aff(B("str"), IND(B("mv"), rev), -1.0, 1.0)
+        if not last:
+            aff(B("t3"), B("fd"), -float(KF))
+            tt(B("t4"), B("t3"), B("ok"), OP.mult)
+            tt(B("kh0"), B("t4"), B("kh0"), OP.add)
+        grp[0] = "ct"
+        if OPT["ct"]:
+            tt(V(CT, 0, n), IND(Xw, su("end", 0, nc)), V("BW", 0, n), OP.add)
+        else:
+            for lo, hi in ((0, nc // 2), (nc // 2, nc)):
+                tt(V("GF", 16 * lo, 16 * hi), IND(Xw, su("end", lo, hi)), V("BW", 16 * lo, 16 * hi), OP.add)
+                act(V(CT, 16 * lo, 16 * hi), V("GF", 16 * lo, 16 * hi), AF.Identity)
+        send(V(CT, 0, n), V(CT, 1024, 1024 + n))
+        grp[0] = "cl"
+        if OPT["ct"]:
+            tt(V("GF", 0, n), IND(Xw, su("end", 0, nc)), V("BW", 0, n), OP.add)
+        mm([conv(PS(7, 0, nc), "Z0", CT, 0, nc)])
+        ts(sm("pa", 0, nc), PS(7, 0, nc), -0.5, OP.is_gt)
+        tt(sm("pb", 0, nc), sm("pa", 0, nc), sm("pN", 0, nc), OP.mult)
+        tt(sm("pa", 0, nc), sm("pb", 0, nc), PS(7, 0, nc), OP.add)
+        ts(su("po", 0, nc), sm("pa", 0, nc), 128.0, OP.add)
+        act(IND(V("RC", 0, 128 + n), su("po", 0, nc)), V("GF", 0, n), AF.Silu)
+        grp[0] = "rep"
+        mm([(PS(7, 128 * a, 128 * a + 128), [(cf(nm), V("RC", 0, 128))]) for a, nm in enumerate(("R1", "R2", "R5"))])
+        tt(V("RP", 768, 1152), PS(7, 0, 384), V("RP", 0, 384), OP.mult)
+        scan(V("GF", 0, 384), V("RP", 384, 768), V("RP", 768, 1152), 0.0, OP.mult, OP.add)
+        ts(su("LK", nc, nc + 8), V("GF", 15, 128, 16), -31.75, OP.add)
+        ts(su("E", 0, 8), V("GF", 143, 256, 16), -31.75, OP.add)
+        grp[0] = "cl2"
+        aff(col("gap%d" % t), col("cnt"), -1.0, 128.0)
+        if not last:
+            aff(sm("body", nc, nc + 8), V("GF", 271, 384, 16), 1.0, -544.0)
+            aff(col("g7"), col("gs"), rm(7))
+            aff(cf("xg"), V("RC", 0, 128), col("m56"), col("g7"))
+            tt(V("BW", n, n + 128), V("BW", n, n + 128), cf("xg"), OP.add)
+            if t == 2:
+                aff(col("g8"), col("gs"), rm(8))
+                aff(col("g9"), col("gap2"), -1.0)
+                aff(col("g7"), col("g9"), rm(9), col("g8"))
+                aff(V("BW", 0, n + 128), V("BW", 0, n + 128), 1.0, col("g7"))
+        aff(col("gs"), col("gap%d" % t), -1.0, col("gs"))
+        aff(col("cum%d" % t), col("gs"), 1.0, n + 128.0)
+        grp[0] = "nq2"
+        for c, lo in enumerate(range(0, L, 512)):
+            if c < OPT["nq"]:
+                tt(V("NQ", lo, lo + 512), IND(Tw, u("nl", 32 * c, 32 * c + 32)), V("A", lo, lo + 512), OP.not_equal)
+            else:
+                act(V("TR", lo, lo + 512), IND(Tw, u("nl", 32 * c, 32 * c + 32)), AF.Identity)
+                mm([(PS(3 + c % 2, 0, 512), [(cb("ID"), V("A", lo, lo + 512)), (cb("NI"), V("TR", lo, lo + 512))])])
+                ts(V("NQ", lo, lo + 512), PS(3 + c % 2, 0, 512), 0.0, OP.not_equal)
+        grp[0] = "scan"
+        for i in range(0, 16, 2):
+            b = 1 + (i // 2) % 2
+            mm([(PS(b, 256 * h, 256 * h + K), [(cb("C%d" % (i + h)), B("m"))]) for h in range(2)])
+            for h in range(2):
+                lo = O + (i + h) * K
+                scan(V("V", lo, lo + K), V("NQ", i + h, L, 16), PS(b, 256 * h, 256 * h + K), V("V", lo - 1, lo), OP.add, OP.mult)
+        grp[0] = "cf"
+        o_, i_ = V("RR", 0, n), IND(Vw, su("end", 0, nc))
+        add([("a", lambda e, o=o_, i=i_: e.activation(o["ap"], i["ap"], AF.Relu, bias=230.0, scale=-256.0), ac(o_, i_)),
+             ("v", tsf(o_, i_, 0.9, OP.is_lt, 16.0, OP.mult), vc(o_, [i_]))], [o_], [i_])
+        tt(V("CF", 0, n), IND(Tw, su("LK", 0, nc)), V("RR", 0, n), OP.min)
+        cp(ii("vi", 0, 128), IND(Vw, su("E", 0, 8)))
+        tt(bb("eq", 0, 128), IND(Vw, su("E", 0, 8)), ii("vi", 0, 128), OP.is_equal)
+        tt(V("CF", n, n + 128), IND(Tw, su("LK", nc, nc + 8)), bb("eq", 0, 128), OP.mult)
+        if not last:
+            table(t + 1)
+        Cw = V(CT, 0, 1024 + n)
+        for c in range(4):
+            grp[0] = "j%d" % c
+            aff(V("J", 16 * q * c, 16 * q * (c + 1)), IND(Cw, u("ck", q * c, q * c + q)))
+            if c % 2:
+                mm([conv(PS(0, q * (c - 1), q * (c + 1)), "Z0", "J", 16 * q * (c - 1), 2 * q)])
+        grp[0] = "n2"
+        ts(B("w"), PS(0, 0, K), -0.5, OP.is_lt, 1.0, OP.add)
+        tt(B("wsr"), IND(B("w"), rev), B("str"), OP.mult)
+        tt(B("wm"), B("w"), B("mv"), OP.mult)
+        Wi = f("W", 4, K + 4)
+        scan(Wi, B("one"), B("w"), 0.0, OP.mult, OP.add)
+        scan(N("s0"), B("nlr"), B("wsr"), 0.0, OP.mult, OP.add)
+        scan(N("cum"), B("nf"), B("wm"), 0.0, OP.mult, OP.add)
+        mm([(PS(5, 0, 1), [(cf("LB"), f("s0", K - 1, K))])])
+        mm([(PS(6, 0, 1), [(cf("LK"), f("cum", K - 1, K))]), (PS(6, 1, 2), [(cf("UT"), f("W", K + 3, K + 4))]),
+            (PS(6, 2, 3), [(cf("BO"), f("W", K + 3, K + 4))])])
+        scan(N("rs1"), B("nlr"), B("wsr"), PS(5, 0, 1), OP.mult, OP.add)
+        scan(N("sm1"), B("nf"), B("wm"), PS(6, 0, 1), OP.mult, OP.add)
+        tt(N("t1"), IND(N("rs1"), rev), B("mv"), OP.mult)
+        tt(N("t2"), N("sm1"), B("st"), OP.mult)
+        tt(N("t3"), f("W", 3, K + 3), N("t2"), OP.subtract)
+        tt(N("t2"), N("t3"), N("t1"), OP.add)
+        ts(u("pos", 0, K), N("t2"), PS(6, 1, 2), OP.add, float(O), OP.add)
+        grp[0] = "end"
+        aff(col("cw"), PS(6, 1, 2), 1.0, O - 1.0)
+        if not last:
+            aff(col("thr"), PS(6, 2, 3), 1.0, col("lk2"))
+            ts(f("real", 0, K2), f("ci", 0, K2), col("thr"), OP.is_lt, 65536.0, OP.mult)
+            aff(f("cap", 0, K2), f("real", 0, K2), 1.0, float(PAD))
+        aff(col("len"), PS(6, 2, 3), 1.0, col("len"))
+        aff(N("ec"), Wi, 1.0, col("cw"))
+        if OPT["ep"]:
+            mm([(PS(5, 0, K), [(cf("I"), Wi), (cf("NI"), N("sm1"))])])
+            aff(N("ep"), PS(5, 0, K), 1.0, col("cw"))
+        else:
+            tt(N("ep"), N("ec"), N("sm1"), OP.subtract)
+        dma("s", V("X", O, O + L, lane=4), N("ec"))
+        dma("s", V("X", O, O + L, lane=3), N("ep"))
+        for i in range(0, 16, 2):
+            b = 3 + (i // 2) % 2
+            grp[0] = "s"
+            mm([(PS(b, 256 * h, 256 * h + K), [(cb("A%d" % (i + h)), B("kh0")),
+                                               (cb("M1" if last else "MC"), V("J", i + h, L, 16))]) for h in range(2)])
+            for h in range(2):
+                grp[0] = "s%d" % (b - 3)
+                aff(V("S", i + h, L, 16, tag=i + h), PS(b, 256 * h, 256 * h + K), 1.0, col("bias"))
+        grp[0] = "sc"
+        ka = LAST if last else K
+        act(IND(V("WA", 0, L2 + O), u("pos", 0, ka)), V("S", 0, 16 * ka), AF.Silu)
+        if last:
+            for ln in range(3):
+                fill("V", ln, L2 + O)
+            cp(IND(V("V", 0, L2 + O), u("pos", ka, K)), V("S", 16 * ka, L))
+        M = lambda name: f(name, 0, K2)
+        I = lambda name: ii(name, 0, K2)
+        got = [("pv", 0, O - 1), ("rk", 1, O - 1), ("v", 0, O)] + ([("bd", 2, O)] if last else [])
+        for k_, (nm, ln, lo) in enumerate(got):
+            dma("as"[k_ % 2], M(nm), V("WA", lo, lo + L2, lane=ln))
+        if last:
+            for nm, (_, ln, lo) in zip(("fkg", "lkey", "lkn", "nd"), got):
+                dma("s", M(nm), V("V", lo, lo + L2, lane=ln))
+        grp[0] = "ew"
+        aff(V("EW", 0, n), IND(Xw, su("end", 0, nc)))
+        aff(V("EW", n, n + 128), IND(Xw, su("E", 0, 8)))
+        mm4(conv(PS(7, 0, nc), "Z3", "EW", 0, nc, cm))
+        mm4(conv(PS(7, nc, nc + 8), "Z4", "EW", n, 8, cm))
+        if not last:
+            cp(su("end", 0, nc + 8), PS(7, 0, nc + 8))
+            grp[0] = "n3"
+            cp(I("ka"), M("pv"))
+            tt(M("t1"), M("v"), M("cap"), OP.min)
+            ts(I("kb"), I("ka"), 7168, OP.bitwise_and)
+            tt(M("t3"), M("rk"), I("kb"), OP.add)
+            tt(I("kf"), M("t3"), M("t1"), OP.min)
+            finish(t + 1, KO + KF - 0.5)
+            continue
+        ts(col("thr"), col("lane"), -256.0, OP.mult, col("len"), OP.add)
+        ts(M("cap"), M("ci"), col("thr"), OP.is_lt, 65536.0, OP.mult)
+        grp[0] = "yf"
+        acc = sm("pN")
+        for s in range(4):
+            ts(sm("pa"), sm("pN"), col("cum%d" % s), OP.is_ge, col("gap%d" % s) if s < 3 else 1024.0, OP.mult)
+            tt(sm("pb"), acc, sm("pa"), OP.add)
+            acc = sm("pb")
+        ts(su("yo"), acc, 1024.0, OP.min)
+        aff(V("RR", 0, 1024), IND(V("CF", 0, 1040), su("yo")), -1.0, 15.0)
+        dma("s", T.yform[:], V("RR", 0, 1024), 256e3)
+        grp[0] = "ye"
+        ts(sm("rs"), PS(7, 0, 64), 0.5, OP.is_lt)
+        aff(sm("pc"), sm("pN"), 1.0, 4112.0 - 512)
+        tt(sm("pc"), sm("pc"), sm("rs"), OP.mult)
+        tt(sm("rs"), sm("pc"), PS(7, 0, 64), OP.add)
+        cp(su("eo"), sm("rs"))
+        aff(V("GF", 0, 640), V("X", 0, 640), 1.0, 1.0)
+        for s in range(1, 4):
+            lo = 512 + 128 * s
+            ts(V("GF", lo, lo + 128), V("X", lo, lo + 128), col("cum%d" % (s - 1)), OP.add, 1.0 - lo, OP.add)
+        fill("X", 2, 4112)
+        cp(IND(V("X", 0, 4624), su("eo")), V("GF", 0, 1024))
+        dma("s", M("ec"), V("X", O, O + 4096, lane=2))
+        ts(su("rev", 32, 48), sm("pN", 0, 16), -1.0, OP.mult, 255.0, OP.add)
+        red(col("nb"), M("ec"), OP.max)
+        ts(cb("hf"), f("zero", 0, 128), col("nb"), OP.add, 0.5, OP.is_gt)
+        link("LO", cf("LB"), 4)
+        cp(M("fk"), IND(M("ec"), su("rev", 32, 48)))
+        ts(bb("nlr", 0, 256), M("fk"), 0.5, OP.is_lt)
+        scan(M("s0"), bb("nlr", 0, 256), M("fk"), 0.0, OP.mult, OP.add)
+        mm([(PS(5, 0, 1), [(cf("LB"), f("s0", 255, 256))])])
+        scan(M("rs1"), bb("nlr", 0, 256), M("fk"), PS(5, 0, 1), OP.mult, OP.add)
+        aff(M("ep"), IND(M("rs1"), su("rev", 32, 48)), 1.0, -1.0)
+        dma("s", T.ycallee[:], M("ep"))
+        grp[0] = "ys"
+        tt(M("v"), M("v"), M("lkn"), OP.add)
+        act(M("t1"), M("v"), AF.Relu, 1.0, -1.0)
+        tt(M("pv"), M("pv"), M("fkg"), OP.add)
+        tt(M("rk"), M("rk"), M("lkey"), OP.add)
+        tt(M("bd"), M("bd"), M("nd"), OP.add)
+        for y, q_, a, b, i_, t_ in ((T.ysite, "s", "pv", "v", "ka", "t2"), (T.ycaller, "a", "rk", "bd", "kb", "t3")):
+            tt(M(t_), M(a), M("t1"), OP.mult)
+            tt(I(i_), M(t_), M(b), OP.add)
+            tt(M(a), I(i_), M("cap"), OP.min)
+            ts(M(t_), M(a), 1023.0, OP.max, -1024.0, OP.add)
+            dma(q_, y[:], M(t_))
+    return ops
+
+
+def order(ops):
+    hist = {}
+    for k, o in enumerate(ops):
+        dep = set()
+        for acc, w in ((o["rd"], False), (o["wr"], True)):
+            for b, lo, hi, tag in acc:
+                for k2, w2, lo2, hi2, tag2 in hist.get(b, []):
+                    if (w or w2) and lo < hi2 and lo2 < hi and (tag is None or tag2 is None or tag == tag2):
+                        dep.add(k2)
+        dep.discard(k)
+        for b, lo, hi, tag in o["wr"]:
+            h = hist.setdefault(b, [])
+            h[:] = [e for e in h if not (lo <= e[2] and e[3] <= hi and (tag is None or tag == e[4]))]
+            h.append((k, True, lo, hi, tag))
+        for b, lo, hi, tag in o["rd"]:
+            hist.setdefault(b, []).append((k, False, lo, hi, tag))
+        o["dep"] = sorted(dep)
+        o["pre"] = o["dep"] + ([o["after"]] if "after" in o else [])
+    succ = [[] for _ in ops]
+    for k, o in enumerate(ops):
+        for d in o["pre"]:
+            succ[d].append(k)
+    pr = [0.0] * len(ops)
+    for k in range(len(ops) - 1, -1, -1):
+        pr[k] = ops[k]["alts"][0][2] + ops[k]["lat"] + HOP + max([pr[s] for s in succ[k]] + [0.0])
+    for k, o in enumerate(ops):
+        pr[k] += BOOST.get(o["g"], 0.0)
+        o["bias"] = BIAS.get(o["g"], 2.0)
+    left = [len(o["pre"]) for o in ops]
+    ready = [k for k in range(len(ops)) if left[k] == 0]
+    free, done, at, seq = {}, [0.0] * len(ops), [0.0] * len(ops), []
+    while ready:
+        pick = {}
+        for k in ready:
+            best = None
+            for n_, (q, fn, c) in enumerate(ops[k]["alts"]):
+                s = max(free.get(q, 0.0), at[k])
+                if best is None or s + c + ops[k]["bias"] < best[0] + best[3]:
+                    best = (s, q, fn, c)
+            pick[k] = best
+        k0 = min(ready, key=lambda k: (pick[k][0], -pr[k]))
+        s0, q0 = pick[k0][0], pick[k0][1]
+        k = max([x for x in ready if pick[x][1] == q0 and pick[x][0] <= s0 + min(LOOK, 0.3 * pick[k0][3] + 0.05)], key=lambda x: pr[x])
+        o = ops[k]
+        s, o["q"], o["fn"], o["cost"] = pick[k]
+        if o["q"] is not None:
+            free[o["q"]] = s + o["cost"]
+        done[k] = s + o["cost"] + o["lat"]
+        o["t"] = (s, done[k])
+        ready.remove(k)
+        seq.append(k)
+        for x in succ[k]:
+            left[x] -= 1
+            at[x] = max(at[x], done[k] + HOP)
+            if left[x] == 0:
+                ready.append(x)
+    return seq
+
+
+BOOST = {'ct': 22, 'cl': 7, 'j0': 16, 'j1': 6, 'n2': 14, 's': 26, 's0': 4, 's1': 10, 'sc': 17, 'scan': -5, 'cf': -9, 'prep': -15, 'ew': -8,
+         'ct3': 39, 'j03': 23, 'j13': 8, 'j23': -15, 'j33': 1, 'n23': 10, 's3': -4, 's03': 5, 's13': 22, 'sc3': 2, 'scan3': -4, 'cf3': 7,
+         'prep3': -3, 'ew3': 5, 'arg': 9, 'nq23': -2, 'n1': -6, 'fin2': -1, 'ye3': 4, 'cl2': 6, 'm3': -11, 'rep': 2, 'rep3': 5, 'cl23': 4,
+         'end': -6, 'm': 8, 'n13': 21, 'arg3': -19, 'nq2': -3, 'yf3': -2, 'init': 8, 'j3': -6, 'nl3': 20, 'ys3': -5, 'n3': 11, 'cl3': 3,
+         'end3': -19, 'nl': -1, 'fin': -5, 'init1': -1, 'j2': 18}
+BIAS = {'j0': 1, 'j1': 0, 'j2': 2, 'j3': 4, 'cf': 0, 's0': 1, 's1': 0.3, 'j03': -1, 'j13': 4, 'j23': 4, 'j33': 4, 'cf3': 4, 's03': 2,
+        's13': 4, 'ew3': 2, 'prep3': 50, 'cl2': 0.3, 'ye3': 1, 'yf3': 50, 'm3': 0, 'end3': 1, 'cl23': 0, 'fin2': 2, 'init1': 2,
+        'init2': 50, 'prep': 1, 'm': 4, 'init': 0.3, 'ew': 50}
+LOOK, LAST, SCAT, OPT = 0.3, 128, 3.8, {"ct": 0, "ep": 1, "nq": 9}
+
+
+def rank_program(g, core, T, topo):
+    rank = T.rank_of(core)
+    if rank is None:
+        return
+    nxt = T.cores[(rank + 1) % len(T.cores)]
+    ops = plan(T, core, nxt, topo)
+    seq = order(ops)
+    Q = {"v": g.vector, "a": g.scalar, "t": g.tensor, "g": g, "s": g.sync}
+    count, seen, top, nd = {}, {q: {} for q in Q}, {}, [0]
+    for k in seq:
+        o = ops[k]
+        if o["kind"] == "r":
+            o["sig"] = ("r%d" % o["k"], o["cnt"])
+            top[o["sig"][0]] = o["cnt"]
+            continue
+        q = o["q"]
+        need = {}
+        for d in o["dep"]:
+            s, val = ops[d]["sig"]
+            if q == "t" and s == "et":
+                continue
+            need[s] = max(need.get(s, 0), val)
+        for s in sorted(need):
+            if seen[q].get(s, 0) < need[s]:
+                Q[q].wait_ge(T.sem[s], need[s])
+                seen[q][s] = need[s]
+        ins = o["fn"](Q[q])
+        if o["kind"] == "c":
+            s = "e" + q
+            count[s] = count.get(s, 0) + 1
+            ins.then_inc(T.sem[s], 1)
+            o["sig"] = (s, count[s])
+        elif o["kind"] == "d":
+            s = "d%d" % nd[0]
+            nd[0] += 1
+            ins.then_inc(T.sem[s], 16)
+            o["sig"] = (s, 16)
+        else:
+            o["sig"] = ("l%d" % o["k"], o["cnt"])
+        top[o["sig"][0]] = o["sig"][1]
+    for s in sorted(top):
+        if all(seen[q].get(s, 0) < top[s] for q in Q):
+            g.wait_ge(T.sem[s], top[s])

@@ -1,31 +1,35 @@
 from concourse.mybir import AluOpType as OP, AxisListType as AX, ActivationFunctionType as AF
 
-F32, BF, I32, U16 = "float32", "bfloat16", "int32", "uint16"
+F32, BF, I32, U16, F16 = "float32", "bfloat16", "int32", "uint16", "float16"
 NW = 272
 O = 16
-NF, NB, NI, NU = 29, 23, 7, 5
+NF, NB, NI, NU, NH = 20, 23, 4, 5, 8
 CJ = (0, 2048, 4096, 1024)
-KO, KF = 16384, 8192
-PAD = KO + 1023
+KO = 8192
+NFB = 16384
+PAD = KO + 5119
+JP = 131072.0
+MAGIC = 12582912.0
 SCRATCH = {
-    "J": ("sbuf", [128, 4096], BF), "H": ("sbuf", [128, 4096], BF), "TT": ("sbuf", [128, 5120], BF),
+    "J": ("sbuf", [128, 4096], BF), "H": ("sbuf", [128, 4096], BF), "TT": ("sbuf", [128, 5136], BF),
     "TR": ("sbuf", [128, 4096], BF), "A": ("sbuf", [128, 4096], BF), "NQ": ("sbuf", [128, 3584], BF),
-    "S": ("sbuf", [128, 3584], F32), "V": ("sbuf", [128, 4112], F32), "X": ("sbuf", [128, 4624], F32),
-    "WA": ("sbuf", [128, 4112], F32),
+    "S": ("sbuf", [128, 3600], F32), "V": ("sbuf", [128, 3600], F32), "X": ("sbuf", [128, 4128], F32),
+    "WA": ("sbuf", [128, 4128], F32),
     "CF": ("sbuf", [128, 1040], BF), "RR": ("sbuf", [128, 1024], BF), "BW": ("sbuf", [128, 1024], F32),
-    "GF": ("sbuf", [128, 1024], F32), "RC": ("sbuf", [128, 1024], F32), "EW": ("sbuf", [128, 1024], F32),
-    "N": ("sbuf", [128, NF * NW], F32), "SM": ("sbuf", [128, 12 * 64], F32), "SU": ("sbuf", [128, 12 * 64], U16),
+    "GF": ("sbuf", [128, 896], F32), "RC": ("sbuf", [128, 1024], F32), "EW": ("sbuf", [128, 1024], F32),
+    "N": ("sbuf", [128, NF * NW], F32), "SM": ("sbuf", [128, 16 * 64], F32), "SU": ("sbuf", [128, 10 * 64], U16),
     "NBF": ("sbuf", [128, NB * NW], BF), "NIN": ("sbuf", [128, NI * NW], I32), "NUN": ("sbuf", [128, NU * NW], U16),
-    "CM": ("sbuf", [128, 15 * 160], F32), "CB": ("sbuf", [128, 48 * 128], BF), "COL": ("sbuf", [128, 56 * 4], F32),
-    "RP": ("sbuf", [128, 3 * 384], F32),
+    "NHF": ("sbuf", [128, NH * NW], F16),
+    "CM": ("sbuf", [128, 12 * 160], F32), "CB": ("sbuf", [128, 80 * 128], BF), "COL": ("sbuf", [128, 80 * 4], F32),
+    "RP": ("sbuf", [128, 4 * 384], F32),
 }
 for _t in range(4):
     SCRATCH["CT%d" % _t] = ("sbuf", [128, 1024 + 512 + 128 * _t], BF)
     SCRATCH["TI%d" % _t] = ("sbuf", [128, 512 + 128 * _t], BF)
 for _b in range(8):
     SCRATCH["P%d" % _b] = ("psum", [128, 512], F32)
-SEMAPHORES = ["ev", "ea", "et", "eg"] + ["d%d" % i for i in range(100)] + ["r%d" % i for i in range(16)] + ["l%d" % i for i in range(16)]
-HOP = 0.15
+SEMAPHORES = ["ev", "ea", "et", "eg"] + ["d%d" % i for i in range(110)] + ["r%d" % i for i in range(16)] + ["l%d" % i for i in range(16)]
+HOP, CY, FIX, GFIX, GATHER, SCATTER, TCY, DLAT, RLAT, RBW = 0.25, 0.9e-3, 0.02, 0.25, 1.4, 3.0, 0.4e-3, 1.5, 1.3, 120e3
 
 
 def plan(T, core, nxt, topo):
@@ -37,11 +41,16 @@ def plan(T, core, nxt, topo):
         rows = slice(None) if lane is None else slice(lane, 128, 16)
         ap = T[b][rows, lo:hi] if step == 1 else T[b][rows, lo:hi:step]
         w = SCRATCH[b]
+        assert hi <= w[1][1], (b, hi)
         if w[0] == "psum":
             r = (b, 0, 512, None)
         else:
             r = (b, lo, hi, ("L", lane) if lane is not None else tag)
         return {"ap": ap, "r": [r], "n": len(range(lo, hi, step)), "dt": w[2], "ps": w[0] == "psum", "ind": False}
+
+    def back(x):
+        b, lo, hi, _ = x["r"][0]
+        return dict(x, ap=T[b][:, hi - 1:(lo - 1 if lo else None):-1])
 
     def tile(b, w):
         def at(name, lo=0, hi=w, slots=1):
@@ -53,7 +62,7 @@ def plan(T, core, nxt, topo):
             return V(b, d[name] * w + lo, d[name] * w + hi)
         return at
 
-    f, bb, ii, u = tile("N", NW), tile("NBF", NW), tile("NIN", NW), tile("NUN", NW)
+    f, bb, ii, u, hh = tile("N", NW), tile("NBF", NW), tile("NIN", NW), tile("NUN", NW), tile("NHF", NW)
     sm, su, cm, cb, col4 = tile("SM", 64), tile("SU", 64), tile("CM", 160), tile("CB", 128), tile("COL", 4)
     col = lambda name: col4(name, 0, 1)
     cf = lambda name, lo=0, hi=128: cm(name, lo, hi)
@@ -66,12 +75,12 @@ def plan(T, core, nxt, topo):
         rd, wr = [], []
         for x in ins:
             if isinstance(x, dict):
-                (wr if x["ps"] else rd).extend(x["r"])
+                rd.extend(x["r"])
                 rd.extend(x.get("o", []))
         for x in outs:
             wr.extend(x["r"])
             rd.extend(x.get("o", []))
-        ops.append({"alts": alts, "rd": rd, "wr": wr, "kind": kind, "lat": lat, "g": grp[0] + grp[1]})
+        ops.append({"alts": alts, "rd": rd, "wr": wr, "kind": kind, "lat": lat, "g": grp[0] + grp[1], "g0": grp[0]})
         return len(ops) - 1
 
     def ap(x):
@@ -79,15 +88,15 @@ def plan(T, core, nxt, topo):
 
     def vc(o, ins, base=1.0):
         if o["ind"]:
-            base = SCAT
+            base = SCATTER
         elif any(x["ind"] for x in ins):
-            base = 1.6
-        elif all(x["dt"] in (BF, U16) for x in ins + [o]):
+            base = GATHER
+        elif all(x["dt"] in (BF, U16, F16) for x in ins + [o]):
             base = base / 2
-        return 0.06 + max(64, ins[0]["n"] * base) * 1e-3
+        return FIX + max(64, ins[0]["n"] * base) * CY
 
     def ac(o, i):
-        return 0.07 + max(64, i["n"] * (SCAT if o["ind"] else 1.6 if i["ind"] else 1.0)) * 1e-3
+        return FIX + 0.015 + max(64, i["n"] * (SCATTER if o["ind"] else GATHER if i["ind"] else 1.0)) * CY
 
     def cp(o, i):
         add([("v", lambda e: e.tensor_copy(o["ap"], i["ap"]), vc(o, [i]))], [o], [i])
@@ -106,45 +115,62 @@ def plan(T, core, nxt, topo):
     def scan(o, a, b, init, o0, o1):
         add([("v", lambda e: e.tensor_tensor_scan(o["ap"], a["ap"], b["ap"], ap(init), o0, o1), vc(o, [a, b]))], [o], [a, b, init])
 
-    def red(o, a, op):
-        add([("v", lambda e: e.tensor_reduce(o["ap"], a["ap"], AX.X, op), 0.06 + max(64, a["n"]) * 1e-3)], [o], [a])
-
     def ms(o, c):
         add([("v", lambda e: e.memset(o["ap"], c), vc(o, [o]))], [o], [])
 
-    def act(o, i, fn, bias=0.0, scale=1.0):
+    def act(o, i, fn, bias=0.0, scale=1.0, acc=None):
         if o["ind"]:
             fa = lambda e: e.activation(o["ap"], i["ap"], fn)
+        elif acc is not None:
+            fa = lambda e: e.activation(o["ap"], i["ap"], fn, bias=ap(bias), scale=ap(scale), accum_out=acc["ap"])
         else:
             fa = lambda e: e.activation(o["ap"], i["ap"], fn, bias=ap(bias), scale=ap(scale))
-        add([("a", fa, ac(o, i))], [o], [i, bias, scale])
+        add([("a", fa, ac(o, i))], [o] + ([acc] if acc else []), [i, bias, scale])
 
-    def aff(o, i, scale=1.0, bias=0.0):
-        add([("a", lambda e: e.activation(o["ap"], i["ap"], AF.Identity, bias=ap(bias), scale=ap(scale)), ac(o, i)),
-             ("v", tsf(o, i, scale, OP.mult, bias, OP.add), vc(o, [i]))], [o], [i, bias, scale])
+    def aff(o, i, scale=1.0, bias=0.0, more=()):
+        add(list(more) + [("a", lambda e: e.activation(o["ap"], i["ap"], AF.Identity, bias=ap(bias), scale=ap(scale)), ac(o, i)),
+                          ("v", tsf(o, i, scale, OP.mult, bias, OP.add), vc(o, [i]))], [o], [i, bias, scale])
 
-    def mm(groups, first=True, final=True):
+    def relu(o, i, bias):
+        add([("a", lambda e: e.activation(o["ap"], i["ap"], AF.Relu, bias=ap(bias), scale=1.0), ac(o, i)),
+             ("v", tsf(o, i, bias, OP.add, 0.0, OP.max), vc(o, [i]))], [o], [i, bias])
+
+    def mm(groups, first=True, final=True, one=False):
         def fm(e):
-            for o, lst in groups:
+            for x, (o, lst) in enumerate(groups):
                 for k, (l, r) in enumerate(lst):
-                    last = e.matmul(o["ap"], l["ap"], r["ap"], first and k == 0, final and k == len(lst) - 1)
+                    last = e.matmul(o["ap"], l["ap"], r["ap"], first and k == 0 and not (one and x),
+                                    final and k == len(lst) - 1 and not (one and x < len(groups) - 1))
             return last
         c = sum(max(64, r["n"]) * (4 if r["dt"] == F32 else 1) for o, lst in groups for l, r in lst)
-        add([("t", fm, 0.06 + c * 0.6e-3)], [o for o, _ in groups], [x for _, lst in groups for lr in lst for x in lr])
+        add([("t", fm, 0.06 + c * TCY)], [o for o, _ in groups], [x for _, lst in groups for lr in lst for x in lr])
 
     def mm4(group):
         for a in range(0, 16, 4):
             mm([(group[0], group[1][a:a + 4])], a == 0, a == 12)
 
     def dma(q, o, i, nb=0):
-        add([(q, lambda e: e.dma_start(ap(o), ap(i)), 0.1)], [o] if isinstance(o, dict) else [], [i], "d", 1.9 + nb / 150e3)
+        add([(q, lambda e: e.dma_start(ap(o), ap(i)), 0.1)], [o] if isinstance(o, dict) else [], [i], "d", DLAT + nb / 150e3)
+
+    def iotaf(o, pat, base, chm):
+        kw = {} if o["dt"] == I32 else {"allow_small_or_imprecise_dtypes": True}
+        return ("g", lambda e: e.iota(o["ap"], pat, base, chm, **kw), GFIX + 0.13 + 2 * CY * o["n"])
 
     def iota(o, pat, base, chm):
-        kw = {} if o["dt"] == I32 else {"allow_small_or_imprecise_dtypes": True}
-        add([("g", lambda e: e.iota(o["ap"], pat, base, chm, **kw), 0.13 + 2e-3 * o["n"])], [o], [])
+        add([iotaf(o, pat, base, chm)], [o], [])
+
+    def const(o, c):
+        alts = [("v", lambda e: e.memset(o["ap"], float(c)), vc(o, [o])), iotaf(o, [[0, o["n"]]], c, 0)]
+        add(alts[::-1] if grp[0] in OPT["gfill"] else alts, [o], [])
+
+    def aself(o, i, pat, cmp, base, chm):
+        return ("g", lambda e: e.affine_select(o["ap"], i["ap"], pat, cmp, 0.0, base, chm), GFIX + 0.17 + 2 * CY * o["n"])
 
     def asel(o, i, step, cmp, base, chm):
-        add([("g", lambda e: e.affine_select(o["ap"], i["ap"], [[step, 128]], cmp, 0.0, base, chm), 0.43)], [o], [i])
+        add([aself(o, i, [[step, 128]], cmp, base, chm)], [o], [i])
+
+    def pick(o, i, lane):
+        aff(o, i, rm(lane), 0.0, [aself(o, i, [[-16, 8], [0, 16]], OP.is_equal, -lane, 1)])
 
     nsend = [0]
 
@@ -154,7 +180,7 @@ def plan(T, core, nxt, topo):
         rid, pid = topo.addr(nxt, core)
         m = topo.mask(core, nxt)
         fs = lambda e: e.remote_dma(dst["ap"], src["ap"], T.sem["r%d" % k], T.sem["l%d" % k], pid, rid, m)
-        s = add([("g", fs, 1.0)], [], [src], "s", 1.5 + src["n"] * 256 / 80e3)
+        s = add([("g", fs, 0.7)], [], [src], "s", RLAT + src["n"] * 256 / RBW)
         r = add([(None, None, 0.0)], [dst], [], "r")
         for x in (s, r):
             ops[x]["k"] = k
@@ -170,52 +196,45 @@ def plan(T, core, nxt, topo):
             dma("s", ii("calls", 0, 128), T.calls[:])
     iota(ii("runb", 64, 65), [[0, 1]], 0, 1)
     iota(cf("xg"), [[16, 8], [0, 16]], 0, 0)
-    iota(f("ci", 0, 256), [[1, 256]], 0, 0)
+    iota(f("ci", 0, 160), [[1, 160]], 0, 0)
     ts(ii("runb", 68, 69), ii("runb", 64, 65), 15, OP.bitwise_and)
     ts(ii("runb", 72, 73), ii("runb", 64, 65), 112, OP.bitwise_and)
     cp(col("lane"), ii("runb", 68, 69))
     cp(col("g16"), ii("runb", 72, 73))
-    ts(cf("BO"), cf("xg"), col("g16"), OP.is_equal)
+    cp(col("p"), ii("runb", 64, 65))
+    ts(cb("BO"), cf("xg"), col("g16"), OP.is_equal)
+    ts(cb("IW", 0, 132, 2), f("ci", 0, 132), -2.0, OP.add, col("p"), OP.is_equal)
+    ts(cm("IW", 0, 132), f("ci", 0, 132), -2.0, OP.add, col("p"), OP.is_equal)
+    IB, IW = lambda s: cb("IW", s, s + 128), lambda s: cm("IW", s, s + 128)
+    ID = IB(2)
     ts(sm("rm", 0, 16), f("ci", 0, 16), col("lane"), OP.is_equal)
     rm = lambda i: sm("rm", i, i + 1)
     ts(cm("xm"), f("ci", 0, 160), col("g16"), OP.subtract)
     ts(cb("Z", 0, 144, 2), cm("xm", 0, 144), 15.0, OP.is_equal)
     ts(cb("Z0", 0, 144, 2), cb("Z", 0, 144), rm(0), OP.mult)
-    asel(cf("UT"), cf("BO"), 1, OP.is_gt, 0, -1)
-    asel(cb("ID"), cf("BO"), 1, OP.is_equal, 0, -1)
-    asel(cf("LO"), cf("BO"), -1, OP.is_gt, 0, 1)
-    asel(cf("SH"), cf("BO"), -1, OP.is_equal, -1, 1)
-    ms(f("one", 0, 272), 1.0)
+    for nm, cmp in (("UT", OP.is_gt), ("LO", OP.is_lt)):
+        ts(cb("M2"), f("ci", 0, 128), col("p"), cmp)
+        tt(cb(nm), cb("M2"), cb("BO"), OP.mult)
+    ms(f("one", 0, 128), 1.0)
     ms(bb("one", 0, 272), 1.0)
-    ms(f("zero", 0, 257), 0.0)
-    ms(f("kfc", 0, 129), float(KF))
-    aff(cf("I"), cb("ID"))
-    aff(cf("NI"), cb("ID"), -1.0)
-    aff(cb("NI"), cb("ID"), -1.0)
-    ms(col("m129"), -129.0 / 16)
+    ms(f("zero", 0, 258), 0.0)
     ts(sm("pN"), f("ci", 0, 64), 16.0, OP.mult, col("lane"), OP.add)
-    for lo in range(0, 2064, 516):
-        iota(V("X", lo, lo + 516), [[1, 516]], lo, 0)
     for nm in ("UT", "LO"):
-        aff(cb(nm), cf(nm))
-        tt(cb(nm + "i"), cb(nm), cb("ID"), OP.add)
         aff(cb(nm + "b"), cb(nm), -64.0, 64.0)
-    aff(cm("Z3", 0, 144), cb("Z", 0, 144), rm(3))
-    aff(cm("Z4", 0, 144), cb("Z", 0, 144), rm(4))
+
+    def mix(name, *terms):
+        acc = 0.0
+        for k, (lane, c) in enumerate(terms):
+            o = col(name if k == len(terms) - 1 else name + "%d" % (k % 2))
+            aff(o, rm(lane), float(c), acc)
+            acc = o
+        return acc
 
     def fill(b, lane, w, src="zero"):
         dma("s", V(b, 0, w, lane=lane), f(src, 0, w // 16), 30e3)
 
     def conv(out, Zn, src, lo, ncol, band=cb):
         return (out, [(band(Zn, 15 - i, 143 - i), V(src, lo + i, lo + 16 * ncol, 16)) for i in range(16)])
-
-    def link(tri, out, bank, s2=None):
-        mm([(PS(bank, 0, 128), [(cb("hf"), cb(tri)), (cb("ID"), cb(tri + "b"))]),
-            (PS(bank, 128, 129), [(cb(tri + "i"), cb("hf", 0, 1))])])
-        if s2 is None:
-            ts(out, PS(bank, 0, 128), PS(bank, 128, 129), OP.is_equal)
-        else:
-            ts(out, PS(bank, 0, 128), PS(bank, 128, 129), OP.is_equal, s2, OP.mult)
 
     def table(t):
         n = 512 + 128 * t
@@ -229,245 +248,280 @@ def plan(T, core, nxt, topo):
             if j == 3:
                 send(V("TR", 3072, 3072 + n), V("TI%d" % t, 0, n))
             else:
-                act(V("TT", CJ[j], CJ[j] + n), V("TR", j * 1024, j * 1024 + n), AF.Abs)
-        act(V("TT", CJ[3], CJ[3] + n), V("TI%d" % t, 0, n), AF.Abs)
+                act(V("TT", O + CJ[j], O + CJ[j] + n), V("TR", j * 1024, j * 1024 + n), AF.Abs)
+        act(V("TT", O + CJ[3], O + CJ[3] + n), V("TI%d" % t, 0, n), AF.Abs)
 
-    def finish(t, thr):
+    def finish(t):
         K = 128 + 32 * t
-        kf, key = ii("kf", 0, K), ii("key", 0, K)
+        kf, v, fb, nf, hb = ii("kf", 0, K), f("v", 0, K), f("fk", 0, K), bb("nf", 0, K), f("l0", K - 1, K)
         grp[0] = "fin"
-        red(col("nb"), f("v", 0, K), OP.min)
-        ts(cb("hf"), f("zero", 0, 128), col("nb"), OP.add, thr, OP.is_lt)
-        link("UT", cf("LK"), 3)
-        ts(bb("nf", 0, K), kf, KO + KF - 0.5, OP.is_gt)
-        ts(f("fk", 0, K), kf, -float(KO + KF), OP.add, 0.0, OP.min)
-        scan(f("s0", 0, K), bb("nf", 0, K), f("fk", 0, K), 0.0, OP.mult, OP.add)
-        ts(key, kf, KF - 1, OP.bitwise_and)
-        cp(u("key", 0, K), key)
-        mm([(PS(5, 0, 1), [(cf("LK"), f("s0", K - 1, K))])])
-        scan(f("lkn", 0, K), bb("nf", 0, K), f("fk", 0, K), PS(5, 0, 1), OP.mult, OP.add)
-        ts(u("lk", 0, K), f("lkn", 0, K), float(KF), OP.add)
+        ts(u("key", 0, K), kf, float(O - KO), OP.add)
+        scan(f("l0", 0, K), fb, v, 0.0, OP.max, OP.min)
+        mm([(PS(5, 0, 1), [(cf("SX"), hb)]), (PS(5, 1, 2), [(IW(1), hb)])])
+        ts(col("c1"), PS(5, 0, 1), PS(5, 1, 2), OP.max)
+        scan(f("lkn", 0, K), fb, v, col("c1"), OP.max, OP.min)
+        ts(u("lk", 0, K), f("lkn", 0, K), 0.25 + O - KO, OP.add)
         grp[0] = "fin2"
-        aff(f("lkey", 0, K), f("lkn", 0, K), 1.0, float(KF))
+        ts(nf, fb, 16.0, OP.is_lt)
+        aff(cb("hL"), cb("LO"), hb)
+        mm([(PS(1, 0, 128), [(cb("hL"), cb("UT")), (ID, cb("UTb"))])])
+        act(cb("LK"), PS(1, 0, 128), AF.Relu, 1.0, -1.0)
+        act(cf("LK"), PS(1, 0, 128), AF.Relu, 1.0, -1.0)
         ts(ii("ka", 0, K), kf, 2047, OP.bitwise_and)
         cp(u("ck", 0, K), ii("ka", 0, K))
-        aff(col("nf0"), bb("nf", 0, 1))
-        mm([(PS(6, 0, 1), [(cf("SH"), col("nf0"))])])
+        mm([(PS(6, 0, 1), [(IB(3), bb("nf", 0, 1))])])
         aff(bb("nf", K, K + 1), PS(6, 0, 1))
-        ts(su("rev", 0, K // 16), sm("pN", 0, K // 16), -1.0, OP.mult, K - 1.0, OP.add)
-        ts(su("rev", 16, 16 + K // 16), sm("pN", 0, K // 16), -1.0, OP.mult, K + 0.0, OP.add)
-        aff(bb("nlr", 0, K), IND(bb("nf", 0, K + 1), su("rev", 16, 16 + K // 16)))
-        link("LO", cf("LB"), 4, col("nf0"))
+        aff(cb("hU"), cb("UT"), hb)
+        mm([(PS(2, 0, 128), [(cb("hU"), cb("LO")), (ID, cb("LOb"))])])
+        act(cb("LB"), PS(2, 0, 128), AF.Relu, bb("nf", 0, 1), -1.0)
         if t < 3:
-            ts(ii("kb", 0, K), kf, 31744, OP.bitwise_and)
-            cp(bb("kh0", 0, K), ii("kb", 0, K))
+            aff(f("t1", 0, K), nf, float(NFB), JP - 511.5)
+            tt(bb("jp", 0, K), f("t1", 0, K), kf, OP.add)
         else:
-            ts(ii("kb", 0, K), kf, 6144, OP.bitwise_and)
-            ts(ii("vi", 0, K), kf, 1024, OP.bitwise_and)
-            ts(bb("t1", 0, K), ii("kb", 0, K), 0.25, OP.mult, 1024.0, OP.add)
-            ts(bb("t2", 0, K), ii("vi", 0, K), 1.5, OP.mult)
-            tt(bb("kh0", 0, K), bb("t1", 0, K), bb("t2", 0, K), OP.add)
+            ts(bb("t1", 0, K), kf, 0.25, OP.mult, 65536 - 255.875, OP.add)
+            ts(bb("t2", 0, K), ii("ka", 0, K), 1023.5, OP.is_gt, 1536.0, OP.mult)
+            tt(bb("jp", 0, K), bb("t1", 0, K), bb("t2", 0, K), OP.add)
 
     ts(V("CF", 0, 512), V("RR", 0, 512), -1.0, OP.mult, 15.0, OP.add)
     aff(sm("body", 0, 32), sm("pN", 0, 32))
     for n_, j in enumerate((3, 0, 1, 2)):
         ts(V("A", j * 1024, j * 1024 + 1024), V("J", j * 1024, j * 1024 + 1024), 14.5, OP.is_lt, -15.0, OP.mult)
+        if n_ < OPT["hv"]:
+            tt(V("H", j * 1024, j * 1024 + 1024), V("J", j * 1024, j * 1024 + 1024), V("A", j * 1024, j * 1024 + 1024), OP.add)
+            continue
         for h in range(2):
             lo = j * 1024 + 512 * h
             b = 1 + (2 * n_ + h) % 2
-            mm([(PS(b, 0, 512), [(cb("ID"), V("J", lo, lo + 512)), (cb("ID"), V("A", lo, lo + 512))])])
+            mm([(PS(b, 0, 512), [(ID, V("J", lo, lo + 512)), (ID, V("A", lo, lo + 512))])])
             act(V("H", lo, lo + 512), PS(b, 0, 512), AF.Identity)
-    ms(V("TT", 512, 1024), 0.0)
-    ms(V("TT", 1536, 2048), 0.0)
-    ms(V("TT", 2560, 4096), 0.0)
-    ms(V("TT", 4608, 5120), 0.0)
-    fill("WA", 0, 2064, "kfc")
+    for lo, hi in ((-O, 0), (512, 1024), (1536, 2048), (2560, 4096), (4608, 5120)):
+        ms(V("TT", O + lo, O + hi), 0.0)
+    aff(cf("NI"), IW(1), -2.0)
+    tt(cf("SX"), cf("NI"), IW(0), OP.add)
+    ms(f("t1", 0, 129), float(NFB))
+    fill("WA", 0, 2064, "t1")
     cp(sm("runb", 0, 32), ii("runb", 0, 32))
     scan(sm("rs", 0, 32), f("one", 0, 32), sm("runb", 0, 32), 0.0, OP.mult, OP.add)
+    aff(cf("UT"), cb("UT"))
     mm([(PS(5, 0, 1), [(cf("UT"), sm("rs", 31, 32))])])
     tt(sm("rs2", 0, 32), sm("rs", 0, 32), sm("runb", 0, 32), OP.subtract)
     ts(su("st", 0, 32), sm("rs2", 0, 32), PS(5, 0, 1), OP.add, float(O), OP.add)
-    ms(V("RC", 0, 512), 0.0)
+    const(V("RC", 0, 512), 0)
     act(IND(V("WA", 0, 2064), su("st", 0, 32)), V("RC", 0, 512), AF.Silu)
-    dma("s", f("v", 0, 128), V("WA", O, O + 2048, lane=0))
+    dma("s", f("ep", 0, 128), V("WA", O, O + 2048, lane=0))
+    aff(f("fk", 0, 128), f("ep", 0, 128), -1.0, float(NFB))
     ts(ii("ka", 0, 128), ii("calls", 0, 128), 9, OP.logical_shift_right)
-    ts(f("t1", 0, 128), ii("ka", 0, 128), 1536.0, OP.mult, float(KO), OP.add)
-    ts(f("t2", 0, 128), ii("calls", 0, 128), 1535.5, OP.is_gt, -5120.0, OP.mult)
-    tt(f("t3", 0, 128), f("t1", 0, 128), ii("calls", 0, 128), OP.add)
-    tt(f("t1", 0, 128), f("t3", 0, 128), f("t2", 0, 128), OP.add)
-    tt(ii("kf", 0, 128), f("t1", 0, 128), f("v", 0, 128), OP.add)
+    ts(f("t2", 0, 128), ii("ka", 0, 128), 1536.0, OP.mult, float(KO), OP.add)
+    ts(f("t3", 0, 128), ii("calls", 0, 128), 1535.5, OP.is_gt, -5120.0, OP.mult)
+    tt(f("rk", 0, 128), f("t2", 0, 128), ii("calls", 0, 128), OP.add)
+    tt(ii("kf", 0, 128), f("rk", 0, 128), f("t3", 0, 128), OP.add)
+    tt(f("v", 0, 128), f("ep", 0, 128), ii("kf", 0, 128), OP.add)
     table(0)
-    finish(0, 1.0)
+    finish(0)
     grp[0] = "init1"
-    ms(V("EW", 0, 1024), 0.0)
+    iota(V("S", 0, 516), [[1, 516]], 0, 0)
+    ts(sm("xo", 0, 8), f("ci", 0, 8), 516.0, OP.mult, rm(2), OP.mult)
+    for k in range(4):
+        aff(V("X", 516 * k, 516 * k + 516), V("S", 0, 516), rm(2), sm("xo", k, k + 1))
+    aff(cm("Z34", 0, 144), cb("Z", 0, 144), mix("m34", (3, 1), (4, 1)))
+    for h in range(2):
+        const(V("EW", 512 * h, 512 * h + 512), 0)
     cp(sm("rs", 0, 32), su("st", 0, 32))
     tt(sm("rs2", 0, 32), sm("rs", 0, 32), sm("runb", 0, 32), OP.add)
     dma("s", V("EW", 0, 512, lane=3), sm("rs2", 0, 32))
     dma("s", V("EW", 512, 1024, lane=3), sm("rs", 0, 32))
-    mm4(conv(PS(7, 0, 64), "Z3", "EW", 0, 64, cm))
+    mm4(conv(PS(7, 0, 64), "Z34", "EW", 0, 64, cm))
     ts(su("end", 0, 32), PS(7, 0, 32), -1.0, OP.add)
     cp(su("stw", 0, 32), PS(7, 32, 64))
-    aff(f("ec", 0, 128), f("t1", 0, 128), 1.0, -float(KO))
+    ts(f("ec", 0, 128), ii("kf", 0, 128), float(O - KO), OP.add)
     dma("s", V("X", O, O + 2048, lane=4), f("ec", 0, 128))
-    aff(V("EW", 0, 512), IND(V("X", 0, 2064), su("stw", 0, 32)))
-    mm4(conv(PS(7, 0, 32), "Z4", "EW", 0, 32, cm))
+    aff(V("EW", 0, 512), IND(V("X", 0, 2064), su("stw", 0, 32)), rm(4))
+    mm4(conv(PS(7, 0, 32), "Z34", "EW", 0, 32, cm))
     cp(su("LK", 0, 32), PS(7, 0, 32))
     grp[0] = "init2"
-    for lo in range(2064, 3600, 512):
-        iota(V("X", lo, lo + 512), [[1, 512]], lo, 0)
-    for ln in range(5, 12):
-        fill("X", ln, 3600)
-    aff(col("m56"), rm(5), 1.0, rm(6))
-    aff(col("w56"), rm(5), 16.0, rm(6))
-    aff(col("m12"), rm(1), 1.0, rm(2))
-    aff(col("o12"), col("m12"), 32.0)
-    aff(col("o56"), col("m56"), 32.0, col("o12"))
-    aff(col("hi"), rm(5), 1.0, rm(10))
-    aff(col("lo"), rm(6), 1.0, rm(11))
-    aff(col("wab"), rm(10), 16.0, rm(11))
-    aff(col("wa7"), rm(7), 1.0, col("wab"))
-    aff(col("w0c"), rm(0), 1.0, rm(12))
-    aff(col("w08"), rm(0), 1.0, rm(8))
-    aff(col("w089"), rm(9), 1.0, col("w08"))
-    aff(col("pc1"), rm(10), 63.0)
-    aff(col("pc2"), rm(11), 15.0, col("pc1"))
-    aff(col("padc"), rm(12), float(KO), col("pc2"))
-    for h in range(2):
-        iota(V("GF", 512 * h, 512 * h + 512), [[1, 32], [0, 16]], 32 * h, 0)
-    iota(V("RC", 512, 1024), [[0, 32], [1, 16]], 0, 0)
-    aff(V("BW", 0, 512), V("GF", 0, 512), col("hi"), col("o56"))
-    aff(V("BW", 512, 1024), V("GF", 512, 1024), rm(10), col("o12"))
-    aff(V("GF", 0, 512), V("RC", 512, 1024), col("lo"))
-    aff(V("GF", 512, 1024), V("RC", 512, 1024), rm(11))
-    for h in range(2):
-        tt(V("BW", 512 * h, 512 * h + 512), V("BW", 512 * h, 512 * h + 512), V("GF", 512 * h, 512 * h + 512), OP.add)
-    aff(cf("R1"), cf("BO"), rm(1))
-    aff(cf("R2"), cf("BO"), rm(2))
-    aff(cf("R5"), cf("BO"), col("w56"))
-    aff(cb("MC"), cb("Z", 14, 142), col("w0c"))
-    aff(cb("M2"), cb("Z", 15, 143), col("wab"))
-    tt(cb("MC"), cb("MC"), cb("M2"), OP.add)
-    aff(cb("M1"), cb("Z", 14, 142), col("w089"))
-    aff(cb("M2"), cb("Z", 15, 143), col("w56"))
-    tt(cb("M1"), cb("M1"), cb("M2"), OP.add)
-    aff(cb("M2"), cb("Z", 13, 141), col("wa7"))
-    tt(cb("M1"), cb("M1"), cb("M2"), OP.add)
-    ms(f("nod", 0, 257), 40000.0)
-    ms(f("W", 0, 4), 0.0)
-    iota(V("RP", 384, 768), [[0, 24], [1, 16]], 0, 0)
-    ts(V("RP", 0, 384), V("RP", 384, 768), col("lane"), OP.is_equal)
-    ts(V("RP", 384, 768), V("RP", 384, 768), 0.5, OP.is_gt)
+    for k in range(4, 7):
+        aff(V("X", 516 * k, 516 * k + 516), V("X", 0, 516), rm(2), sm("xo", k, k + 1))
+    aff(cf("NI"), ID, -1.0)
+    aff(cb("NI"), ID, -1.0)
+    aff(cb("I5"), ID, 4096.0)
+    aff(cb("NI5"), ID, -4096.0)
+    ms(bb("m129", 0, 1), -129.0 / 16)
+    iota(V("NQ", 2048, 3072), [[1, 64], [0, 16]], 0, 0)
+    iota(V("NQ", 3072, 3584), [[0, 32], [1, 16]], 0, 0)
+    mix("o12", (2, 32), (12, 1))
+    aff(col("o56"), mix("m56", (5, 1), (6, 1)), 32.0, col("o12"))
+    for h, (hi, lo, c) in enumerate(((mix("hi", (5, 1), (10, 1)), mix("lo", (6, 1), (11, 1)), col("o56")), (rm(10), rm(11), col("o12")))):
+        aff(cb("M1"), ID, hi)
+        aff(cb("M2"), ID, lo)
+        mm([(PS(3 + h, 0, 512), [(cb("M1"), V("NQ", 2048 + 512 * h, 2560 + 512 * h)), (cb("M2"), V("NQ", 3072, 3584))])])
+        aff(V("BW", 512 * h, 512 * h + 512), PS(3 + h, 0, 512), 1.0, c)
+    aff(col("sg"), mix("s7", (0, 1), (7, 1), (8, 1), (9, 1)), -2.0, 1.0)
+    mix("padc", (10, 63), (11, 15), (12, 1), (13, 1), (5, -31), (6, 15), (7, 1024))
+    for t in range(4):
+        grp[0] = "ctp%d" % t
+        const(V("CT%d" % t, 512 + 128 * t, 1008), 0)
+        aff(V("CT%d" % t, 1008, 1024), f("one", 0, 16), col("padc"))
+    grp[0] = "init2"
+    aff(cb("Zw", 0, 144, 2), cb("Z", 0, 144), mix("cw1", (12, 2), (13, -1)))
+    aff(cb("Zp", 0, 144, 2), cb("Z", 0, 144), mix("cp1", (0, -1), (12, 128), (13, 2048)))
+    aff(sm("pN1"), sm("pN"), 1.0, 128.0)
+    aff(cf("R1"), cb("BO"), rm(1))
+    aff(cf("R2"), cb("BO"), rm(2))
+    aff(cf("R5"), cb("BO"), mix("w56", (5, 16), (6, 1)))
+    aff(col("rcf"), rm(1), KO - 32.0, 32.0)
+    ts(V("RP", 0, 384), V("NQ", 3072, 3456), col("lane"), OP.is_equal)
+    ts(V("RP", 384, 768), V("NQ", 3072, 3456), 0.5, OP.is_gt)
+
+    def lanes(name, terms):
+        for k, (lane, w) in enumerate(terms):
+            aff(cb("M2") if k else cb(name), cb("Z", 15 - lane, 143 - lane), w)
+            if k:
+                tt(cb(name), cb(name), cb("M2"), OP.add)
+
+    wab = mix("wab", (10, 16), (11, 1))
+    lanes("MC", [(0, wab), (2, wab), (1, mix("w0c", (0, -1), (13, 2 * NFB)))])
+    aff(col("ssc"), rm(2), -3.0, 1.0)
+    aff(col("b0"), rm(2), 40000 + 3 * JP, -JP)
+    aff(cb("Z2", 0, 144, 2), cb("Z", 0, 144), 2.0)
+    ms(bb("m17", 0, 224), -17.0 / 16)
+    ms(f("pad", 0, 258), float(NFB + PAD))
+    ts(hh("W", 0, 8), f("zero", 0, 8), 0.0, OP.add)
+    grp[0] = "initC"
     for i in range(16):
-        aff(cb("C%d" % i), cf("BO"), rm(i))
-    for i in range(16):
-        aff(cb("A%d" % i), cb("Z", 15, 143), rm(i))
+        aff(cb("C%d" % i), cb("BO"), rm(i))
+    grp[0] = "initA"
     ms(V("V", 0, O), 0.0)
     ms(V("CF", 1024, 1040), 0.0)
-    ms(col("len"), 2048.0 - 2048 - 2560 - 3072 - 3584)
     ms(col("gs"), 0.0)
-    aff(col("b0"), rm(0), -544.0)
-    aff(col("b2"), rm(2), 1024.0, col("b0"))
+    aff(col("pad1"), rm(1), 2.0 * NFB, float(PAD))
+    aff(col("padS"), rm(2), 40000.0 - 3 * PAD, col("pad1"))
+    aff(col("n15"), rm(15), -1.0, 1.0)
+    aff(col("sp0"), col("lane"), col("n15"), float(O))
+    grp[0] = "init3"
+    for i in range(16):
+        pick(cb("A%d" % i), cb("Z", 15, 143), i)
+        pick(cb("E%d" % i), cb("Z", 12, 140), i)
+    aff(col("wa7"), rm(7), -1.0, wab)
+    lanes("M1", [(0, col("w56")), (4, col("wa7")), (5, mix("w089", (0, -1), (8, -1), (9, -1), (13, -KO)))])
+    mix("b3", (0, 1024 - 544 - 67584), (3, 1024 - 33), (4, 1024), (5, 2048))
+    aff(col("padL"), rm(5), -1023.0, 1023.0)
+    aff(sm("pc"), sm("pN"), 1.0, 3600.0 - 512)
 
     for t in range(4):
         K = 128 + 32 * t
         L, n, K2, q = 16 * K, 512 + 128 * t, K + 32, K // 4
         L2, last, nc = 16 * K2, t == 3, n // 16
+        WW = L2 + O + 16
         N = lambda name: f(name, 0, K)
         B = lambda name: bb(name, 0, K)
+        Hf = lambda name: hh(name, 0, K)
+        nl1 = bb("nf", 1, K + 1)
         CT = "CT%d" % t
-        Tw = V("TT", 0, 4096 + n)
+        Tw = V("TT", 0, 5120 + O)
         Xw, Vw = V("X", 0, L + O), V("V", 0, L + O)
-        rev = su("rev", 0, K // 16)
-        grp[0], grp[1] = "prep", "3" if last else ""
-        for lo in range(n, 1024, 256):
-            aff(V(CT, lo, min(lo + 256, 1024)), f("one", 0, min(256, 1024 - lo)), col("padc"))
-        aff(V("RC", 0, 128), f("one", 0, 128), 32.0)
+        grp[0], grp[1] = "prep", ".%d" % t
+        aff(V("RC", 0, 128), f("one", 0, 128), col("rcf"))
+        aff(col("spare"), col("n15"), L2 + 1.0, col("sp0"))
+        aff(V("S", L, L + 16), f("one", 0, 16), col("padL" if last else "padS"))
         if last:
-            for ln in range(3):
-                fill("WA", ln, L2 + O)
-            aff(col("bias"), rm(1), n + 128.0 + 1024, col("b2"))
+            grp[0] = "ye"
+            fill("WA", 2, WW)
+            aff(V("EW", 0, 640), V("X", 0, 640), 1.0, 33.0)
+            for s in range(1, 3):
+                lo = 512 + 128 * s
+                aff(col("ce%d" % s), col("cum%d" % (s - 1)), 1.0, 33.0 - lo)
+                aff(V("EW", lo, lo + 128), V("X", lo, lo + 128), 1.0, col("ce%d" % s))
+            act(IND(V("WA", 0, WW), su("eo", 0, nc)), V("EW", 0, n), AF.Silu)
+            dma("s", N("ec"), V("WA", O, O + L, lane=2))
+            aff(col("c3"), col("cum2"), 1.0, 128.0 + 33)
+            grp[0] = "prep"
+            for ln in (0, 3, 4, 5):
+                fill("WA", ln, WW)
         else:
-            fill("WA", 0, L2 + O, "nod")
-            fill("WA", 1, L2 + O, "nod")
-            aff(col("bias"), rm(1), KO + KF + n + 128.0)
-            aff(col("lk2"), col("lane"), -float(K2))
+            fill("WA", 0, WW, "pad")
+            fill("WA", 1, WW, "pad")
+            fill("WA", 2, WW)
+            aff(col("bias"), rm(1), n + 128.0, col("b0"))
         grp[0] = "arg"
-        for c in range(4):
-            act(V("A", 16 * q * c, 16 * q * (c + 1)), IND(Tw, u("key", q * c, q * c + q)), AF.Identity)
-            tt(V("NQ", 16 * q * c, 16 * q * (c + 1)), IND(Tw, u("lk", q * c, q * c + q)), V("A", 16 * q * c, 16 * q * (c + 1)), OP.not_equal)
-            if c == 2:
-                mm([conv(PS(0, 0, 3 * q), "Z", "NQ", 0, 3 * q)])
-        mm([conv(PS(0, 3 * q, K), "Z", "NQ", 48 * q, q)])
+        cut = [K * x // 16 // 2 * 2 for x in OPT["cut"]]
+        for c, (lo, hi) in enumerate(zip(cut, cut[1:])):
+            act(V("A", 16 * lo, 16 * hi), IND(Tw, u("key", lo, hi)), AF.Identity)
+            tt(V("NQ", 16 * lo, 16 * hi), IND(Tw, u("lk", lo, hi)), V("A", 16 * lo, 16 * hi), OP.not_equal)
+            if c >= len(cut) - 3:
+                a = 0 if c == len(cut) - 3 else lo
+                o_, lst = conv(PS(0, a, hi), "Z2", "NQ", 16 * a, hi - a)
+                mm([(o_, [(cb("BO"), bb("m17", a, hi))] + lst)])
         grp[0] = "n1"
-        ts(B("dis"), PS(0, 0, K), 8.5, OP.is_gt)
-        scan(N("s0"), B("nf"), B("dis"), 0.0, OP.mult, OP.add)
-        mm([(PS(5, 0, 1), [(cf("LK"), f("s0", K - 1, K))])])
-        scan(bb("s1", 8, K + 8), B("nf"), B("dis"), PS(5, 0, 1), OP.mult, OP.add)
-        cp(bb("s1", 7, 8), PS(5, 0, 1))
-        tt(B("fd"), B("dis"), bb("s1", 7, K + 7), OP.is_gt)
-        scan(N("cum"), B("one"), B("fd"), 0.0, OP.mult, OP.add)
-        mm([(PS(5, 0, 1), [(cf("UT"), f("cum", K - 1, K)), (cf("BO"), col("m129"))]), (PS(5, 1, 2), [(cf("BO"), f("cum", K - 1, K))])])
-        tt(N("fk"), B("fd"), ii("key", 0, K), OP.mult)
-        scan(N("s0"), B("nf"), N("fk"), 0.0, OP.mult, OP.add)
+        s1, s1b = bb("s1", 8, K + 8), bb("s1", 7, K + 7)
+        scan(B("s0"), B("nf"), PS(0, 0, K), 0.0, OP.mult, OP.max)
+        ts(B("dis"), PS(0, 0, K), 0.0, OP.is_gt)
+        mm([(PS(b, 0, 1), [(cb("LK"), bb("s0", K - 1, K))]) for b in (5, 6)])
+        scan(s1, B("nf"), B("dis"), PS(5, 0, 1), OP.mult, OP.max)
+        aff(bb("s1", 7, 8), PS(6, 0, 1))
+        tt(B("fd"), B("dis"), s1b, OP.is_gt)
+        scan(B("cum"), B("one"), B("fd"), 0.0, OP.mult, OP.add)
+        mm([(PS(5, 0, 1), [(cb("UT"), bb("cum", K - 1, K)), (cb("BO"), bb("m129", 0, 1))]), (PS(6, 0, 1), [(cb("BO"), bb("cum", K - 1, K))])])
+        act(col("gap%d" % t), PS(6, 0, 1), AF.Relu, 128.0, -1.0)
+        tt(N("t2"), B("fd"), ii("kf", 0, K), OP.mult)
+        scan(N("s0"), B("nf"), N("t2"), 0.0, OP.mult, OP.add)
         mm([(PS(6, 0, 1), [(cf("LK"), f("s0", K - 1, K))])])
-        act(B("has"), bb("s1", 8, K + 8), AF.Sign)
-        ts(B("rn"), N("cum"), PS(5, 0, 1), OP.add, 0.0, OP.min)
-        ts(B("ok"), N("cum"), PS(5, 0, 1), OP.add, -0.5, OP.is_lt)
-        ts(col("cnt"), PS(5, 1, 2), 128.0, OP.min)
-        tt(N("r1"), B("rn"), B("has"), OP.mult)
-        dma("s", V("X", O, O + L, lane=0), N("r1"))
-        if not last:
-            act(N("nd"), N("r1"), AF.Relu, float(KO), float(KO))
-            dma("a", V("X", O, O + L, lane=12), N("nd"))
-        scan(N("fkg"), B("nf"), N("fk"), PS(6, 0, 1), OP.mult, OP.add)
+        act(B("s0"), s1, AF.Relu, 1000.0, -1000.0)
+        tt(B("rn"), B("cum"), B("s0"), OP.add)
+        ts(N("rn"), B("rn"), PS(5, 0, 1), OP.add, 0.0, OP.min)
+        dma("s", V("X", O, O + L, lane=0), N("rn"))
+        dma("a", V("X", O, O + L, lane=13), N("rn"))
+        scan(N("fkg"), B("nf"), N("t2"), PS(6, 0, 1), OP.mult, OP.add)
         dma("s", V("X", O, O + L, lane=1), N("fkg"))
+        ts(B("ok"), B("cum"), PS(5, 0, 1), OP.add, -0.5, OP.is_lt)
         tt(B("mv"), B("ok"), B("dis"), OP.mult)
         grp[0] = "nl"
-        mm([(PS(3, 0, K), [(cf("I"), N("fkg")), (cf("NI"), N("lkey"))])])
+        mm([(PS(3, 0, K), [(IW(2), N("fkg")), (cf("NI"), N("lkn"))])])
         tt(N("t1"), PS(3, 0, K), B("mv"), OP.mult)
-        mm([(PS(4, 0, K), [(cf("I"), N("t1")), (cf("I"), N("lkey"))])])
-        cp(u("nl", 0, K), PS(4, 0, K))
+        mm([(PS(4, 0, K), [(IW(2), N("t1")), (IW(2), N("lkn"))])])
+        ts(u("nl", 0, K), PS(4, 0, K), 0.25 + O - KO, OP.add)
         grp[0] = "m"
-        aff(col("mv0"), bb("mv", 0, 1))
-        mm([(PS(6, 0, 1), [(cf("SH"), col("mv0"))])])
-        aff(B("wi"), B("mv"), 511.0 / 512, 1.0 / 512)
-        aff(bb("wi", K, K + 1), PS(6, 0, 1), 511.0 / 512, 1.0 / 512)
-        aff(B("t1"), B("mv"), -511.0, 512.0)
-        tt(B("t2"), B("t1"), B("nf"), OP.mult)
-        tt(B("m"), B("t2"), bb("wi", 1, K + 1), OP.mult)
+        mm([(PS(6, 0, 1), [(IB(3), bb("mv", 0, 1))])])
+        aff(B("wi"), B("mv"), 4095.0 / 4096, 1.0 / 4096)
+        aff(bb("wi", K, K + 1), PS(6, 0, 1), 4095.0 / 4096, 1.0 / 4096)
+        mm([(PS(1, 0, K), [(cb("I5"), B("nf")), (cb("NI5"), B("mv")), (ID, B("mv"))])])
+        tt(B("m"), PS(1, 0, K), bb("wi", 1, K + 1), OP.mult)
         aff(B("st"), B("mv"), -1.0, 1.0)
-        aff(B("str"), IND(B("mv"), rev), -1.0, 1.0)
+        aff(B("stB"), B("mv"), -4096.0, 4096.0)
         if not last:
-            aff(B("t3"), B("fd"), -float(KF))
-            tt(B("t4"), B("t3"), B("ok"), OP.mult)
-            tt(B("kh0"), B("t4"), B("kh0"), OP.add)
-        grp[0] = "ct"
-        if OPT["ct"]:
-            tt(V(CT, 0, n), IND(Xw, su("end", 0, nc)), V("BW", 0, n), OP.add)
+            aff(B("t2"), B("mv"), float(NFB))
+            tt(B("t1"), B("fd"), B("t2"), OP.mult)
+            tt(B("jp"), B("jp"), B("t1"), OP.subtract)
         else:
-            for lo, hi in ((0, nc // 2), (nc // 2, nc)):
-                tt(V("GF", 16 * lo, 16 * hi), IND(Xw, su("end", lo, hi)), V("BW", 16 * lo, 16 * hi), OP.add)
-                act(V(CT, 16 * lo, 16 * hi), V("GF", 16 * lo, 16 * hi), AF.Identity)
+            grp[0] = "ye"
+            scan(back(Hf("r1")), back(nl1), back(N("ec")), 0.0, OP.mult, OP.add)
+            mm([(PS(7, 0, 1), [(cb("LB"), hh("r1", 0, 1))])])
+            scan(back(Hf("ce")), back(nl1), back(N("ec")), PS(7, 0, 1), OP.mult, OP.add)
+            aff(N("t3"), N("rn"), 1.0, col("c3"))
+            tt(Hf("r1"), N("t3"), B("stB"), OP.subtract)
+            tt(Hf("ce"), Hf("r1"), Hf("ce"), OP.max)
+        grp[0] = "ct"
+        for lo, hi in ((0, nc // 2), (nc // 2, nc)):
+            tt(V("GF", 16 * lo, 16 * hi), IND(Xw, su("end", lo, hi)), V("BW", 16 * lo, 16 * hi), OP.add)
+            act(V(CT, 16 * lo, 16 * hi), V("GF", 16 * lo, 16 * hi), AF.Relu, rm(13), col("sg"))
         send(V(CT, 0, n), V(CT, 1024, 1024 + n))
+        if last:
+            for ln in (0, 3, 4, 5):
+                fill("X", ln, WW)
         grp[0] = "cl"
-        if OPT["ct"]:
-            tt(V("GF", 0, n), IND(Xw, su("end", 0, nc)), V("BW", 0, n), OP.add)
-        mm([conv(PS(7, 0, nc), "Z0", CT, 0, nc)])
-        ts(sm("pa", 0, nc), PS(7, 0, nc), -0.5, OP.is_gt)
-        tt(sm("pb", 0, nc), sm("pa", 0, nc), sm("pN", 0, nc), OP.mult)
-        tt(sm("pa", 0, nc), sm("pb", 0, nc), PS(7, 0, nc), OP.add)
-        ts(su("po", 0, nc), sm("pa", 0, nc), 128.0, OP.add)
+        mm([conv(PS(7, 0, nc), "Zp", CT, 0, nc)])
+        tt(sm("pa", 0, nc), PS(7, 0, nc), sm("pN1", 0, nc), OP.min)
+        cp(su("po", 0, nc), sm("pa", 0, nc))
         act(IND(V("RC", 0, 128 + n), su("po", 0, nc)), V("GF", 0, n), AF.Silu)
         grp[0] = "rep"
-        mm([(PS(7, 128 * a, 128 * a + 128), [(cf(nm), V("RC", 0, 128))]) for a, nm in enumerate(("R1", "R2", "R5"))])
-        tt(V("RP", 768, 1152), PS(7, 0, 384), V("RP", 0, 384), OP.mult)
-        scan(V("GF", 0, 384), V("RP", 384, 768), V("RP", 768, 1152), 0.0, OP.mult, OP.add)
-        ts(su("LK", nc, nc + 8), V("GF", 15, 128, 16), -31.75, OP.add)
-        ts(su("E", 0, 8), V("GF", 143, 256, 16), -31.75, OP.add)
+        rw = 256 if last else 384
+        mm([(PS(7, 128 * a, 128 * a + 128), [(cf(nm), V("RC", 0, 128))]) for a, nm in enumerate(("R1", "R2", "R5")[:rw // 128])])
+        tt(V("RP", 768, 768 + rw), PS(7, 0, rw), V("RP", 0, rw), OP.mult)
+        scan(V("RP", 1152, 1152 + rw), V("RP", 384, 384 + rw), V("RP", 768, 768 + rw), 0.0, OP.mult, OP.add)
+        ts(su("LK", nc, nc + 8), V("RP", 1152 + 15, 1152 + 128, 16), 0.25 + O - KO, OP.add)
+        ts(su("E", 0, 8), V("RP", 1152 + 143, 1152 + 256, 16), -31.75, OP.add)
         grp[0] = "cl2"
-        aff(col("gap%d" % t), col("cnt"), -1.0, 128.0)
         if not last:
-            aff(sm("body", nc, nc + 8), V("GF", 271, 384, 16), 1.0, -544.0)
+            aff(sm("body", nc, nc + 8), V("RP", 1152 + 271, 1152 + 384, 16), 1.0, -544.0)
             aff(col("g7"), col("gs"), rm(7))
             aff(cf("xg"), V("RC", 0, 128), col("m56"), col("g7"))
             tt(V("BW", n, n + 128), V("BW", n, n + 128), cf("xg"), OP.add)
@@ -480,12 +534,15 @@ def plan(T, core, nxt, topo):
         aff(col("cum%d" % t), col("gs"), 1.0, n + 128.0)
         grp[0] = "nq2"
         for c, lo in enumerate(range(0, L, 512)):
-            if c < OPT["nq"]:
+            if c >= OPT["nq"][t]:
                 tt(V("NQ", lo, lo + 512), IND(Tw, u("nl", 32 * c, 32 * c + 32)), V("A", lo, lo + 512), OP.not_equal)
             else:
                 act(V("TR", lo, lo + 512), IND(Tw, u("nl", 32 * c, 32 * c + 32)), AF.Identity)
-                mm([(PS(3 + c % 2, 0, 512), [(cb("ID"), V("A", lo, lo + 512)), (cb("NI"), V("TR", lo, lo + 512))])])
-                ts(V("NQ", lo, lo + 512), PS(3 + c % 2, 0, 512), 0.0, OP.not_equal)
+                mm([(PS(3 + c % 2, 0, 512), [(ID, V("A", lo, lo + 512)), (cb("NI"), V("TR", lo, lo + 512))])])
+                if last:
+                    ts(V("NQ", lo, lo + 512), PS(3 + c % 2, 0, 512), 0.0, OP.not_equal)
+                else:
+                    act(V("NQ", lo, lo + 512), PS(3 + c % 2, 0, 512), AF.Abs)
         grp[0] = "scan"
         for i in range(0, 16, 2):
             b = 1 + (i // 2) % 2
@@ -498,90 +555,102 @@ def plan(T, core, nxt, topo):
         add([("a", lambda e, o=o_, i=i_: e.activation(o["ap"], i["ap"], AF.Relu, bias=230.0, scale=-256.0), ac(o_, i_)),
              ("v", tsf(o_, i_, 0.9, OP.is_lt, 16.0, OP.mult), vc(o_, [i_]))], [o_], [i_])
         tt(V("CF", 0, n), IND(Tw, su("LK", 0, nc)), V("RR", 0, n), OP.min)
-        cp(ii("vi", 0, 128), IND(Vw, su("E", 0, 8)))
-        tt(bb("eq", 0, 128), IND(Vw, su("E", 0, 8)), ii("vi", 0, 128), OP.is_equal)
+        cp(ii("ka", 0, 128), IND(Vw, su("E", 0, 8)))
+        tt(bb("eq", 0, 128), IND(Vw, su("E", 0, 8)), ii("ka", 0, 128), OP.is_equal)
         tt(V("CF", n, n + 128), IND(Tw, su("LK", nc, nc + 8)), bb("eq", 0, 128), OP.mult)
         if not last:
             table(t + 1)
         Cw = V(CT, 0, 1024 + n)
-        for c in range(4):
-            grp[0] = "j%d" % c
-            aff(V("J", 16 * q * c, 16 * q * (c + 1)), IND(Cw, u("ck", q * c, q * c + q)))
-            if c % 2:
-                mm([conv(PS(0, q * (c - 1), q * (c + 1)), "Z0", "J", 16 * q * (c - 1), 2 * q)])
+        for c in range(K // 32):
+            grp[0] = "j%d" % (c % 2)
+            aff(V("J", 512 * c, 512 * c + 512), IND(Cw, u("ck", 32 * c, 32 * c + 32)))
+        grp[0] = "jw"
+        mm([conv(PS(0, 0, K - 64), "Zw", "J", 0, K - 64)])
+        mm([conv(PS(0, K - 64, K), "Zw", "J", 16 * (K - 64), 64)])
         grp[0] = "n2"
-        ts(B("w"), PS(0, 0, K), -0.5, OP.is_lt, 1.0, OP.add)
-        tt(B("wsr"), IND(B("w"), rev), B("str"), OP.mult)
-        tt(B("wm"), B("w"), B("mv"), OP.mult)
-        Wi = f("W", 4, K + 4)
-        scan(Wi, B("one"), B("w"), 0.0, OP.mult, OP.add)
-        scan(N("s0"), B("nlr"), B("wsr"), 0.0, OP.mult, OP.add)
-        scan(N("cum"), B("nf"), B("wm"), 0.0, OP.mult, OP.add)
-        mm([(PS(5, 0, 1), [(cf("LB"), f("s0", K - 1, K))])])
-        mm([(PS(6, 0, 1), [(cf("LK"), f("cum", K - 1, K))]), (PS(6, 1, 2), [(cf("UT"), f("W", K + 3, K + 4))]),
-            (PS(6, 2, 3), [(cf("BO"), f("W", K + 3, K + 4))])])
-        scan(N("rs1"), B("nlr"), B("wsr"), PS(5, 0, 1), OP.mult, OP.add)
-        scan(N("sm1"), B("nf"), B("wm"), PS(6, 0, 1), OP.mult, OP.add)
-        tt(N("t1"), IND(N("rs1"), rev), B("mv"), OP.mult)
-        tt(N("t2"), N("sm1"), B("st"), OP.mult)
-        tt(N("t3"), f("W", 3, K + 3), N("t2"), OP.subtract)
-        tt(N("t2"), N("t3"), N("t1"), OP.add)
-        ts(u("pos", 0, K), N("t2"), PS(6, 1, 2), OP.add, float(O), OP.add)
-        grp[0] = "end"
-        aff(col("cw"), PS(6, 1, 2), 1.0, O - 1.0)
-        if not last:
-            aff(col("thr"), PS(6, 2, 3), 1.0, col("lk2"))
-            ts(f("real", 0, K2), f("ci", 0, K2), col("thr"), OP.is_lt, 65536.0, OP.mult)
-            aff(f("cap", 0, K2), f("real", 0, K2), 1.0, float(PAD))
-        aff(col("len"), PS(6, 2, 3), 1.0, col("len"))
-        aff(N("ec"), Wi, 1.0, col("cw"))
-        if OPT["ep"]:
-            mm([(PS(5, 0, K), [(cf("I"), Wi), (cf("NI"), N("sm1"))])])
-            aff(N("ep"), PS(5, 0, K), 1.0, col("cw"))
+        Wi = hh("W", 8, K + 8)
+        tt(B("ws"), PS(0, 0, K), B("st"), OP.mult)
+        tt(B("wm"), PS(0, 0, K), B("mv"), OP.mult)
+        scan(back(Hf("r1")), back(nl1), back(B("ws")), 0.0, OP.mult, OP.add)
+        scan(Hf("m1"), B("nf"), B("wm"), 0.0, OP.mult, OP.subtract)
+        scan(Wi, B("ws"), B("wm"), 0.0, OP.add, OP.add)
+        mm([(PS(5, 0, 1), [(cb("LB"), hh("r1", 0, 1))])])
+        mm([(PS(6, 0, 1), [(cb("LK"), hh("m1", K - 1, K))]), (PS(6, 1, 2), [(cb("UT"), hh("W", K + 7, K + 8))]),
+            (PS(6, 2, 3), [(cb("BO"), hh("W", K + 7, K + 8))])])
+        scan(back(Hf("r2")), back(nl1), back(B("ws")), PS(5, 0, 1), OP.mult, OP.add)
+        scan(Hf("m2"), B("nf"), B("wm"), PS(6, 0, 1), OP.mult, OP.subtract)
+        if OPT["n2"]:
+            tt(Hf("wa"), hh("W", 7, K + 7), B("stB"), OP.subtract)
+            tt(Hf("r1"), Hf("r2"), Hf("wa"), OP.add)
+            tt(Hf("m1"), Hf("m2"), hh("W", 7, K + 7), OP.add)
+            tt(Hf("r2"), Hf("r1"), Hf("m1"), OP.max)
         else:
-            tt(N("ep"), N("ec"), N("sm1"), OP.subtract)
-        dma("s", V("X", O, O + L, lane=4), N("ec"))
-        dma("s", V("X", O, O + L, lane=3), N("ep"))
-        for i in range(0, 16, 2):
-            b = 3 + (i // 2) % 2
-            grp[0] = "s"
-            mm([(PS(b, 256 * h, 256 * h + K), [(cb("A%d" % (i + h)), B("kh0")),
-                                               (cb("M1" if last else "MC"), V("J", i + h, L, 16))]) for h in range(2)])
-            for h in range(2):
-                grp[0] = "s%d" % (b - 3)
-                aff(V("S", i + h, L, 16, tag=i + h), PS(b, 256 * h, 256 * h + K), 1.0, col("bias"))
-        grp[0] = "sc"
-        ka = LAST if last else K
-        act(IND(V("WA", 0, L2 + O), u("pos", 0, ka)), V("S", 0, 16 * ka), AF.Silu)
-        if last:
-            for ln in range(3):
-                fill("V", ln, L2 + O)
-            cp(IND(V("V", 0, L2 + O), u("pos", ka, K)), V("S", 16 * ka, L))
-        M = lambda name: f(name, 0, K2)
-        I = lambda name: ii(name, 0, K2)
-        got = [("pv", 0, O - 1), ("rk", 1, O - 1), ("v", 0, O)] + ([("bd", 2, O)] if last else [])
-        for k_, (nm, ln, lo) in enumerate(got):
-            dma("as"[k_ % 2], M(nm), V("WA", lo, lo + L2, lane=ln))
-        if last:
-            for nm, (_, ln, lo) in zip(("fkg", "lkey", "lkn", "nd"), got):
-                dma("s", M(nm), V("V", lo, lo + L2, lane=ln))
-        grp[0] = "ew"
-        aff(V("EW", 0, n), IND(Xw, su("end", 0, nc)))
-        aff(V("EW", n, n + 128), IND(Xw, su("E", 0, 8)))
-        mm4(conv(PS(7, 0, nc), "Z3", "EW", 0, nc, cm))
-        mm4(conv(PS(7, nc, nc + 8), "Z4", "EW", n, 8, cm))
+            tt(Hf("r1"), Hf("r2"), B("stB"), OP.subtract)
+            tt(Hf("m1"), Hf("r1"), Hf("m2"), OP.max)
+            tt(Hf("r2"), Hf("m1"), hh("W", 7, K + 7), OP.add)
+        ts(u("pos", K, K + 1), PS(6, 2, 3), rm(15), OP.mult, col("spare"), OP.add)
+        ts(u("pos", 0, K), Hf("r2"), PS(6, 1, 2), OP.add, float(O), OP.add)
         if not last:
+            grp[0] = "end"
+            aff(col("cw"), PS(6, 1, 2), 1.0, O - 1.0)
+            mm([(PS(0, 0, K), [(ID, Wi)]), (PS(0, 256, 256 + K), [(ID, Wi), (ID, Hf("m2"))])])
+            aff(N("ec"), PS(0, 0, K), 1.0, col("cw"))
+            aff(N("ep"), PS(0, 256, 256 + K), 1.0, col("cw"))
+            dma("s", V("V", O, O + L, lane=4), N("ec"))
+            dma("s", V("V", O, O + L, lane=3), N("ep"))
+        ka = OPT["last"] if last else K + 1
+        for x, (lo, hi) in enumerate(((0, ka), (ka, K)) if last and OPT["byi"] else ()):
+            for i in range(0, 16, 4):
+                b = 3 + i // 4 % 2
+                grp[0] = "s"
+                for h in range(4):
+                    mm([(PS(b, 128 * h, 128 * h + hi - lo), [(cb("A%d" % (i + h)), bb("jp", lo, hi)), (cb("E%d" % (i + h)), hh("ce", lo, hi)),
+                                                             (cb("M1"), V("J", 16 * lo + i + h, 16 * hi, 16))])])
+                grp[0] = "s%d" % x
+                for h in range(4):
+                    relu(V("S", 16 * lo + i + h, 16 * hi, 16, tag=i + h), PS(b, 128 * h, 128 * h + hi - lo), col("b3"))
+        for c in range(0 if last and OPT["byi"] else K // 32):
+            b = 3 + c % 2
+            grp[0] = "s"
+            parts = [(PS(b, 0, 512), cb("M1" if last else "MC"), V("J", 512 * c, 512 * c + 512))]
+            for i in range(16):
+                parts.append((V("P%d" % b, i, 512, 16), cb(("A%d" if last else "C%d") % i), bb("jp", 32 * c, 32 * c + 32)))
+                if last:
+                    parts.append((V("P%d" % b, i, 512, 16), cb("E%d" % i), hh("ce", 32 * c, 32 * c + 32)))
+            for a in range(0, len(parts), 9):
+                mm([(o, [(l, r)]) for o, l, r in parts[a:a + 9]], a == 0, a + 9 >= len(parts), True)
+            grp[0] = "s0"
+            if last:
+                relu(V("S", 512 * c, 512 * c + 512), PS(b, 0, 512), col("b3"))
+            else:
+                aff(V("S", 512 * c, 512 * c + 512), PS(b, 0, 512), col("ssc"), col("bias"))
+        grp[0] = "sc"
+        act(IND(V("WA", 0, WW), u("pos", 0, ka)), V("S", 0, 16 * ka), AF.Silu)
+        M = lambda name: f(name, 0, K2)
+        if not last:
+            for k_, (nm, ln, lo) in enumerate((("v", 0, O), ("fk", 2, O), ("rk", 1, O - 1))):
+                dma("as"[k_ % 2], M(nm), V("WA", lo, lo + L2, lane=ln))
+            grp[0] = "ew"
+            aff(V("EW", 0, n), IND(Vw, su("end", 0, nc)), rm(3))
+            aff(V("EW", n, n + 128), IND(Vw, su("E", 0, 8)), rm(4))
+            mm4(conv(PS(7, 0, nc + 8), "Z34", "EW", 0, nc + 8, cm))
             cp(su("end", 0, nc + 8), PS(7, 0, nc + 8))
+            if t == 2:
+                ts(sm("pa", 0, nc + 8), PS(7, 0, nc + 8), 0.5, OP.is_lt)
+                tt(sm("pb", 0, nc + 8), sm("pa", 0, nc + 8), sm("pc", 0, nc + 8), OP.mult)
+                tt(sm("pa", 0, nc + 8), sm("pb", 0, nc + 8), PS(7, 0, nc + 8), OP.add)
+                cp(su("eo", 0, nc + 8), sm("pa", 0, nc + 8))
             grp[0] = "n3"
-            cp(I("ka"), M("pv"))
-            tt(M("t1"), M("v"), M("cap"), OP.min)
-            ts(I("kb"), I("ka"), 7168, OP.bitwise_and)
-            tt(M("t3"), M("rk"), I("kb"), OP.add)
-            tt(I("kf"), M("t3"), M("t1"), OP.min)
-            finish(t + 1, KO + KF - 0.5)
+            tt(ii("ka", 0, K2), M("v"), M("rk"), OP.min)
+            ts(ii("kf", 0, K2), ii("ka", 0, K2), NFB - 1, OP.bitwise_and)
+            finish(t + 1)
             continue
-        ts(col("thr"), col("lane"), -256.0, OP.mult, col("len"), OP.add)
-        ts(M("cap"), M("ci"), col("thr"), OP.is_lt, 65536.0, OP.mult)
+        cp(IND(V("X", 0, WW), u("pos", ka, K + 1)), V("S", 16 * ka, L + 16))
+        got = (("s", 0, O), ("e", 3, O), ("c", 4, O), ("k", 5, O - 1))
+        names = {"sW": "v", "eW": "rk", "cW": "fk", "kW": "t1", "sX": "t2", "eX": "t3", "cX": "lkn", "kX": "fkg"}
+        for k_, (nm, ln, lo) in enumerate(got):
+            dma("as"[k_ % 2], M(names[nm + "W"]), V("WA", lo, lo + L2, lane=ln))
+            dma("s", M(names[nm + "X"]), V("X", lo, lo + L2, lane=ln))
         grp[0] = "yf"
         acc = sm("pN")
         for s in range(4):
@@ -591,54 +660,40 @@ def plan(T, core, nxt, topo):
         ts(su("yo"), acc, 1024.0, OP.min)
         aff(V("RR", 0, 1024), IND(V("CF", 0, 1040), su("yo")), -1.0, 15.0)
         dma("s", T.yform[:], V("RR", 0, 1024), 256e3)
-        grp[0] = "ye"
-        ts(sm("rs"), PS(7, 0, 64), 0.5, OP.is_lt)
-        aff(sm("pc"), sm("pN"), 1.0, 4112.0 - 512)
-        tt(sm("pc"), sm("pc"), sm("rs"), OP.mult)
-        tt(sm("rs"), sm("pc"), PS(7, 0, 64), OP.add)
-        cp(su("eo"), sm("rs"))
-        aff(V("GF", 0, 640), V("X", 0, 640), 1.0, 1.0)
-        for s in range(1, 4):
-            lo = 512 + 128 * s
-            ts(V("GF", lo, lo + 128), V("X", lo, lo + 128), col("cum%d" % (s - 1)), OP.add, 1.0 - lo, OP.add)
-        fill("X", 2, 4112)
-        cp(IND(V("X", 0, 4624), su("eo")), V("GF", 0, 1024))
-        dma("s", M("ec"), V("X", O, O + 4096, lane=2))
-        ts(su("rev", 32, 48), sm("pN", 0, 16), -1.0, OP.mult, 255.0, OP.add)
-        red(col("nb"), M("ec"), OP.max)
-        ts(cb("hf"), f("zero", 0, 128), col("nb"), OP.add, 0.5, OP.is_gt)
-        link("LO", cf("LB"), 4)
-        cp(M("fk"), IND(M("ec"), su("rev", 32, 48)))
-        ts(bb("nlr", 0, 256), M("fk"), 0.5, OP.is_lt)
-        scan(M("s0"), bb("nlr", 0, 256), M("fk"), 0.0, OP.mult, OP.add)
-        mm([(PS(5, 0, 1), [(cf("LB"), f("s0", 255, 256))])])
-        scan(M("rs1"), bb("nlr", 0, 256), M("fk"), PS(5, 0, 1), OP.mult, OP.add)
-        aff(M("ep"), IND(M("rs1"), su("rev", 32, 48)), 1.0, -1.0)
-        dma("s", T.ycallee[:], M("ep"))
         grp[0] = "ys"
-        tt(M("v"), M("v"), M("lkn"), OP.add)
-        act(M("t1"), M("v"), AF.Relu, 1.0, -1.0)
-        tt(M("pv"), M("pv"), M("fkg"), OP.add)
-        tt(M("rk"), M("rk"), M("lkey"), OP.add)
-        tt(M("bd"), M("bd"), M("nd"), OP.add)
-        for y, q_, a, b, i_, t_ in ((T.ysite, "s", "pv", "v", "ka", "t2"), (T.ycaller, "a", "rk", "bd", "kb", "t3")):
-            tt(M(t_), M(a), M("t1"), OP.mult)
-            tt(I(i_), M(t_), M(b), OP.add)
-            tt(M(a), I(i_), M("cap"), OP.min)
-            ts(M(t_), M(a), 1023.0, OP.max, -1024.0, OP.add)
-            dma(q_, y[:], M(t_))
+        G = lambda k: M(names[k])
+        tt(M("s0"), G("sW"), G("sX"), OP.add)
+        ts(bb("t1", 0, K2), M("s0"), 16.0, OP.is_lt)
+        mm([(PS(5, 0, 1), [(IW(1), f("s0", K2 - 1, K2))])])
+        scan(M("rn"), bb("t1", 0, K2), M("s0"), PS(5, 0, 1), OP.mult, OP.add)
+        ts(M("sp"), M("rn"), 1023.0, OP.max, MAGIC, OP.add)
+        aff(M("rn"), M("sp"), 1.0, -MAGIC - 1024)
+        dma("s", T.ysite[:], M("rn"))
+        tt(hh("m1", 0, K2), G("eW"), G("eX"), OP.add)
+        mm([(PS(6, 0, 1), [(IB(1), hh("m1", K2 - 1, K2))])])
+        scan(hh("m2", 0, K2), bb("t1", 0, K2), hh("m1", 0, K2), PS(6, 0, 1), OP.mult, OP.add)
+        ts(M("ec"), hh("m2", 0, K2), 1023.0, OP.max, -1024.0, OP.add)
+        dma("s", T.ycallee[:], M("ec"))
+        mm([(PS(1, 0, K2), [(IW(2), G(k)) for k in ("cX", "kX", "cW", "kW")])])
+        ts(hh("r2", 0, K2), PS(1, 0, K2), 1023.0, OP.max)
+        ts(M("ep"), hh("r2", 0, K2), -1024.0, OP.add)
+        dma("a", T.ycaller[:], M("ep"))
     return ops
 
 
 def order(ops):
     hist = {}
     for k, o in enumerate(ops):
-        dep = set()
+        dep, soft = set(), set()
         for acc, w in ((o["rd"], False), (o["wr"], True)):
             for b, lo, hi, tag in acc:
                 for k2, w2, lo2, hi2, tag2 in hist.get(b, []):
                     if (w or w2) and lo < hi2 and lo2 < hi and (tag is None or tag2 is None or tag == tag2):
                         dep.add(k2)
+                    elif SCRATCH[b][0] == "psum":
+                        soft.add(k2)
+        o["soft"] = soft - dep - {k}
+        dep |= soft
         dep.discard(k)
         for b, lo, hi, tag in o["wr"]:
             h = hist.setdefault(b, [])
@@ -652,52 +707,91 @@ def order(ops):
     for k, o in enumerate(ops):
         for d in o["pre"]:
             succ[d].append(k)
-    pr = [0.0] * len(ops)
-    for k in range(len(ops) - 1, -1, -1):
-        pr[k] = ops[k]["alts"][0][2] + ops[k]["lat"] + HOP + max([pr[s] for s in succ[k]] + [0.0])
+    if "best" not in KEPT:
+        KEPT["best"] = arrange(ops, [o["pre"] for o in ops], succ)
+    start, alt = KEPT["best"]
     for k, o in enumerate(ops):
-        pr[k] += BOOST.get(o["g"], 0.0)
-        o["bias"] = BIAS.get(o["g"], 2.0)
-    left = [len(o["pre"]) for o in ops]
-    ready = [k for k in range(len(ops)) if left[k] == 0]
-    free, done, at, seq = {}, [0.0] * len(ops), [0.0] * len(ops), []
+        o["q"], o["fn"], o["cost"] = o["alts"][alt[k]]
+        o["t"] = (start[k], start[k] + o["cost"] + o["lat"])
+    return sorted(range(len(ops)), key=lambda k: (start[k], k))
+
+
+def gap(busy, t, c):
+    lo, hi = 0, len(busy)
+    while lo < hi:
+        mid = (lo + hi) // 2
+        if busy[mid][1] <= t:
+            lo = mid + 1
+        else:
+            hi = mid
+    while lo < len(busy) and busy[lo][0] < t + c:
+        t = max(t, busy[lo][1])
+        lo += 1
+    return t, lo
+
+
+def place(ops, pre, succ, pr, alt, rev):
+    n = len(ops)
+    left = [len(p) for p in pre]
+    ready = [k for k in range(n) if left[k] == 0]
+    busy, done, start, took = {}, [0.0] * n, [0.0] * n, [0] * n
     while ready:
-        pick = {}
-        for k in ready:
-            best = None
-            for n_, (q, fn, c) in enumerate(ops[k]["alts"]):
-                s = max(free.get(q, 0.0), at[k])
-                if best is None or s + c + ops[k]["bias"] < best[0] + best[3]:
-                    best = (s, q, fn, c)
-            pick[k] = best
-        k0 = min(ready, key=lambda k: (pick[k][0], -pr[k]))
-        s0, q0 = pick[k0][0], pick[k0][1]
-        k = max([x for x in ready if pick[x][1] == q0 and pick[x][0] <= s0 + min(LOOK, 0.3 * pick[k0][3] + 0.05)], key=lambda x: pr[x])
-        o = ops[k]
-        s, o["q"], o["fn"], o["cost"] = pick[k]
-        if o["q"] is not None:
-            free[o["q"]] = s + o["cost"]
-        done[k] = s + o["cost"] + o["lat"]
-        o["t"] = (s, done[k])
+        k = max(ready, key=lambda x: pr[x])
         ready.remove(k)
-        seq.append(k)
+        o, best = ops[k], None
+        for a in ([alt[k]] if alt else range(len(o["alts"]))):
+            q, _, c = o["alts"][a]
+            at = 0.0
+            for p in pre[k]:
+                same = ops[p]["alts"][took[p]][0] == q and ops[p]["kind"] == "c"
+                free = same and (q == "t" or p in o["soft"] or k in ops[p]["soft"])
+                at = max(at, done[p] + (0.0 if free or not q else HOP))
+            if rev:
+                at += o["lat"]
+            s, i = gap(busy.setdefault(q, []), at, c) if q else (at, 0)
+            if best is None or s + c + BIAS.get(o["g"], BIAS.get(o["g0"], BIAS0)) < best[0] + best[3]:
+                best = (s, i, a, c, q)
+        s, i, took[k], c, q = best
+        if q:
+            busy[q].insert(i, (s, s + c))
+        start[k], done[k] = s, s + c + (0.0 if rev else o["lat"])
         for x in succ[k]:
             left[x] -= 1
-            at[x] = max(at[x], done[k] + HOP)
             if left[x] == 0:
                 ready.append(x)
-    return seq
+    return start, done, took
 
 
-BOOST = {'ct': 22, 'cl': 7, 'j0': 16, 'j1': 6, 'n2': 14, 's': 26, 's0': 4, 's1': 10, 'sc': 17, 'scan': -5, 'cf': -9, 'prep': -15, 'ew': -8,
-         'ct3': 39, 'j03': 23, 'j13': 8, 'j23': -15, 'j33': 1, 'n23': 10, 's3': -4, 's03': 5, 's13': 22, 'sc3': 2, 'scan3': -4, 'cf3': 7,
-         'prep3': -3, 'ew3': 5, 'arg': 9, 'nq23': -2, 'n1': -6, 'fin2': -1, 'ye3': 4, 'cl2': 6, 'm3': -11, 'rep': 2, 'rep3': 5, 'cl23': 4,
-         'end': -6, 'm': 8, 'n13': 21, 'arg3': -19, 'nq2': -3, 'yf3': -2, 'init': 8, 'j3': -6, 'nl3': 20, 'ys3': -5, 'n3': 11, 'cl3': 3,
-         'end3': -19, 'nl': -1, 'fin': -5, 'init1': -1, 'j2': 18}
-BIAS = {'j0': 1, 'j1': 0, 'j2': 2, 'j3': 4, 'cf': 0, 's0': 1, 's1': 0.3, 'j03': -1, 'j13': 4, 'j23': 4, 'j33': 4, 'cf3': 4, 's03': 2,
-        's13': 4, 'ew3': 2, 'prep3': 50, 'cl2': 0.3, 'ye3': 1, 'yf3': 50, 'm3': 0, 'end3': 1, 'cl23': 0, 'fin2': 2, 'init1': 2,
-        'init2': 50, 'prep': 1, 'm': 4, 'init': 0.3, 'ew': 50}
-LOOK, LAST, SCAT, OPT = 0.3, 128, 3.8, {"ct": 0, "ep": 1, "nq": 9}
+def arrange(ops, pre, succ):
+    n = len(ops)
+    pr = [0.0] * n
+    for k in range(n - 1, -1, -1):
+        pr[k] = min(a[2] for a in ops[k]["alts"]) + ops[k]["lat"] + HOP + max([pr[s] for s in succ[k]] + [0.0])
+    best = None
+    for turn in range(TURNS):
+        start, done, alt = place(ops, pre, succ, [pr[k] + BOOST.get(o["g0"], 0.0) + BOOST.get(o["g"] + "!", 0.0) for k, o in enumerate(ops)], None, False)
+        if best is None or max(done) < best[0]:
+            best = (max(done), start, alt)
+        if turn < 2:
+            pr = place(ops, succ, pre, done, alt, True)[1]
+            continue
+        late, nxt = [max(done)] * n, {}
+        for k in sorted(range(n), key=lambda x: (-start[x], -x)):
+            q, _, c = ops[k]["alts"][alt[k]]
+            t = min([late[s] - HOP for s in succ[k]] + [max(done)]) - ops[k]["lat"]
+            late[k] = min(t, nxt.get(q, t)) - c
+            if q:
+                nxt[q] = late[k]
+            pr[k] += PUSH * max(0.0, 1.0 - (t - c - start[k]) / REACH)
+    return best[1:]
+
+
+BOOST = {'cl': 10, 'arg': 11, 'ew.2!': 16, 'end.2!': 6, 'init': 3, 'cf': -2, 'ys': 5, 's1.3!': -6, 'fin2.2!': 4, 'ct.0!': 2, 'ew': -4, 'nl.2!': -1, 'n1.0!': -6, 'fin2': -3, 's0.1!': -2, 'end.0!': -6, 'n1.3!': -6, 'initA': 8, 'initC': 5, 'rep': 2, 'ct.2!': -1, 'nl.3!': 1, 'nq2.3!': -4, 'jw.3!': 1, 'yf': -2, 'nq2.1!': -2, 'cl.3!': 4, 'cf.0!': -4, 'rep.2!': -1, 'cl2': -2, 'ctp2': 4, 'fin2.0!': 6, 'm.3!': -2, 'cl.0!': 3, 's1': 3, 'ctp3': 1, 'cl2.0!': 7, 'ctp0': 7, 'sc': 1, 'tab.0!': 1, 'scan.2!': -3, 'ye.3!': 2, 'arg.2!': -3, 'cl2.1!': 2, 'prep.0!': 3, 'cl2.3!': 7, 'cl.2!': 1, 's0.2!': 10, 'rep.0!': -1, 'sc.0!': 2, 'j0.3!': 1, 'rep.1!': 12, 'n2.2!': 1, 'nl.1!': 1, 'cf.2!': 1, 'ct.3!': -1, 'sc.3!': -2, 'scan.3!': 3, 'prep.3!': 6, 'n1.2!': 1, 'ye': 2, 'j0.0!': 2, 'cf.3!': 3, 'end.1!': -6, 'ct': 3, 'sc.2!': -2, 'cl2.2!': 2, 'nl': -1, 'j0': 2}
+BIAS = {'ctp2': 0.5, 'ctp3': 0.2, 'ew': 50, 'ew.2': 0, 'j0.1': 50, 'j0': 2, 'm': -1, 'cf.3': 0, 's1.3': 0.5, 's0.3': 0.2, 's1': 0, 'end': 4, 'm.1': 0, 'end.0': 2, 'j1.0': -1, 'cf.1': -1, 'ye': 2, 'ys': 1, 'ctp0': -1, 'init': 0, 'ye.3': 0.5, 'fin2.1': 2, 'n1.3': 0, 'm.2': 0.5, 'fin2.2': 0, 'ys.3': 2, 'cl2.3': 4, 'initA': -1, 'prep.0': -1, 'm.0': 2, 'n1.0': 4, 'm.3': -1, 'prep': 0.2, 'end.1': 0, 'cf.2': 0.5, 'cl2.2': 2, 'j1.2': 0.2, 'fin2': 0.5, 'cl2.1': 50, 'init1': 0.5, 'yf.3': 0.2, 'yf': 0.5}
+BOOST = {'cl': 6, 'arg': 11, 'jw': 11, 'ew.2!': 11, 'end.2!': 4, 'init': 3, 'ys': 1, 'init3': -2, 'prep.3!': 6, 'prep.2!': 6, 's1': 6, 'ctp2': 12, 'jw.2!': -3, 'cl2.0!': -2, 'cl2.3!': 9, 'initA': 2, 'ctp0': 4, 'cl.1!': -6, 'm.0!': 2, 'fin': 1, 'fin2.0!': 5, 's0.1!': 2, 'jw.0!': 6, 'sc.1!': 2, 'n1.1!': 3, 'sc': 2, 'end': 3, 's0.2!': 1, 'ctp1': -2, 'fin.1!': -1, 'cl.0!': -6, 'n1.3!': 2, 'jw.1!': 6, 'sc.3!': -1, 'm.1!': 5, 'ys.3!': 1, 'cf.2!': -2, 'ct': 3, 'end.1!': -2, 'ct.1!': -2, 'cf.0!': 1, 'ct.0!': 1, 'nq2.1!': 6, 'm.2!': 2}
+BIAS = {'ew': 1, 'ew.2': 0, 'end': 0.2, 'cl2': 4, 'cf.0': -1, 'initA': 0.5, 'n1.3': 0.2, 'end.1': 4, 'm.2': 0.5, 'ys.3': 0, 'cl2.0': 4, 'prep.3': 0.5, 's0.3': 50, 'j1.3': 0.2, 'm.3': 50, 'init2': 1, 's0.2': 4, 'prep.1': -1, 'ctp0': -1, 'cf.1': 0, 'ctp2': 0.5, 'cl2.1': 4, 's0.0': 50, 'm.0': 0.5, 'j1.1': 0.5, 'm': 0.5, 'ye': 0.5, 'j0.0': 1, 'n1.2': 4, 's0': 1, 'init': 50}
+BIAS0, TURNS, PUSH, REACH, KEPT = 0.5, 2, 1.0, 1.0, {}
+OPT = {"n2": 1, "byi": 1, "gfill": ("ctp1", "ctp2", "ctp3"), "hv": 0, "cut": (0, 4, 8, 12, 16), "nq": (0, 1, 1, 0), "last": 128}
 
 
 def rank_program(g, core, T, topo):
@@ -719,7 +813,7 @@ def rank_program(g, core, T, topo):
         need = {}
         for d in o["dep"]:
             s, val = ops[d]["sig"]
-            if q == "t" and s == "et":
+            if s == "e" + q and (q == "t" or d in o["soft"]):
                 continue
             need[s] = max(need.get(s, 0), val)
         for s in sorted(need):

from concourse.mybir import AluOpType as OP, AxisListType as AX, ActivationFunctionType as AF

F32, BF, I32, U16, F16 = "float32", "bfloat16", "int32", "uint16", "float16"
NW = 272
O = 16
NF, NB, NI, NU, NH = 20, 23, 4, 5, 8
CJ = (0, 2048, 4096, 1024)
KO = 8192
NFB = 16384
PAD = KO + 5119
JP = 131072.0
MAGIC = 12582912.0
SCRATCH = {
    "J": ("sbuf", [128, 4096], BF), "H": ("sbuf", [128, 4096], BF), "TT": ("sbuf", [128, 5136], BF),
    "TR": ("sbuf", [128, 4096], BF), "A": ("sbuf", [128, 4096], BF), "NQ": ("sbuf", [128, 3584], BF),
    "S": ("sbuf", [128, 3600], F32), "V": ("sbuf", [128, 3600], F32), "X": ("sbuf", [128, 4128], F32),
    "WA": ("sbuf", [128, 4128], F32),
    "CF": ("sbuf", [128, 1040], BF), "RR": ("sbuf", [128, 1024], BF), "BW": ("sbuf", [128, 1024], F32),
    "GF": ("sbuf", [128, 896], F32), "RC": ("sbuf", [128, 1024], F32), "EW": ("sbuf", [128, 1024], F32),
    "N": ("sbuf", [128, NF * NW], F32), "SM": ("sbuf", [128, 16 * 64], F32), "SU": ("sbuf", [128, 10 * 64], U16),
    "NBF": ("sbuf", [128, NB * NW], BF), "NIN": ("sbuf", [128, NI * NW], I32), "NUN": ("sbuf", [128, NU * NW], U16),
    "NHF": ("sbuf", [128, NH * NW], F16),
    "CM": ("sbuf", [128, 12 * 160], F32), "CB": ("sbuf", [128, 80 * 128], BF), "COL": ("sbuf", [128, 80 * 4], F32),
    "RP": ("sbuf", [128, 4 * 384], F32),
}
for _t in range(4):
    SCRATCH["CT%d" % _t] = ("sbuf", [128, 1024 + 512 + 128 * _t], BF)
    SCRATCH["TI%d" % _t] = ("sbuf", [128, 512 + 128 * _t], BF)
for _b in range(8):
    SCRATCH["P%d" % _b] = ("psum", [128, 512], F32)
SEMAPHORES = ["ev", "ea", "et", "eg"] + ["d%d" % i for i in range(110)] + ["r%d" % i for i in range(16)] + ["l%d" % i for i in range(16)]
HOP, CY, FIX, GFIX, GATHER, SCATTER, TCY, DLAT, RLAT, RBW = 0.25, 0.9e-3, 0.02, 0.25, 1.4, 3.0, 0.4e-3, 1.5, 1.3, 120e3


def plan(T, core, nxt, topo):
    ops = []
    tiles = {}
    grp = ["init", ""]

    def V(b, lo, hi, step=1, tag=None, lane=None):
        rows = slice(None) if lane is None else slice(lane, 128, 16)
        ap = T[b][rows, lo:hi] if step == 1 else T[b][rows, lo:hi:step]
        w = SCRATCH[b]
        assert hi <= w[1][1], (b, hi)
        if w[0] == "psum":
            r = (b, 0, 512, None)
        else:
            r = (b, lo, hi, ("L", lane) if lane is not None else tag)
        return {"ap": ap, "r": [r], "n": len(range(lo, hi, step)), "dt": w[2], "ps": w[0] == "psum", "ind": False}

    def back(x):
        b, lo, hi, _ = x["r"][0]
        return dict(x, ap=T[b][:, hi - 1:(lo - 1 if lo else None):-1])

    def tile(b, w):
        def at(name, lo=0, hi=w, slots=1):
            d = tiles.setdefault(b, {})
            if name not in d:
                d[name] = len(d)
                if slots > 1:
                    d[name + "+"] = len(d)
            return V(b, d[name] * w + lo, d[name] * w + hi)
        return at

    f, bb, ii, u, hh = tile("N", NW), tile("NBF", NW), tile("NIN", NW), tile("NUN", NW), tile("NHF", NW)
    sm, su, cm, cb, col4 = tile("SM", 64), tile("SU", 64), tile("CM", 160), tile("CB", 128), tile("COL", 4)
    col = lambda name: col4(name, 0, 1)
    cf = lambda name, lo=0, hi=128: cm(name, lo, hi)
    PS = lambda b, lo, hi: V("P%d" % b, lo, hi)

    def IND(w, o):
        return {"ap": w["ap"].indirect(o["ap"]), "r": w["r"], "o": o["r"], "n": 16 * o["n"], "dt": w["dt"], "ps": False, "ind": True}

    def add(alts, outs, ins, kind="c", lat=0.0):
        rd, wr = [], []
        for x in ins:
            if isinstance(x, dict):
                rd.extend(x["r"])
                rd.extend(x.get("o", []))
        for x in outs:
            wr.extend(x["r"])
            rd.extend(x.get("o", []))
        ops.append({"alts": alts, "rd": rd, "wr": wr, "kind": kind, "lat": lat, "g": grp[0] + grp[1], "g0": grp[0]})
        return len(ops) - 1

    def ap(x):
        return x["ap"] if isinstance(x, dict) else x

    def vc(o, ins, base=1.0):
        if o["ind"]:
            base = SCATTER
        elif any(x["ind"] for x in ins):
            base = GATHER
        elif all(x["dt"] in (BF, U16, F16) for x in ins + [o]):
            base = base / 2
        return FIX + max(64, ins[0]["n"] * base) * CY

    def ac(o, i):
        return FIX + 0.015 + max(64, i["n"] * (SCATTER if o["ind"] else GATHER if i["ind"] else 1.0)) * CY

    def cp(o, i):
        add([("v", lambda e: e.tensor_copy(o["ap"], i["ap"]), vc(o, [i]))], [o], [i])

    def tt(o, a, b, op):
        add([("v", lambda e: e.tensor_tensor(o["ap"], a["ap"], b["ap"], op), vc(o, [a, b], 1.0 if a["ps"] or b["ps"] else 2.0))], [o], [a, b])

    def tsf(o, a, s1, o0, s2, o1):
        if o1 is None:
            return lambda e: e.tensor_scalar(o["ap"], a["ap"], ap(s1), None, o0)
        return lambda e: e.tensor_scalar(o["ap"], a["ap"], ap(s1), ap(s2), o0, o1)

    def ts(o, a, s1, o0, s2=None, o1=None):
        add([("v", tsf(o, a, s1, o0, s2, o1), vc(o, [a]))], [o], [a, s1, s2])

    def scan(o, a, b, init, o0, o1):
        add([("v", lambda e: e.tensor_tensor_scan(o["ap"], a["ap"], b["ap"], ap(init), o0, o1), vc(o, [a, b]))], [o], [a, b, init])

    def ms(o, c):
        add([("v", lambda e: e.memset(o["ap"], c), vc(o, [o]))], [o], [])

    def act(o, i, fn, bias=0.0, scale=1.0, acc=None):
        if o["ind"]:
            fa = lambda e: e.activation(o["ap"], i["ap"], fn)
        elif acc is not None:
            fa = lambda e: e.activation(o["ap"], i["ap"], fn, bias=ap(bias), scale=ap(scale), accum_out=acc["ap"])
        else:
            fa = lambda e: e.activation(o["ap"], i["ap"], fn, bias=ap(bias), scale=ap(scale))
        add([("a", fa, ac(o, i))], [o] + ([acc] if acc else []), [i, bias, scale])

    def aff(o, i, scale=1.0, bias=0.0, more=()):
        add(list(more) + [("a", lambda e: e.activation(o["ap"], i["ap"], AF.Identity, bias=ap(bias), scale=ap(scale)), ac(o, i)),
                          ("v", tsf(o, i, scale, OP.mult, bias, OP.add), vc(o, [i]))], [o], [i, bias, scale])

    def relu(o, i, bias):
        add([("a", lambda e: e.activation(o["ap"], i["ap"], AF.Relu, bias=ap(bias), scale=1.0), ac(o, i)),
             ("v", tsf(o, i, bias, OP.add, 0.0, OP.max), vc(o, [i]))], [o], [i, bias])

    def mm(groups, first=True, final=True, one=False):
        def fm(e):
            for x, (o, lst) in enumerate(groups):
                for k, (l, r) in enumerate(lst):
                    last = e.matmul(o["ap"], l["ap"], r["ap"], first and k == 0 and not (one and x),
                                    final and k == len(lst) - 1 and not (one and x < len(groups) - 1))
            return last
        c = sum(max(64, r["n"]) * (4 if r["dt"] == F32 else 1) for o, lst in groups for l, r in lst)
        add([("t", fm, 0.06 + c * TCY)], [o for o, _ in groups], [x for _, lst in groups for lr in lst for x in lr])

    def mm4(group):
        for a in range(0, 16, 4):
            mm([(group[0], group[1][a:a + 4])], a == 0, a == 12)

    def dma(q, o, i, nb=0):
        add([(q, lambda e: e.dma_start(ap(o), ap(i)), 0.1)], [o] if isinstance(o, dict) else [], [i], "d", DLAT + nb / 150e3)

    def iotaf(o, pat, base, chm):
        kw = {} if o["dt"] == I32 else {"allow_small_or_imprecise_dtypes": True}
        return ("g", lambda e: e.iota(o["ap"], pat, base, chm, **kw), GFIX + 0.13 + 2 * CY * o["n"])

    def iota(o, pat, base, chm):
        add([iotaf(o, pat, base, chm)], [o], [])

    def const(o, c):
        alts = [("v", lambda e: e.memset(o["ap"], float(c)), vc(o, [o])), iotaf(o, [[0, o["n"]]], c, 0)]
        add(alts[::-1] if grp[0] in OPT["gfill"] else alts, [o], [])

    def aself(o, i, pat, cmp, base, chm):
        return ("g", lambda e: e.affine_select(o["ap"], i["ap"], pat, cmp, 0.0, base, chm), GFIX + 0.17 + 2 * CY * o["n"])

    def asel(o, i, step, cmp, base, chm):
        add([aself(o, i, [[step, 128]], cmp, base, chm)], [o], [i])

    def pick(o, i, lane):
        aff(o, i, rm(lane), 0.0, [aself(o, i, [[-16, 8], [0, 16]], OP.is_equal, -lane, 1)])

    nsend = [0]

    def send(src, dst):
        k = nsend[0]
        nsend[0] += 1
        rid, pid = topo.addr(nxt, core)
        m = topo.mask(core, nxt)
        fs = lambda e: e.remote_dma(dst["ap"], src["ap"], T.sem["r%d" % k], T.sem["l%d" % k], pid, rid, m)
        s = add([("g", fs, 0.7)], [], [src], "s", RLAT + src["n"] * 256 / RBW)
        r = add([(None, None, 0.0)], [dst], [], "r")
        for x in (s, r):
            ops[x]["k"] = k
            ops[x]["cnt"] = len(topo.engines(core, nxt))
        ops[r]["after"] = s

    dma("s", ii("runb", 0, 32), T.runs[:])
    dma("a", V("RR", 0, 512), T.form[:], 128e3)
    for n_, j in enumerate((3, 0, 1, 2)):
        for sp in range(2):
            dma("sa"[sp], V("J", j * 1024 + sp * 512, j * 1024 + sp * 512 + 512), T.jump[:, sp * 2048 + j * 512: sp * 2048 + j * 512 + 512], 128e3 * (2 * n_ + 2))
        if n_ == 0:
            dma("s", ii("calls", 0, 128), T.calls[:])
    iota(ii("runb", 64, 65), [[0, 1]], 0, 1)
    iota(cf("xg"), [[16, 8], [0, 16]], 0, 0)
    iota(f("ci", 0, 160), [[1, 160]], 0, 0)
    ts(ii("runb", 68, 69), ii("runb", 64, 65), 15, OP.bitwise_and)
    ts(ii("runb", 72, 73), ii("runb", 64, 65), 112, OP.bitwise_and)
    cp(col("lane"), ii("runb", 68, 69))
    cp(col("g16"), ii("runb", 72, 73))
    cp(col("p"), ii("runb", 64, 65))
    ts(cb("BO"), cf("xg"), col("g16"), OP.is_equal)
    ts(cb("IW", 0, 132, 2), f("ci", 0, 132), -2.0, OP.add, col("p"), OP.is_equal)
    ts(cm("IW", 0, 132), f("ci", 0, 132), -2.0, OP.add, col("p"), OP.is_equal)
    IB, IW = lambda s: cb("IW", s, s + 128), lambda s: cm("IW", s, s + 128)
    ID = IB(2)
    ts(sm("rm", 0, 16), f("ci", 0, 16), col("lane"), OP.is_equal)
    rm = lambda i: sm("rm", i, i + 1)
    ts(cm("xm"), f("ci", 0, 160), col("g16"), OP.subtract)
    ts(cb("Z", 0, 144, 2), cm("xm", 0, 144), 15.0, OP.is_equal)
    ts(cb("Z0", 0, 144, 2), cb("Z", 0, 144), rm(0), OP.mult)
    for nm, cmp in (("UT", OP.is_gt), ("LO", OP.is_lt)):
        ts(cb("M2"), f("ci", 0, 128), col("p"), cmp)
        tt(cb(nm), cb("M2"), cb("BO"), OP.mult)
    ms(f("one", 0, 128), 1.0)
    ms(bb("one", 0, 272), 1.0)
    ms(f("zero", 0, 258), 0.0)
    ts(sm("pN"), f("ci", 0, 64), 16.0, OP.mult, col("lane"), OP.add)
    for nm in ("UT", "LO"):
        aff(cb(nm + "b"), cb(nm), -64.0, 64.0)

    def mix(name, *terms):
        acc = 0.0
        for k, (lane, c) in enumerate(terms):
            o = col(name if k == len(terms) - 1 else name + "%d" % (k % 2))
            aff(o, rm(lane), float(c), acc)
            acc = o
        return acc

    def fill(b, lane, w, src="zero"):
        dma("s", V(b, 0, w, lane=lane), f(src, 0, w // 16), 30e3)

    def conv(out, Zn, src, lo, ncol, band=cb):
        return (out, [(band(Zn, 15 - i, 143 - i), V(src, lo + i, lo + 16 * ncol, 16)) for i in range(16)])

    def table(t):
        n = 512 + 128 * t
        grp[0] = "tab"
        mm([conv(PS(7, 0, n // 16), "Z0", "CF", 0, n // 16)])
        ts(sm("jo", 0, n // 16), PS(7, 0, n // 16), 0.5, OP.is_gt, 512.0, OP.mult)
        tt(sm("jo2", 0, n // 16), sm("jo", 0, n // 16), sm("body", 0, n // 16), OP.add)
        ts(su("jo", 0, n // 16), sm("jo2", 0, n // 16), 0.25, OP.add)
        for j in (3, 0, 1, 2):
            tt(V("TR", j * 1024, j * 1024 + n), IND(V("H", j * 1024, j * 1024 + 1024), su("jo", 0, n // 16)), V("CF", 0, n), OP.min)
            if j == 3:
                send(V("TR", 3072, 3072 + n), V("TI%d" % t, 0, n))
            else:
                act(V("TT", O + CJ[j], O + CJ[j] + n), V("TR", j * 1024, j * 1024 + n), AF.Abs)
        act(V("TT", O + CJ[3], O + CJ[3] + n), V("TI%d" % t, 0, n), AF.Abs)

    def finish(t):
        K = 128 + 32 * t
        kf, v, fb, nf, hb = ii("kf", 0, K), f("v", 0, K), f("fk", 0, K), bb("nf", 0, K), f("l0", K - 1, K)
        grp[0] = "fin"
        ts(u("key", 0, K), kf, float(O - KO), OP.add)
        scan(f("l0", 0, K), fb, v, 0.0, OP.max, OP.min)
        mm([(PS(5, 0, 1), [(cf("SX"), hb)]), (PS(5, 1, 2), [(IW(1), hb)])])
        ts(col("c1"), PS(5, 0, 1), PS(5, 1, 2), OP.max)
        scan(f("lkn", 0, K), fb, v, col("c1"), OP.max, OP.min)
        ts(u("lk", 0, K), f("lkn", 0, K), 0.25 + O - KO, OP.add)
        grp[0] = "fin2"
        ts(nf, fb, 16.0, OP.is_lt)
        aff(cb("hL"), cb("LO"), hb)
        mm([(PS(1, 0, 128), [(cb("hL"), cb("UT")), (ID, cb("UTb"))])])
        act(cb("LK"), PS(1, 0, 128), AF.Relu, 1.0, -1.0)
        act(cf("LK"), PS(1, 0, 128), AF.Relu, 1.0, -1.0)
        ts(ii("ka", 0, K), kf, 2047, OP.bitwise_and)
        cp(u("ck", 0, K), ii("ka", 0, K))
        mm([(PS(6, 0, 1), [(IB(3), bb("nf", 0, 1))])])
        aff(bb("nf", K, K + 1), PS(6, 0, 1))
        aff(cb("hU"), cb("UT"), hb)
        mm([(PS(2, 0, 128), [(cb("hU"), cb("LO")), (ID, cb("LOb"))])])
        act(cb("LB"), PS(2, 0, 128), AF.Relu, bb("nf", 0, 1), -1.0)
        if t < 3:
            aff(f("t1", 0, K), nf, float(NFB), JP - 511.5)
            tt(bb("jp", 0, K), f("t1", 0, K), kf, OP.add)
        else:
            ts(bb("t1", 0, K), kf, 0.25, OP.mult, 65536 - 255.875, OP.add)
            ts(bb("t2", 0, K), ii("ka", 0, K), 1023.5, OP.is_gt, 1536.0, OP.mult)
            tt(bb("jp", 0, K), bb("t1", 0, K), bb("t2", 0, K), OP.add)

    ts(V("CF", 0, 512), V("RR", 0, 512), -1.0, OP.mult, 15.0, OP.add)
    aff(sm("body", 0, 32), sm("pN", 0, 32))
    for n_, j in enumerate((3, 0, 1, 2)):
        ts(V("A", j * 1024, j * 1024 + 1024), V("J", j * 1024, j * 1024 + 1024), 14.5, OP.is_lt, -15.0, OP.mult)
        if n_ < OPT["hv"]:
            tt(V("H", j * 1024, j * 1024 + 1024), V("J", j * 1024, j * 1024 + 1024), V("A", j * 1024, j * 1024 + 1024), OP.add)
            continue
        for h in range(2):
            lo = j * 1024 + 512 * h
            b = 1 + (2 * n_ + h) % 2
            mm([(PS(b, 0, 512), [(ID, V("J", lo, lo + 512)), (ID, V("A", lo, lo + 512))])])
            act(V("H", lo, lo + 512), PS(b, 0, 512), AF.Identity)
    for lo, hi in ((-O, 0), (512, 1024), (1536, 2048), (2560, 4096), (4608, 5120)):
        ms(V("TT", O + lo, O + hi), 0.0)
    aff(cf("NI"), IW(1), -2.0)
    tt(cf("SX"), cf("NI"), IW(0), OP.add)
    ms(f("t1", 0, 129), float(NFB))
    fill("WA", 0, 2064, "t1")
    cp(sm("runb", 0, 32), ii("runb", 0, 32))
    scan(sm("rs", 0, 32), f("one", 0, 32), sm("runb", 0, 32), 0.0, OP.mult, OP.add)
    aff(cf("UT"), cb("UT"))
    mm([(PS(5, 0, 1), [(cf("UT"), sm("rs", 31, 32))])])
    tt(sm("rs2", 0, 32), sm("rs", 0, 32), sm("runb", 0, 32), OP.subtract)
    ts(su("st", 0, 32), sm("rs2", 0, 32), PS(5, 0, 1), OP.add, float(O), OP.add)
    const(V("RC", 0, 512), 0)
    act(IND(V("WA", 0, 2064), su("st", 0, 32)), V("RC", 0, 512), AF.Silu)
    dma("s", f("ep", 0, 128), V("WA", O, O + 2048, lane=0))
    aff(f("fk", 0, 128), f("ep", 0, 128), -1.0, float(NFB))
    ts(ii("ka", 0, 128), ii("calls", 0, 128), 9, OP.logical_shift_right)
    ts(f("t2", 0, 128), ii("ka", 0, 128), 1536.0, OP.mult, float(KO), OP.add)
    ts(f("t3", 0, 128), ii("calls", 0, 128), 1535.5, OP.is_gt, -5120.0, OP.mult)
    tt(f("rk", 0, 128), f("t2", 0, 128), ii("calls", 0, 128), OP.add)
    tt(ii("kf", 0, 128), f("rk", 0, 128), f("t3", 0, 128), OP.add)
    tt(f("v", 0, 128), f("ep", 0, 128), ii("kf", 0, 128), OP.add)
    table(0)
    finish(0)
    grp[0] = "init1"
    iota(V("S", 0, 516), [[1, 516]], 0, 0)
    ts(sm("xo", 0, 8), f("ci", 0, 8), 516.0, OP.mult, rm(2), OP.mult)
    for k in range(4):
        aff(V("X", 516 * k, 516 * k + 516), V("S", 0, 516), rm(2), sm("xo", k, k + 1))
    aff(cm("Z34", 0, 144), cb("Z", 0, 144), mix("m34", (3, 1), (4, 1)))
    for h in range(2):
        const(V("EW", 512 * h, 512 * h + 512), 0)
    cp(sm("rs", 0, 32), su("st", 0, 32))
    tt(sm("rs2", 0, 32), sm("rs", 0, 32), sm("runb", 0, 32), OP.add)
    dma("s", V("EW", 0, 512, lane=3), sm("rs2", 0, 32))
    dma("s", V("EW", 512, 1024, lane=3), sm("rs", 0, 32))
    mm4(conv(PS(7, 0, 64), "Z34", "EW", 0, 64, cm))
    ts(su("end", 0, 32), PS(7, 0, 32), -1.0, OP.add)
    cp(su("stw", 0, 32), PS(7, 32, 64))
    ts(f("ec", 0, 128), ii("kf", 0, 128), float(O - KO), OP.add)
    dma("s", V("X", O, O + 2048, lane=4), f("ec", 0, 128))
    aff(V("EW", 0, 512), IND(V("X", 0, 2064), su("stw", 0, 32)), rm(4))
    mm4(conv(PS(7, 0, 32), "Z34", "EW", 0, 32, cm))
    cp(su("LK", 0, 32), PS(7, 0, 32))
    grp[0] = "init2"
    for k in range(4, 7):
        aff(V("X", 516 * k, 516 * k + 516), V("X", 0, 516), rm(2), sm("xo", k, k + 1))
    aff(cf("NI"), ID, -1.0)
    aff(cb("NI"), ID, -1.0)
    aff(cb("I5"), ID, 4096.0)
    aff(cb("NI5"), ID, -4096.0)
    ms(bb("m129", 0, 1), -129.0 / 16)
    iota(V("NQ", 2048, 3072), [[1, 64], [0, 16]], 0, 0)
    iota(V("NQ", 3072, 3584), [[0, 32], [1, 16]], 0, 0)
    mix("o12", (2, 32), (12, 1))
    aff(col("o56"), mix("m56", (5, 1), (6, 1)), 32.0, col("o12"))
    for h, (hi, lo, c) in enumerate(((mix("hi", (5, 1), (10, 1)), mix("lo", (6, 1), (11, 1)), col("o56")), (rm(10), rm(11), col("o12")))):
        aff(cb("M1"), ID, hi)
        aff(cb("M2"), ID, lo)
        mm([(PS(3 + h, 0, 512), [(cb("M1"), V("NQ", 2048 + 512 * h, 2560 + 512 * h)), (cb("M2"), V("NQ", 3072, 3584))])])
        aff(V("BW", 512 * h, 512 * h + 512), PS(3 + h, 0, 512), 1.0, c)
    aff(col("sg"), mix("s7", (0, 1), (7, 1), (8, 1), (9, 1)), -2.0, 1.0)
    mix("padc", (10, 63), (11, 15), (12, 1), (13, 1), (5, -31), (6, 15), (7, 1024))
    for t in range(4):
        grp[0] = "ctp%d" % t
        const(V("CT%d" % t, 512 + 128 * t, 1008), 0)
        aff(V("CT%d" % t, 1008, 1024), f("one", 0, 16), col("padc"))
    grp[0] = "init2"
    aff(cb("Zw", 0, 144, 2), cb("Z", 0, 144), mix("cw1", (12, 2), (13, -1)))
    aff(cb("Zp", 0, 144, 2), cb("Z", 0, 144), mix("cp1", (0, -1), (12, 128), (13, 2048)))
    aff(sm("pN1"), sm("pN"), 1.0, 128.0)
    aff(cf("R1"), cb("BO"), rm(1))
    aff(cf("R2"), cb("BO"), rm(2))
    aff(cf("R5"), cb("BO"), mix("w56", (5, 16), (6, 1)))
    aff(col("rcf"), rm(1), KO - 32.0, 32.0)
    ts(V("RP", 0, 384), V("NQ", 3072, 3456), col("lane"), OP.is_equal)
    ts(V("RP", 384, 768), V("NQ", 3072, 3456), 0.5, OP.is_gt)

    def lanes(name, terms):
        for k, (lane, w) in enumerate(terms):
            aff(cb("M2") if k else cb(name), cb("Z", 15 - lane, 143 - lane), w)
            if k:
                tt(cb(name), cb(name), cb("M2"), OP.add)

    wab = mix("wab", (10, 16), (11, 1))
    lanes("MC", [(0, wab), (2, wab), (1, mix("w0c", (0, -1), (13, 2 * NFB)))])
    aff(col("ssc"), rm(2), -3.0, 1.0)
    aff(col("b0"), rm(2), 40000 + 3 * JP, -JP)
    aff(cb("Z2", 0, 144, 2), cb("Z", 0, 144), 2.0)
    ms(bb("m17", 0, 224), -17.0 / 16)
    ms(f("pad", 0, 258), float(NFB + PAD))
    ts(hh("W", 0, 8), f("zero", 0, 8), 0.0, OP.add)
    grp[0] = "initC"
    for i in range(16):
        aff(cb("C%d" % i), cb("BO"), rm(i))
    grp[0] = "initA"
    ms(V("V", 0, O), 0.0)
    ms(V("CF", 1024, 1040), 0.0)
    ms(col("gs"), 0.0)
    aff(col("pad1"), rm(1), 2.0 * NFB, float(PAD))
    aff(col("padS"), rm(2), 40000.0 - 3 * PAD, col("pad1"))
    aff(col("n15"), rm(15), -1.0, 1.0)
    aff(col("sp0"), col("lane"), col("n15"), float(O))
    grp[0] = "init3"
    for i in range(16):
        pick(cb("A%d" % i), cb("Z", 15, 143), i)
        pick(cb("E%d" % i), cb("Z", 12, 140), i)
    aff(col("wa7"), rm(7), -1.0, wab)
    lanes("M1", [(0, col("w56")), (4, col("wa7")), (5, mix("w089", (0, -1), (8, -1), (9, -1), (13, -KO)))])
    mix("b3", (0, 1024 - 544 - 67584), (3, 1024 - 33), (4, 1024), (5, 2048))
    aff(col("padL"), rm(5), -1023.0, 1023.0)
    aff(sm("pc"), sm("pN"), 1.0, 3600.0 - 512)

    for t in range(4):
        K = 128 + 32 * t
        L, n, K2, q = 16 * K, 512 + 128 * t, K + 32, K // 4
        L2, last, nc = 16 * K2, t == 3, n // 16
        WW = L2 + O + 16
        N = lambda name: f(name, 0, K)
        B = lambda name: bb(name, 0, K)
        Hf = lambda name: hh(name, 0, K)
        nl1 = bb("nf", 1, K + 1)
        CT = "CT%d" % t
        Tw = V("TT", 0, 5120 + O)
        Xw, Vw = V("X", 0, L + O), V("V", 0, L + O)
        grp[0], grp[1] = "prep", ".%d" % t
        aff(V("RC", 0, 128), f("one", 0, 128), col("rcf"))
        aff(col("spare"), col("n15"), L2 + 1.0, col("sp0"))
        aff(V("S", L, L + 16), f("one", 0, 16), col("padL" if last else "padS"))
        if last:
            grp[0] = "ye"
            fill("WA", 2, WW)
            aff(V("EW", 0, 640), V("X", 0, 640), 1.0, 33.0)
            for s in range(1, 3):
                lo = 512 + 128 * s
                aff(col("ce%d" % s), col("cum%d" % (s - 1)), 1.0, 33.0 - lo)
                aff(V("EW", lo, lo + 128), V("X", lo, lo + 128), 1.0, col("ce%d" % s))
            act(IND(V("WA", 0, WW), su("eo", 0, nc)), V("EW", 0, n), AF.Silu)
            dma("s", N("ec"), V("WA", O, O + L, lane=2))
            aff(col("c3"), col("cum2"), 1.0, 128.0 + 33)
            grp[0] = "prep"
            for ln in (0, 3, 4, 5):
                fill("WA", ln, WW)
        else:
            fill("WA", 0, WW, "pad")
            fill("WA", 1, WW, "pad")
            fill("WA", 2, WW)
            aff(col("bias"), rm(1), n + 128.0, col("b0"))
        grp[0] = "arg"
        cut = [K * x // 16 // 2 * 2 for x in OPT["cut"]]
        for c, (lo, hi) in enumerate(zip(cut, cut[1:])):
            act(V("A", 16 * lo, 16 * hi), IND(Tw, u("key", lo, hi)), AF.Identity)
            tt(V("NQ", 16 * lo, 16 * hi), IND(Tw, u("lk", lo, hi)), V("A", 16 * lo, 16 * hi), OP.not_equal)
            if c >= len(cut) - 3:
                a = 0 if c == len(cut) - 3 else lo
                o_, lst = conv(PS(0, a, hi), "Z2", "NQ", 16 * a, hi - a)
                mm([(o_, [(cb("BO"), bb("m17", a, hi))] + lst)])
        grp[0] = "n1"
        s1, s1b = bb("s1", 8, K + 8), bb("s1", 7, K + 7)
        scan(B("s0"), B("nf"), PS(0, 0, K), 0.0, OP.mult, OP.max)
        ts(B("dis"), PS(0, 0, K), 0.0, OP.is_gt)
        mm([(PS(b, 0, 1), [(cb("LK"), bb("s0", K - 1, K))]) for b in (5, 6)])
        scan(s1, B("nf"), B("dis"), PS(5, 0, 1), OP.mult, OP.max)
        aff(bb("s1", 7, 8), PS(6, 0, 1))
        tt(B("fd"), B("dis"), s1b, OP.is_gt)
        scan(B("cum"), B("one"), B("fd"), 0.0, OP.mult, OP.add)
        mm([(PS(5, 0, 1), [(cb("UT"), bb("cum", K - 1, K)), (cb("BO"), bb("m129", 0, 1))]), (PS(6, 0, 1), [(cb("BO"), bb("cum", K - 1, K))])])
        act(col("gap%d" % t), PS(6, 0, 1), AF.Relu, 128.0, -1.0)
        tt(N("t2"), B("fd"), ii("kf", 0, K), OP.mult)
        scan(N("s0"), B("nf"), N("t2"), 0.0, OP.mult, OP.add)
        mm([(PS(6, 0, 1), [(cf("LK"), f("s0", K - 1, K))])])
        act(B("s0"), s1, AF.Relu, 1000.0, -1000.0)
        tt(B("rn"), B("cum"), B("s0"), OP.add)
        ts(N("rn"), B("rn"), PS(5, 0, 1), OP.add, 0.0, OP.min)
        dma("s", V("X", O, O + L, lane=0), N("rn"))
        dma("a", V("X", O, O + L, lane=13), N("rn"))
        scan(N("fkg"), B("nf"), N("t2"), PS(6, 0, 1), OP.mult, OP.add)
        dma("s", V("X", O, O + L, lane=1), N("fkg"))
        ts(B("ok"), B("cum"), PS(5, 0, 1), OP.add, -0.5, OP.is_lt)
        tt(B("mv"), B("ok"), B("dis"), OP.mult)
        grp[0] = "nl"
        mm([(PS(3, 0, K), [(IW(2), N("fkg")), (cf("NI"), N("lkn"))])])
        tt(N("t1"), PS(3, 0, K), B("mv"), OP.mult)
        mm([(PS(4, 0, K), [(IW(2), N("t1")), (IW(2), N("lkn"))])])
        ts(u("nl", 0, K), PS(4, 0, K), 0.25 + O - KO, OP.add)
        grp[0] = "m"
        mm([(PS(6, 0, 1), [(IB(3), bb("mv", 0, 1))])])
        aff(B("wi"), B("mv"), 4095.0 / 4096, 1.0 / 4096)
        aff(bb("wi", K, K + 1), PS(6, 0, 1), 4095.0 / 4096, 1.0 / 4096)
        mm([(PS(1, 0, K), [(cb("I5"), B("nf")), (cb("NI5"), B("mv")), (ID, B("mv"))])])
        tt(B("m"), PS(1, 0, K), bb("wi", 1, K + 1), OP.mult)
        aff(B("st"), B("mv"), -1.0, 1.0)
        aff(B("stB"), B("mv"), -4096.0, 4096.0)
        if not last:
            aff(B("t2"), B("mv"), float(NFB))
            tt(B("t1"), B("fd"), B("t2"), OP.mult)
            tt(B("jp"), B("jp"), B("t1"), OP.subtract)
        else:
            grp[0] = "ye"
            scan(back(Hf("r1")), back(nl1), back(N("ec")), 0.0, OP.mult, OP.add)
            mm([(PS(7, 0, 1), [(cb("LB"), hh("r1", 0, 1))])])
            scan(back(Hf("ce")), back(nl1), back(N("ec")), PS(7, 0, 1), OP.mult, OP.add)
            aff(N("t3"), N("rn"), 1.0, col("c3"))
            tt(Hf("r1"), N("t3"), B("stB"), OP.subtract)
            tt(Hf("ce"), Hf("r1"), Hf("ce"), OP.max)
        grp[0] = "ct"
        for lo, hi in ((0, nc // 2), (nc // 2, nc)):
            tt(V("GF", 16 * lo, 16 * hi), IND(Xw, su("end", lo, hi)), V("BW", 16 * lo, 16 * hi), OP.add)
            act(V(CT, 16 * lo, 16 * hi), V("GF", 16 * lo, 16 * hi), AF.Relu, rm(13), col("sg"))
        send(V(CT, 0, n), V(CT, 1024, 1024 + n))
        if last:
            for ln in (0, 3, 4, 5):
                fill("X", ln, WW)
        grp[0] = "cl"
        mm([conv(PS(7, 0, nc), "Zp", CT, 0, nc)])
        tt(sm("pa", 0, nc), PS(7, 0, nc), sm("pN1", 0, nc), OP.min)
        cp(su("po", 0, nc), sm("pa", 0, nc))
        act(IND(V("RC", 0, 128 + n), su("po", 0, nc)), V("GF", 0, n), AF.Silu)
        grp[0] = "rep"
        rw = 256 if last else 384
        mm([(PS(7, 128 * a, 128 * a + 128), [(cf(nm), V("RC", 0, 128))]) for a, nm in enumerate(("R1", "R2", "R5")[:rw // 128])])
        tt(V("RP", 768, 768 + rw), PS(7, 0, rw), V("RP", 0, rw), OP.mult)
        scan(V("RP", 1152, 1152 + rw), V("RP", 384, 384 + rw), V("RP", 768, 768 + rw), 0.0, OP.mult, OP.add)
        ts(su("LK", nc, nc + 8), V("RP", 1152 + 15, 1152 + 128, 16), 0.25 + O - KO, OP.add)
        ts(su("E", 0, 8), V("RP", 1152 + 143, 1152 + 256, 16), -31.75, OP.add)
        grp[0] = "cl2"
        if not last:
            aff(sm("body", nc, nc + 8), V("RP", 1152 + 271, 1152 + 384, 16), 1.0, -544.0)
            aff(col("g7"), col("gs"), rm(7))
            aff(cf("xg"), V("RC", 0, 128), col("m56"), col("g7"))
            tt(V("BW", n, n + 128), V("BW", n, n + 128), cf("xg"), OP.add)
            if t == 2:
                aff(col("g8"), col("gs"), rm(8))
                aff(col("g9"), col("gap2"), -1.0)
                aff(col("g7"), col("g9"), rm(9), col("g8"))
                aff(V("BW", 0, n + 128), V("BW", 0, n + 128), 1.0, col("g7"))
        aff(col("gs"), col("gap%d" % t), -1.0, col("gs"))
        aff(col("cum%d" % t), col("gs"), 1.0, n + 128.0)
        grp[0] = "nq2"
        for c, lo in enumerate(range(0, L, 512)):
            if c >= OPT["nq"][t]:
                tt(V("NQ", lo, lo + 512), IND(Tw, u("nl", 32 * c, 32 * c + 32)), V("A", lo, lo + 512), OP.not_equal)
            else:
                act(V("TR", lo, lo + 512), IND(Tw, u("nl", 32 * c, 32 * c + 32)), AF.Identity)
                mm([(PS(3 + c % 2, 0, 512), [(ID, V("A", lo, lo + 512)), (cb("NI"), V("TR", lo, lo + 512))])])
                if last:
                    ts(V("NQ", lo, lo + 512), PS(3 + c % 2, 0, 512), 0.0, OP.not_equal)
                else:
                    act(V("NQ", lo, lo + 512), PS(3 + c % 2, 0, 512), AF.Abs)
        grp[0] = "scan"
        for i in range(0, 16, 2):
            b = 1 + (i // 2) % 2
            mm([(PS(b, 256 * h, 256 * h + K), [(cb("C%d" % (i + h)), B("m"))]) for h in range(2)])
            for h in range(2):
                lo = O + (i + h) * K
                scan(V("V", lo, lo + K), V("NQ", i + h, L, 16), PS(b, 256 * h, 256 * h + K), V("V", lo - 1, lo), OP.add, OP.mult)
        grp[0] = "cf"
        o_, i_ = V("RR", 0, n), IND(Vw, su("end", 0, nc))
        add([("a", lambda e, o=o_, i=i_: e.activation(o["ap"], i["ap"], AF.Relu, bias=230.0, scale=-256.0), ac(o_, i_)),
             ("v", tsf(o_, i_, 0.9, OP.is_lt, 16.0, OP.mult), vc(o_, [i_]))], [o_], [i_])
        tt(V("CF", 0, n), IND(Tw, su("LK", 0, nc)), V("RR", 0, n), OP.min)
        cp(ii("ka", 0, 128), IND(Vw, su("E", 0, 8)))
        tt(bb("eq", 0, 128), IND(Vw, su("E", 0, 8)), ii("ka", 0, 128), OP.is_equal)
        tt(V("CF", n, n + 128), IND(Tw, su("LK", nc, nc + 8)), bb("eq", 0, 128), OP.mult)
        if not last:
            table(t + 1)
        Cw = V(CT, 0, 1024 + n)
        for c in range(K // 32):
            grp[0] = "j%d" % (c % 2)
            aff(V("J", 512 * c, 512 * c + 512), IND(Cw, u("ck", 32 * c, 32 * c + 32)))
        grp[0] = "jw"
        mm([conv(PS(0, 0, K - 64), "Zw", "J", 0, K - 64)])
        mm([conv(PS(0, K - 64, K), "Zw", "J", 16 * (K - 64), 64)])
        grp[0] = "n2"
        Wi = hh("W", 8, K + 8)
        tt(B("ws"), PS(0, 0, K), B("st"), OP.mult)
        tt(B("wm"), PS(0, 0, K), B("mv"), OP.mult)
        scan(back(Hf("r1")), back(nl1), back(B("ws")), 0.0, OP.mult, OP.add)
        scan(Hf("m1"), B("nf"), B("wm"), 0.0, OP.mult, OP.subtract)
        scan(Wi, B("ws"), B("wm"), 0.0, OP.add, OP.add)
        mm([(PS(5, 0, 1), [(cb("LB"), hh("r1", 0, 1))])])
        mm([(PS(6, 0, 1), [(cb("LK"), hh("m1", K - 1, K))]), (PS(6, 1, 2), [(cb("UT"), hh("W", K + 7, K + 8))]),
            (PS(6, 2, 3), [(cb("BO"), hh("W", K + 7, K + 8))])])
        scan(back(Hf("r2")), back(nl1), back(B("ws")), PS(5, 0, 1), OP.mult, OP.add)
        scan(Hf("m2"), B("nf"), B("wm"), PS(6, 0, 1), OP.mult, OP.subtract)
        if OPT["n2"]:
            tt(Hf("wa"), hh("W", 7, K + 7), B("stB"), OP.subtract)
            tt(Hf("r1"), Hf("r2"), Hf("wa"), OP.add)
            tt(Hf("m1"), Hf("m2"), hh("W", 7, K + 7), OP.add)
            tt(Hf("r2"), Hf("r1"), Hf("m1"), OP.max)
        else:
            tt(Hf("r1"), Hf("r2"), B("stB"), OP.subtract)
            tt(Hf("m1"), Hf("r1"), Hf("m2"), OP.max)
            tt(Hf("r2"), Hf("m1"), hh("W", 7, K + 7), OP.add)
        ts(u("pos", K, K + 1), PS(6, 2, 3), rm(15), OP.mult, col("spare"), OP.add)
        ts(u("pos", 0, K), Hf("r2"), PS(6, 1, 2), OP.add, float(O), OP.add)
        if not last:
            grp[0] = "end"
            aff(col("cw"), PS(6, 1, 2), 1.0, O - 1.0)
            mm([(PS(0, 0, K), [(ID, Wi)]), (PS(0, 256, 256 + K), [(ID, Wi), (ID, Hf("m2"))])])
            aff(N("ec"), PS(0, 0, K), 1.0, col("cw"))
            aff(N("ep"), PS(0, 256, 256 + K), 1.0, col("cw"))
            dma("s", V("V", O, O + L, lane=4), N("ec"))
            dma("s", V("V", O, O + L, lane=3), N("ep"))
        ka = OPT["last"] if last else K + 1
        for x, (lo, hi) in enumerate(((0, ka), (ka, K)) if last and OPT["byi"] else ()):
            for i in range(0, 16, 4):
                b = 3 + i // 4 % 2
                grp[0] = "s"
                for h in range(4):
                    mm([(PS(b, 128 * h, 128 * h + hi - lo), [(cb("A%d" % (i + h)), bb("jp", lo, hi)), (cb("E%d" % (i + h)), hh("ce", lo, hi)),
                                                             (cb("M1"), V("J", 16 * lo + i + h, 16 * hi, 16))])])
                grp[0] = "s%d" % x
                for h in range(4):
                    relu(V("S", 16 * lo + i + h, 16 * hi, 16, tag=i + h), PS(b, 128 * h, 128 * h + hi - lo), col("b3"))
        for c in range(0 if last and OPT["byi"] else K // 32):
            b = 3 + c % 2
            grp[0] = "s"
            parts = [(PS(b, 0, 512), cb("M1" if last else "MC"), V("J", 512 * c, 512 * c + 512))]
            for i in range(16):
                parts.append((V("P%d" % b, i, 512, 16), cb(("A%d" if last else "C%d") % i), bb("jp", 32 * c, 32 * c + 32)))
                if last:
                    parts.append((V("P%d" % b, i, 512, 16), cb("E%d" % i), hh("ce", 32 * c, 32 * c + 32)))
            for a in range(0, len(parts), 9):
                mm([(o, [(l, r)]) for o, l, r in parts[a:a + 9]], a == 0, a + 9 >= len(parts), True)
            grp[0] = "s0"
            if last:
                relu(V("S", 512 * c, 512 * c + 512), PS(b, 0, 512), col("b3"))
            else:
                aff(V("S", 512 * c, 512 * c + 512), PS(b, 0, 512), col("ssc"), col("bias"))
        grp[0] = "sc"
        act(IND(V("WA", 0, WW), u("pos", 0, ka)), V("S", 0, 16 * ka), AF.Silu)
        M = lambda name: f(name, 0, K2)
        if not last:
            for k_, (nm, ln, lo) in enumerate((("v", 0, O), ("fk", 2, O), ("rk", 1, O - 1))):
                dma("as"[k_ % 2], M(nm), V("WA", lo, lo + L2, lane=ln))
            grp[0] = "ew"
            aff(V("EW", 0, n), IND(Vw, su("end", 0, nc)), rm(3))
            aff(V("EW", n, n + 128), IND(Vw, su("E", 0, 8)), rm(4))
            mm4(conv(PS(7, 0, nc + 8), "Z34", "EW", 0, nc + 8, cm))
            cp(su("end", 0, nc + 8), PS(7, 0, nc + 8))
            if t == 2:
                ts(sm("pa", 0, nc + 8), PS(7, 0, nc + 8), 0.5, OP.is_lt)
                tt(sm("pb", 0, nc + 8), sm("pa", 0, nc + 8), sm("pc", 0, nc + 8), OP.mult)
                tt(sm("pa", 0, nc + 8), sm("pb", 0, nc + 8), PS(7, 0, nc + 8), OP.add)
                cp(su("eo", 0, nc + 8), sm("pa", 0, nc + 8))
            grp[0] = "n3"
            tt(ii("ka", 0, K2), M("v"), M("rk"), OP.min)
            ts(ii("kf", 0, K2), ii("ka", 0, K2), NFB - 1, OP.bitwise_and)
            finish(t + 1)
            continue
        cp(IND(V("X", 0, WW), u("pos", ka, K + 1)), V("S", 16 * ka, L + 16))
        got = (("s", 0, O), ("e", 3, O), ("c", 4, O), ("k", 5, O - 1))
        names = {"sW": "v", "eW": "rk", "cW": "fk", "kW": "t1", "sX": "t2", "eX": "t3", "cX": "lkn", "kX": "fkg"}
        for k_, (nm, ln, lo) in enumerate(got):
            dma("as"[k_ % 2], M(names[nm + "W"]), V("WA", lo, lo + L2, lane=ln))
            dma("s", M(names[nm + "X"]), V("X", lo, lo + L2, lane=ln))
        grp[0] = "yf"
        acc = sm("pN")
        for s in range(4):
            ts(sm("pa"), sm("pN"), col("cum%d" % s), OP.is_ge, col("gap%d" % s) if s < 3 else 1024.0, OP.mult)
            tt(sm("pb"), acc, sm("pa"), OP.add)
            acc = sm("pb")
        ts(su("yo"), acc, 1024.0, OP.min)
        aff(V("RR", 0, 1024), IND(V("CF", 0, 1040), su("yo")), -1.0, 15.0)
        dma("s", T.yform[:], V("RR", 0, 1024), 256e3)
        grp[0] = "ys"
        G = lambda k: M(names[k])
        tt(M("s0"), G("sW"), G("sX"), OP.add)
        ts(bb("t1", 0, K2), M("s0"), 16.0, OP.is_lt)
        mm([(PS(5, 0, 1), [(IW(1), f("s0", K2 - 1, K2))])])
        scan(M("rn"), bb("t1", 0, K2), M("s0"), PS(5, 0, 1), OP.mult, OP.add)
        ts(M("sp"), M("rn"), 1023.0, OP.max, MAGIC, OP.add)
        aff(M("rn"), M("sp"), 1.0, -MAGIC - 1024)
        dma("s", T.ysite[:], M("rn"))
        tt(hh("m1", 0, K2), G("eW"), G("eX"), OP.add)
        mm([(PS(6, 0, 1), [(IB(1), hh("m1", K2 - 1, K2))])])
        scan(hh("m2", 0, K2), bb("t1", 0, K2), hh("m1", 0, K2), PS(6, 0, 1), OP.mult, OP.add)
        ts(M("ec"), hh("m2", 0, K2), 1023.0, OP.max, -1024.0, OP.add)
        dma("s", T.ycallee[:], M("ec"))
        mm([(PS(1, 0, K2), [(IW(2), G(k)) for k in ("cX", "kX", "cW", "kW")])])
        ts(hh("r2", 0, K2), PS(1, 0, K2), 1023.0, OP.max)
        ts(M("ep"), hh("r2", 0, K2), -1024.0, OP.add)
        dma("a", T.ycaller[:], M("ep"))
    return ops


def order(ops):
    hist = {}
    for k, o in enumerate(ops):
        dep, soft = set(), set()
        for acc, w in ((o["rd"], False), (o["wr"], True)):
            for b, lo, hi, tag in acc:
                for k2, w2, lo2, hi2, tag2 in hist.get(b, []):
                    if (w or w2) and lo < hi2 and lo2 < hi and (tag is None or tag2 is None or tag == tag2):
                        dep.add(k2)
                    elif SCRATCH[b][0] == "psum":
                        soft.add(k2)
        o["soft"] = soft - dep - {k}
        dep |= soft
        dep.discard(k)
        for b, lo, hi, tag in o["wr"]:
            h = hist.setdefault(b, [])
            h[:] = [e for e in h if not (lo <= e[2] and e[3] <= hi and (tag is None or tag == e[4]))]
            h.append((k, True, lo, hi, tag))
        for b, lo, hi, tag in o["rd"]:
            hist.setdefault(b, []).append((k, False, lo, hi, tag))
        o["dep"] = sorted(dep)
        o["pre"] = o["dep"] + ([o["after"]] if "after" in o else [])
    succ = [[] for _ in ops]
    for k, o in enumerate(ops):
        for d in o["pre"]:
            succ[d].append(k)
    if "best" not in KEPT:
        KEPT["best"] = arrange(ops, [o["pre"] for o in ops], succ)
    start, alt = KEPT["best"]
    for k, o in enumerate(ops):
        o["q"], o["fn"], o["cost"] = o["alts"][alt[k]]
        o["t"] = (start[k], start[k] + o["cost"] + o["lat"])
    return sorted(range(len(ops)), key=lambda k: (start[k], k))


def gap(busy, t, c):
    lo, hi = 0, len(busy)
    while lo < hi:
        mid = (lo + hi) // 2
        if busy[mid][1] <= t:
            lo = mid + 1
        else:
            hi = mid
    while lo < len(busy) and busy[lo][0] < t + c:
        t = max(t, busy[lo][1])
        lo += 1
    return t, lo


def place(ops, pre, succ, pr, alt, rev):
    n = len(ops)
    left = [len(p) for p in pre]
    ready = [k for k in range(n) if left[k] == 0]
    busy, done, start, took = {}, [0.0] * n, [0.0] * n, [0] * n
    while ready:
        k = max(ready, key=lambda x: pr[x])
        ready.remove(k)
        o, best = ops[k], None
        for a in ([alt[k]] if alt else range(len(o["alts"]))):
            q, _, c = o["alts"][a]
            at = 0.0
            for p in pre[k]:
                same = ops[p]["alts"][took[p]][0] == q and ops[p]["kind"] == "c"
                free = same and (q == "t" or p in o["soft"] or k in ops[p]["soft"])
                at = max(at, done[p] + (0.0 if free or not q else HOP))
            if rev:
                at += o["lat"]
            s, i = gap(busy.setdefault(q, []), at, c) if q else (at, 0)
            if best is None or s + c + BIAS.get(o["g"], BIAS.get(o["g0"], BIAS0)) < best[0] + best[3]:
                best = (s, i, a, c, q)
        s, i, took[k], c, q = best
        if q:
            busy[q].insert(i, (s, s + c))
        start[k], done[k] = s, s + c + (0.0 if rev else o["lat"])
        for x in succ[k]:
            left[x] -= 1
            if left[x] == 0:
                ready.append(x)
    return start, done, took


def arrange(ops, pre, succ):
    n = len(ops)
    pr = [0.0] * n
    for k in range(n - 1, -1, -1):
        pr[k] = min(a[2] for a in ops[k]["alts"]) + ops[k]["lat"] + HOP + max([pr[s] for s in succ[k]] + [0.0])
    best = None
    for turn in range(TURNS):
        start, done, alt = place(ops, pre, succ, [pr[k] + BOOST.get(o["g0"], 0.0) + BOOST.get(o["g"] + "!", 0.0) for k, o in enumerate(ops)], None, False)
        if best is None or max(done) < best[0]:
            best = (max(done), start, alt)
        if turn < 2:
            pr = place(ops, succ, pre, done, alt, True)[1]
            continue
        late, nxt = [max(done)] * n, {}
        for k in sorted(range(n), key=lambda x: (-start[x], -x)):
            q, _, c = ops[k]["alts"][alt[k]]
            t = min([late[s] - HOP for s in succ[k]] + [max(done)]) - ops[k]["lat"]
            late[k] = min(t, nxt.get(q, t)) - c
            if q:
                nxt[q] = late[k]
            pr[k] += PUSH * max(0.0, 1.0 - (t - c - start[k]) / REACH)
    return best[1:]


BOOST = {'cl': 10, 'arg': 11, 'ew.2!': 16, 'end.2!': 6, 'init': 3, 'cf': -2, 'ys': 5, 's1.3!': -6, 'fin2.2!': 4, 'ct.0!': 2, 'ew': -4, 'nl.2!': -1, 'n1.0!': -6, 'fin2': -3, 's0.1!': -2, 'end.0!': -6, 'n1.3!': -6, 'initA': 8, 'initC': 5, 'rep': 2, 'ct.2!': -1, 'nl.3!': 1, 'nq2.3!': -4, 'jw.3!': 1, 'yf': -2, 'nq2.1!': -2, 'cl.3!': 4, 'cf.0!': -4, 'rep.2!': -1, 'cl2': -2, 'ctp2': 4, 'fin2.0!': 6, 'm.3!': -2, 'cl.0!': 3, 's1': 3, 'ctp3': 1, 'cl2.0!': 7, 'ctp0': 7, 'sc': 1, 'tab.0!': 1, 'scan.2!': -3, 'ye.3!': 2, 'arg.2!': -3, 'cl2.1!': 2, 'prep.0!': 3, 'cl2.3!': 7, 'cl.2!': 1, 's0.2!': 10, 'rep.0!': -1, 'sc.0!': 2, 'j0.3!': 1, 'rep.1!': 12, 'n2.2!': 1, 'nl.1!': 1, 'cf.2!': 1, 'ct.3!': -1, 'sc.3!': -2, 'scan.3!': 3, 'prep.3!': 6, 'n1.2!': 1, 'ye': 2, 'j0.0!': 2, 'cf.3!': 3, 'end.1!': -6, 'ct': 3, 'sc.2!': -2, 'cl2.2!': 2, 'nl': -1, 'j0': 2}
BIAS = {'ctp2': 0.5, 'ctp3': 0.2, 'ew': 50, 'ew.2': 0, 'j0.1': 50, 'j0': 2, 'm': -1, 'cf.3': 0, 's1.3': 0.5, 's0.3': 0.2, 's1': 0, 'end': 4, 'm.1': 0, 'end.0': 2, 'j1.0': -1, 'cf.1': -1, 'ye': 2, 'ys': 1, 'ctp0': -1, 'init': 0, 'ye.3': 0.5, 'fin2.1': 2, 'n1.3': 0, 'm.2': 0.5, 'fin2.2': 0, 'ys.3': 2, 'cl2.3': 4, 'initA': -1, 'prep.0': -1, 'm.0': 2, 'n1.0': 4, 'm.3': -1, 'prep': 0.2, 'end.1': 0, 'cf.2': 0.5, 'cl2.2': 2, 'j1.2': 0.2, 'fin2': 0.5, 'cl2.1': 50, 'init1': 0.5, 'yf.3': 0.2, 'yf': 0.5}
BOOST = {'cl': 6, 'arg': 11, 'jw': 11, 'ew.2!': 11, 'end.2!': 4, 'init': 3, 'ys': 1, 'init3': -2, 'prep.3!': 6, 'prep.2!': 6, 's1': 6, 'ctp2': 12, 'jw.2!': -3, 'cl2.0!': -2, 'cl2.3!': 9, 'initA': 2, 'ctp0': 4, 'cl.1!': -6, 'm.0!': 2, 'fin': 1, 'fin2.0!': 5, 's0.1!': 2, 'jw.0!': 6, 'sc.1!': 2, 'n1.1!': 3, 'sc': 2, 'end': 3, 's0.2!': 1, 'ctp1': -2, 'fin.1!': -1, 'cl.0!': -6, 'n1.3!': 2, 'jw.1!': 6, 'sc.3!': -1, 'm.1!': 5, 'ys.3!': 1, 'cf.2!': -2, 'ct': 3, 'end.1!': -2, 'ct.1!': -2, 'cf.0!': 1, 'ct.0!': 1, 'nq2.1!': 6, 'm.2!': 2}
BIAS = {'ew': 1, 'ew.2': 0, 'end': 0.2, 'cl2': 4, 'cf.0': -1, 'initA': 0.5, 'n1.3': 0.2, 'end.1': 4, 'm.2': 0.5, 'ys.3': 0, 'cl2.0': 4, 'prep.3': 0.5, 's0.3': 50, 'j1.3': 0.2, 'm.3': 50, 'init2': 1, 's0.2': 4, 'prep.1': -1, 'ctp0': -1, 'cf.1': 0, 'ctp2': 0.5, 'cl2.1': 4, 's0.0': 50, 'm.0': 0.5, 'j1.1': 0.5, 'm': 0.5, 'ye': 0.5, 'j0.0': 1, 'n1.2': 4, 's0': 1, 'init': 50}
BIAS0, TURNS, PUSH, REACH, KEPT = 0.5, 2, 1.0, 1.0, {}
OPT = {"n2": 1, "byi": 1, "gfill": ("ctp1", "ctp2", "ctp3"), "hv": 0, "cut": (0, 4, 8, 12, 16), "nq": (0, 1, 1, 0), "last": 128}


def rank_program(g, core, T, topo):
    rank = T.rank_of(core)
    if rank is None:
        return
    nxt = T.cores[(rank + 1) % len(T.cores)]
    ops = plan(T, core, nxt, topo)
    seq = order(ops)
    Q = {"v": g.vector, "a": g.scalar, "t": g.tensor, "g": g, "s": g.sync}
    count, seen, top, nd = {}, {q: {} for q in Q}, {}, [0]
    for k in seq:
        o = ops[k]
        if o["kind"] == "r":
            o["sig"] = ("r%d" % o["k"], o["cnt"])
            top[o["sig"][0]] = o["cnt"]
            continue
        q = o["q"]
        need = {}
        for d in o["dep"]:
            s, val = ops[d]["sig"]
            if s == "e" + q and (q == "t" or d in o["soft"]):
                continue
            need[s] = max(need.get(s, 0), val)
        for s in sorted(need):
            if seen[q].get(s, 0) < need[s]:
                Q[q].wait_ge(T.sem[s], need[s])
                seen[q][s] = need[s]
        ins = o["fn"](Q[q])
        if o["kind"] == "c":
            s = "e" + q
            count[s] = count.get(s, 0) + 1
            ins.then_inc(T.sem[s], 1)
            o["sig"] = (s, count[s])
        elif o["kind"] == "d":
            s = "d%d" % nd[0]
            nd[0] += 1
            ins.then_inc(T.sem[s], 16)
            o["sig"] = (s, 16)
        else:
            o["sig"] = ("l%d" % o["k"], o["cnt"])
        top[o["sig"][0]] = o["sig"][1]
    for s in sorted(top):
        if all(seen[q].get(s, 0) < top[s] for q in Q):
            g.wait_ge(T.sem[s], top[s])
